import numpy as np
import ml_dtypes


def mxq(x, axis, fmt="e4m3"):
    dtype, down = {"e4m3": (ml_dtypes.float8_e4m3fn, 7), "e5m2": (ml_dtypes.float8_e5m2, 14)}[fmt]
    v = np.moveaxis(np.asarray(x, np.float32).astype(ml_dtypes.bfloat16).astype(np.float64), axis, -1)
    blocks = v.reshape(v.shape[:-1] + (-1, 32))
    amax = np.abs(blocks).max(-1, keepdims=True)
    byte = np.maximum(np.where(amax > 0, np.frexp(amax)[1] - 1 + 127, 0) - down, 1)
    scale = np.exp2(byte - 127.0)
    codes = (blocks / scale).astype(np.float32).astype(dtype).astype(np.float64)
    return np.moveaxis((codes * scale).reshape(v.shape), -1, axis)


WIDE = False


def mx_kscale(k):
    if not WIDE:
        return np.ones(k)
    levels = np.array([24, -24, 12, -12, 0])
    if k % 512:
        return np.exp2(np.random.permutation(np.resize(levels, k // 32))).repeat(32)
    a = np.empty((k // 512, 16))
    for p in range(k // 512):
        a[p, :8] = np.random.permutation(np.resize(levels, 8))
        for g in range(8):
            far = levels[np.abs(levels - a[p, g]) >= 10]
            a[p, g + 8] = far[np.random.randint(len(far))]
    return np.exp2(a.ravel()).repeat(32)


def f64(x):
    return np.asarray(x).astype(np.float64)


def striped(idx):
    return np.tile(idx.reshape(-1, 16).T, (8, 1)).astype(np.uint16)


def unstriped(offs):
    return offs[:16].T.reshape(-1).astype(np.int64)


E2M1 = np.array([0.0, 0.5, 1.0, 1.5, 2.0, 3.0, 4.0, 6.0, -0.0, -0.5, -1.0, -1.5, -2.0, -3.0, -4.0, -6.0])


def pack_weight(w, fmt):
    k, n = w.shape
    w = f64(np.asarray(w, np.float32).astype(ml_dtypes.bfloat16)).reshape(k // 32, 32, n)
    amax = np.abs(w).max(1)
    if fmt == "e4m3":
        byte = np.frexp(amax)[1] - 1 + 127 - 7
    else:
        mant, ex = np.frexp(amax / 6.0)
        byte = np.where(mant > 0.5, ex, ex - 1) + 127
    byte = np.clip(np.where(amax > 0, byte, 1), 1, 254)
    scaled = (w * np.exp2(127.0 - byte)[:, None, :]).reshape(k, n).astype(np.float32)
    by_word = np.ascontiguousarray(scaled.reshape(k // 512, 128, 4, n).transpose(0, 1, 3, 2))
    if fmt == "e4m3":
        words = by_word.astype(ml_dtypes.float8_e4m3fn).view(np.uint8)
    else:
        c = by_word.astype(ml_dtypes.float4_e2m1fn).view(np.uint8) & 0xF
        words = (c[..., 0::2] | (c[..., 1::2] << 4)).reshape(k // 512, 128, 2 * n)
    return np.ascontiguousarray(words), np.ascontiguousarray(byte.astype(np.uint8).reshape(k // 512, 16, n))


def unpack_weight(words, scales, fmt):
    g, _, n = scales.shape
    words = np.ascontiguousarray(words).reshape(g, 128, n, -1)
    if fmt == "e4m3":
        vals = words.view(ml_dtypes.float8_e4m3fn).astype(np.float64)
    else:
        nib = np.empty((g, 128, n, 4), np.uint8)
        nib[..., 0::2] = words & 0xF
        nib[..., 1::2] = words >> 4
        vals = E2M1[nib]
    vals = vals * np.repeat(np.exp2(scales.astype(np.float64) - 127.0), 8, axis=1)[..., None]
    return vals.transpose(0, 1, 3, 2).reshape(g * 512, n)


def planes(y):
    n, m = y.shape
    v = y.astype(np.float32).astype(ml_dtypes.bfloat16).astype(np.float64).reshape(n // 32, 32, m)
    top = np.abs(v).max(1)
    byte = np.clip(np.where(top > 0, np.frexp(top)[1] - 1 + 127 - 7, 1), 1, 254)
    codes = (v * np.exp2(127.0 - byte)[:, None, :]).reshape(n, m).astype(np.float32).astype(ml_dtypes.float8_e4m3fn).view(np.uint8)
    words = codes.reshape(n // 512, 128, 4, m).transpose(0, 1, 3, 2)
    return np.ascontiguousarray(words), np.ascontiguousarray(byte.astype(np.uint8).reshape(n // 512, 16, m))


K, R, N, T, J = 1024, 512, 512, 2048, 1024


def setup_inputs():
    n = np.random.standard_normal
    s = mx_kscale(K)[:, None]
    u = mx_kscale(R)[:, None]
    p_tab = pack_weight(n((K, T)) * s, "e4m3")
    p_ws = pack_weight(n((K, R)) / np.sqrt(2 * K) / s * u.T, "e2m1")
    p_wd = pack_weight(n((R, N)) / np.sqrt(R) / u, "e2m1")
    return {
        "tab_words": p_tab[0],
        "tab_scales": p_tab[1],
        "ws_words": p_ws[0],
        "ws_scales": p_ws[1],
        "wt": (n((K, R)) / np.sqrt(2 * K) / s * u.T).astype(np.float32),
        "wd_words": p_wd[0],
        "wd_scales": p_wd[1],
        "wgo": np.tile(np.random.uniform(0.5, 2.0, J), (128, 1)).astype(np.float32),
        "offs": striped(np.random.permutation(T)[:J]),
        "offs2": striped(np.random.permutation(T)[:J]),
    }


def reference(tab_words, tab_scales, ws_words, ws_scales, wt, wd_words, wd_scales, wgo, offs, offs2):
    idx = unstriped(offs)
    idx2 = unstriped(offs2)
    tab_ = unpack_weight(tab_words, tab_scales, "e4m3")[:, idx]
    tabb_ = unpack_weight(tab_words, tab_scales, "e4m3")[:, idx2]
    ws_ = unpack_weight(ws_words, ws_scales, "e2m1")
    wt_ = mxq(f64(wt), 0, "e4m3")
    a = ws_.T @ tab_ + wt_.T @ tabb_
    h = np.maximum(a, 0.0)
    h_ = mxq(h, 0, "e4m3")
    wd_ = unpack_weight(wd_words, wd_scales, "e2m1")
    y = wd_.T @ h_
    out = np.zeros((N, T))
    out[:, idx2] = f64(wgo)[0] * (y)
    return (out,) + planes(out)

@@ -1,0 +1,268 @@
+from contextlib import ExitStack
+
+import concourse.mybir as mybir
+
+K, R, N, T, J = 1024, 512, 512, 2048, 1024
+FLOPS = 2 * (2 * K * R * J + R * N * J)
+
+F32 = mybir.dt.float32
+BF16 = mybir.dt.bfloat16
+I32 = mybir.dt.int32
+U32 = mybir.dt.uint32
+U16 = mybir.dt.uint16
+U8 = mybir.dt.uint8
+FP8X4 = mybir.dt.float8_e4m3fn_x4
+FP4X4 = mybir.dt.float4_e2m1fn_x4
+ACT = mybir.ActivationFunctionType
+MULT = mybir.AluOpType.mult
+
+P = 128
+PACK = 4
+PASSES = K // (P * PACK)
+BANK_J = 128
+BANKS = J // BANK_J
+CHUNK_J = 256
+CHUNKS = J // CHUNK_J
+OUT_C = 512
+OUT_CHUNKS = T // OUT_C
+
+
+def tile_list_msg_relu_noneP_kernel(
+    tc, tab_words, tab_scales, ws_words, ws_scales, wt, wd_words, wd_scales, wgo, offs, offs2, out_0, out_1, out_2
+):
+    nc = tc.nc
+    with ExitStack() as ctx:
+        keep = ctx.enter_context(tc.tile_pool(name="keep", bufs=1))
+        psum = ctx.enter_context(tc.psum_pool(name="psum", bufs=1))
+
+        def sb(shape, dtype, name, tag=None):
+            return keep.tile(shape, dtype, name=name, tag=tag or name, align_bytes=64)
+
+        src_list = keep.tile([P, J // 16], U16, name="src_list")
+        dst_list = keep.tile([P, J // 16], U16, name="dst_list")
+        lists = (src_list, dst_list)
+
+        def ring(shape, dtype, name):
+            return keep.tile(shape, dtype, name=name, tag="ring", bufs=3, align_bytes=64)
+
+        tab_sc = sb([P, T], U8, "tab_sc")
+        wd_raw = ring([P, 2 * N], U8, "wd_raw")
+        wd_sc_raw = ring([P, N], U8, "wd_sc_raw")
+        ws_sc_raw = ring([P, PASSES, R], U8, "ws_sc_raw")
+        src_sc1 = sb([P, J], U8, "src_sc1")
+        nc.vector.memset(tab_sc[:].bitcast(I32), 0)
+        nc.vector.memset(ws_sc_raw[:].bitcast(I32), 0)
+        nc.vector.memset(wd_sc_raw[:].bitcast(I32), 0)
+        nc.vector.memset(src_sc1[:].bitcast(I32), 0)
+
+        ws_raw = sb([P, PASSES, 2 * R], U8, "ws_raw", tag="tab1")
+        tab = [sb([P, T], I32, "tab0")]
+
+        def load_tab(a):
+            nc.sync.dma_start(tab[a][:], tab_words[a].rearrange("p t i -> p (t i)").bitcast(I32))
+
+        nc.sync.dma_start(src_list[:], offs)
+        nc.sync.dma_start(dst_list[:], offs2)
+        nc.sync.dma_start(ws_raw[:].bitcast(I32), ws_words.rearrange("a p c -> p a c").bitcast(I32))
+        load_tab(0)
+        for q in range(4):
+            nc.scalar.dma_start(
+                tab_sc[32 * q : 32 * q + 8, :].bitcast(I32), tab_scales[:, 4 * q : 4 * q + 4, :].bitcast(I32)
+            )
+        for q in range(4):
+            nc.scalar.dma_start(
+                ws_sc_raw[32 * q : 32 * q + 4, :, :].bitcast(I32),
+                ws_scales[:, 4 * q : 4 * q + 4, :].rearrange("a r c -> r a c").bitcast(I32),
+            )
+        nc.gpsimd.dma_start(wd_raw[:].bitcast(I32), wd_words[0].bitcast(I32))
+        for q in range(4):
+            nc.gpsimd.dma_start(
+                wd_sc_raw[32 * q : 32 * q + 4, :].bitcast(I32), wd_scales[0, 4 * q : 4 * q + 4, :].bitcast(I32)
+            )
+
+        page0 = sb([P, T], F32, "page0")
+        nc.vector.memset(page0[:], 0.0)
+
+        ws = sb([P, PASSES, 2 * R], U8, "ws")
+        wd = sb([P, 2 * N], U8, "wd")
+        ws_sc = sb([P, PASSES, R], U8, "ws_sc")
+        wd_sc = sb([P, N], U8, "wd_sc")
+        nc.vector.tensor_copy(
+            ws[:].bitcast(U16).rearrange("p a (t m) -> p a t m", t=PACK),
+            ws_raw[:].bitcast(U16).rearrange("p a (m t) -> p a t m", t=PACK),
+        )
+        nc.vector.tensor_copy(
+            ws_sc[:].rearrange("p a (t m) -> p a t m", t=PACK),
+            ws_sc_raw[:].rearrange("p a (m t) -> p a t m", t=PACK),
+        )
+        nc.vector.tensor_copy(
+            wd[:].bitcast(U16).rearrange("p (t m) -> p t m", t=PACK),
+            wd_raw[:].bitcast(U16).rearrange("p (m t) -> p t m", t=PACK),
+        )
+        tab.append(sb([P, T], I32, "tab1"))
+        load_tab(1)
+
+        g_words = [[sb([P, J], I32, f"g0_{a}")[:] for a in range(PASSES)]]
+        g_sc = [sb([P, J], U8, "g_sc0")]
+
+        def gather_words(l, a, j0, j1):
+            nc.vector.tensor_copy(
+                g_words[l][a][:, j0:j1].bitcast(U32), tab[a][:].bitcast(U32).indirect(lists[l][:, j0 // 16 : j1 // 16])
+            )
+
+        def gather_scales(l):
+            nc.vector.tensor_copy(g_sc[l][:], tab_sc[:].indirect(lists[l][:]))
+
+        gather_scales(0)
+        nc.gpsimd.dma_start(src_sc1[0 : P - 4, :].bitcast(I32), g_sc[0][4:P, :].bitcast(I32))
+        for j0, j1 in ((0, 256), (256, 512), (512, 1024)):
+            gather_words(0, 0, j0, j1)
+        nc.vector.tensor_copy(
+            wd_sc[:].rearrange("p (t m) -> p t m", t=PACK),
+            wd_sc_raw[:].rearrange("p (m t) -> p t m", t=PACK),
+        )
+        wt_raw = [[ring([P, PACK, R // 2], F32, f"wt_raw{a}_{h}") for h in range(2)] for a in range(PASSES)]
+
+        def load_wt(a, h):
+            rows = wt[a * 512 : (a + 1) * 512, :].rearrange("(p i) c -> p i c", i=PACK)
+            nc.sync.dma_start(wt_raw[a][h][:], rows[:, :, h * 256 : (h + 1) * 256])
+
+        gather_words(0, 1, 0, 512)
+        gather_words(0, 1, 512, 1024)
+
+        wt_bf = [sb([P, R * PACK], BF16, f"wt_bf{a}") for a in range(PASSES)]
+        wt_q = [sb([P, R], I32, f"wt_q{a}") for a in range(PASSES)]
+        wt_sc = [sb([P, R], U8, f"wt_sc{a}") for a in range(PASSES)]
+        for a in range(PASSES):
+            for h in range(2):
+                load_wt(a, h)
+                nc.scalar.activation(
+                    wt_bf[a][:].rearrange("p (t m i) -> p m i t", t=PACK, i=PACK)[:, 64 * h : 64 * (h + 1), :, :],
+                    wt_raw[a][h][:].rearrange("p i (m t) -> p m i t", t=PACK),
+                    ACT.Copy,
+                )
+            nc.vector.quantize_mx(wt_q[a][:].bitcast(FP8X4), wt_sc[a][:], wt_bf[a][:])
+
+        g_sc.append(sb([P, J], U8, "g_sc1", tag="wt_bf0"))
+        gather_scales(1)
+        g_dst = sb([P, PASSES * J], I32, "g_dst", tag="wt_bf1")
+        g_words.append([g_dst[:, a * J : (a + 1) * J] for a in range(PASSES)])
+        edge_w = ring([P, J], F32, "edge_w")
+        nc.sync.dma_start(edge_w[:], wgo)
+
+        acc = [psum.tile([P, PACK, BANK_J], F32, name=f"acc{b}", tag=f"bank{b}") for b in range(BANKS)]
+
+        def first_product(l, a, b):
+            cols = slice(b * BANK_J, (b + 1) * BANK_J)
+            for t in range(PACK):
+                if l == 0:
+                    lhsT = ws[:, a, 2 * P * t : 2 * P * (t + 1)].bitcast(FP4X4)
+                    lhsT_scale = ws_sc[:, a, P * t : P * (t + 1)]
+                    rhs_scale = g_sc[0][:, cols] if a == 0 else src_sc1[:, cols]
+                else:
+                    lhsT = wt_q[a][:, P * t : P * (t + 1)].bitcast(FP8X4)
+                    lhsT_scale = wt_sc[a][:, P * t : P * (t + 1)]
+                    rhs_scale = g_sc[1][4 * a : P, cols]
+                nc.tensor.matmul_mx(
+                    acc[b][:, t, :],
+                    lhsT=lhsT,
+                    lhsT_scale=lhsT_scale,
+                    rhs=g_words[l][a][:, cols].bitcast(FP8X4),
+                    rhs_scale=rhs_scale,
+                    start=(l == 0 and a == 0 and t == 0),
+                    stop=(l == 1 and a == PASSES - 1 and t == PACK - 1),
+                )
+
+        for a in range(PASSES):
+            for b in range(BANKS):
+                first_product(0, a, b)
+
+        h_bf = sb([P, J * PACK], BF16, "h_bf", tag="slot1")
+        h_q = sb([P, J], I32, "h_q", tag="slot2")
+        h_sc = sb([P, J], U8, "h_sc", tag="slot3")
+        y = sb([P, PACK, J], F32, "y")
+
+        def scatter(page, t, j0, j1):
+            nc.vector.tensor_tensor(
+                page[:].indirect(dst_list[:, j0 // 16 : j1 // 16]), y[:, t, j0:j1], edge_w[:, j0:j1], MULT
+            )
+
+        def finish_first(c):
+            j0, j1 = c * CHUNK_J, (c + 1) * CHUNK_J
+            for a in range(PASSES):
+                gather_words(1, a, j0, j1)
+            for b in (2 * c, 2 * c + 1):
+                for a in range(PASSES):
+                    first_product(1, a, b)
+                nc.scalar.activation(
+                    h_bf[:, b * 512 : (b + 1) * 512].rearrange("p (j t) -> p j t", t=PACK),
+                    acc[b][:].rearrange("p t j -> p j t"),
+                    ACT.Relu,
+                )
+
+        def second(c):
+            j0, j1 = c * CHUNK_J, (c + 1) * CHUNK_J
+            nc.vector.quantize_mx(h_q[:, j0:j1].bitcast(FP8X4), h_sc[:, j0:j1], h_bf[:, PACK * j0 : PACK * j1])
+            for u in range(2):
+                res = psum.tile([P, 2, CHUNK_J], F32, name=f"res{c}_{u}", tag=f"bank{2 * c + u}")
+                for e in range(2):
+                    t = 2 * u + e
+                    nc.tensor.matmul_mx(
+                        res[:, e, :],
+                        lhsT=wd[:, 2 * P * t : 2 * P * (t + 1)].bitcast(FP4X4),
+                        lhsT_scale=wd_sc[:, P * t : P * (t + 1)],
+                        rhs=h_q[:, j0:j1].bitcast(FP8X4),
+                        rhs_scale=h_sc[:, j0:j1],
+                        start=True,
+                        stop=True,
+                    )
+                nc.scalar.activation(y[:, 2 * u : 2 * u + 2, j0:j1], res[:], ACT.Copy)
+
+        for c in range(CHUNKS + 2):
+            if c < CHUNKS:
+                finish_first(c)
+            if 1 <= c <= CHUNKS:
+                second(c - 1)
+            if c >= 2:
+                scatter(page0, 0, (c - 2) * CHUNK_J, (c - 1) * CHUNK_J)
+
+        pages = [page0] + [sb([P, T], F32, f"page{t}", tag=f"slot{t}") for t in range(1, PACK)]
+        for t in range(1, PACK):
+            nc.gpsimd.memset(pages[t][:], 0.0)
+
+        o_bf = sb([P, T * PACK], BF16, "o_bf")
+        o_dealt = o_bf[:].rearrange("p (c t) -> p c t", t=PACK)
+        o_q = [sb([P, OUT_C], I32, f"o_q{c}") for c in range(OUT_CHUNKS)]
+        o_sc = sb([P, T], U8, "o_sc")
+        out_rows = out_0.rearrange("(p t) c -> p t c", t=PACK)
+        out_words = out_1[0].rearrange("p c i -> p (c i)").bitcast(I32)
+        V_COLS = 2 * OUT_C
+
+        for t in range(PACK):
+            if t > 0:
+                scatter(pages[t], t, 0, J)
+            nc.sync.dma_start(out_rows[:, t, :], pages[t][:])
+            if t < 2:
+                nc.scalar.activation(o_dealt[:, :, t], pages[t][:], ACT.Copy)
+            elif t == 2:
+                nc.scalar.activation(
+                    o_dealt[:, 0:V_COLS, 2:4], pages[t][:, 0:V_COLS].unsqueeze(2).to_broadcast([P, V_COLS, 2]), ACT.Copy
+                )
+                nc.scalar.activation(o_dealt[:, V_COLS:T, t], pages[t][:, V_COLS:T], ACT.Copy)
+            else:
+                for c in range(OUT_CHUNKS):
+                    cols = slice(c * OUT_C, (c + 1) * OUT_C)
+                    if c * OUT_C < V_COLS:
+                        nc.vector.tensor_copy(o_dealt[:, cols, t], pages[t][:, cols])
+                    else:
+                        nc.scalar.activation(o_dealt[:, cols, t], pages[t][:, cols], ACT.Copy)
+
+        for c in range(OUT_CHUNKS):
+            cols = slice(c * OUT_C, (c + 1) * OUT_C)
+            nc.vector.quantize_mx(
+                o_q[c][:].bitcast(FP8X4), o_sc[:, cols], o_bf[:, PACK * c * OUT_C : PACK * (c + 1) * OUT_C]
+            )
+            nc.sync.dma_start(out_words[:, cols], o_q[c][:])
+        for q in range(4):
+            eng = nc.scalar if q % 2 else nc.sync
+            eng.dma_start(out_2[0, 4 * q : 4 * q + 4, :].bitcast(I32), o_sc[32 * q : 32 * q + 4, :].bitcast(I32))

@@ -42,113 +42,106 @@ def tile_list_msg_relu_noneP_kernel(
         dst_list = keep.tile([P, J // 16], U16, name="dst_list")
         lists = (src_list, dst_list)
 
-        def ring(shape, dtype, name):
-            return keep.tile(shape, dtype, name=name, tag="ring", bufs=3, align_bytes=64)
-
-        tab_sc = sb([P, T], U8, "tab_sc")
-        wd_raw = ring([P, 2 * N], U8, "wd_raw")
-        wd_sc_raw = ring([P, N], U8, "wd_sc_raw")
-        ws_sc_raw = ring([P, PASSES, R], U8, "ws_sc_raw")
-        src_sc1 = sb([P, J], U8, "src_sc1")
+        tab_sc = sb([P, T], U8, "tab_sc", tag="stage2")
+        ws_sc_raw = sb([P, R], U8, "ws_sc_raw", tag="g_src")
+        zeros = sb([P, R // 4], I32, "zeros", tag="tab0")
+        wd_sc_raw = sb([P, N], U8, "wd_sc_raw", tag="page0")
+        lowered = sb([P, J + R], U8, "lowered")
+        src_sc1 = lowered[:, 0:J]
+        ws_sc1 = lowered[:, J : J + R]
+        nc.gpsimd.memset(lowered[:].bitcast(I32), 0)
         nc.vector.memset(tab_sc[:].bitcast(I32), 0)
+        nc.vector.memset(zeros[:], 0)
+        nc.vector.tensor_copy(wd_sc_raw[:].bitcast(I32), zeros[:])
         nc.vector.memset(ws_sc_raw[:].bitcast(I32), 0)
-        nc.vector.memset(wd_sc_raw[:].bitcast(I32), 0)
-        nc.vector.memset(src_sc1[:].bitcast(I32), 0)
 
-        ws_raw = sb([P, PASSES, 2 * R], U8, "ws_raw", tag="tab1")
-        tab = [sb([P, T], I32, "tab0")]
+        ws_raw = sb([P, PASSES, 2 * R], U8, "ws_raw", tag="stage1")
+        wd_raw = sb([P, 2 * N], U8, "wd_raw")
+        tab = []
 
-        def load_tab(a):
+        def load_tab(a, tag):
+            tab.append(sb([P, T], I32, f"tab{a}", tag=tag))
             nc.sync.dma_start(tab[a][:], tab_words[a].rearrange("p t i -> p (t i)").bitcast(I32))
 
+        wt_bf = [sb([P, R * PACK], BF16, f"wt_bf{a}") for a in range(PASSES)]
+
+        def load_and_round_wt(a, h, tag):
+            rows = wt[a * 512 : (a + 1) * 512, :].rearrange("(p i) c -> p i c", i=PACK)
+            wt_raw = sb([P, PACK, R // 2], F32, f"wt_part{a}_{h}", tag=tag)
+            nc.sync.dma_start(wt_raw[:], rows[:, :, h * 256 : (h + 1) * 256])
+            nc.scalar.activation(
+                wt_bf[a][:].rearrange("p (t m i) -> p m i t", t=PACK, i=PACK)[:, 64 * h : 64 * (h + 1), :, :],
+                wt_raw[:].rearrange("p i (m t) -> p m i t", t=PACK),
+                ACT.Copy,
+            )
+
+        def load_planes(eng, tile, rows, scales):
+            for q in range(4):
+                eng.dma_start(tile[32 * q : 32 * q + rows, :].bitcast(I32), scales[:, 4 * q : 4 * q + 4, :].bitcast(I32))
+
+        nc.gpsimd.dma_start(wd_raw[:].bitcast(I32), wd_words[0].bitcast(I32))
+        load_planes(nc.gpsimd, wd_sc_raw, 4, wd_scales)
+        nc.sync.dma_start(ws_raw[:].bitcast(I32), ws_words.rearrange("a p c -> p a c").bitcast(I32))
         nc.sync.dma_start(src_list[:], offs)
         nc.sync.dma_start(dst_list[:], offs2)
-        nc.sync.dma_start(ws_raw[:].bitcast(I32), ws_words.rearrange("a p c -> p a c").bitcast(I32))
-        load_tab(0)
-        for q in range(4):
-            nc.scalar.dma_start(
-                tab_sc[32 * q : 32 * q + 8, :].bitcast(I32), tab_scales[:, 4 * q : 4 * q + 4, :].bitcast(I32)
-            )
-        for q in range(4):
-            nc.scalar.dma_start(
-                ws_sc_raw[32 * q : 32 * q + 4, :, :].bitcast(I32),
-                ws_scales[:, 4 * q : 4 * q + 4, :].rearrange("a r c -> r a c").bitcast(I32),
-            )
-        nc.gpsimd.dma_start(wd_raw[:].bitcast(I32), wd_words[0].bitcast(I32))
-        for q in range(4):
-            nc.gpsimd.dma_start(
-                wd_sc_raw[32 * q : 32 * q + 4, :].bitcast(I32), wd_scales[0, 4 * q : 4 * q + 4, :].bitcast(I32)
-            )
-
-        page0 = sb([P, T], F32, "page0")
-        nc.vector.memset(page0[:], 0.0)
+        load_and_round_wt(0, 0, "stage0")
+        load_planes(nc.sync, tab_sc, 8, tab_scales)
+        load_tab(0, "tab0")
+        load_planes(nc.sync, ws_sc_raw, 8, ws_scales)
 
         ws = sb([P, PASSES, 2 * R], U8, "ws")
-        wd = sb([P, 2 * N], U8, "wd")
-        ws_sc = sb([P, PASSES, R], U8, "ws_sc")
-        wd_sc = sb([P, N], U8, "wd_sc")
+        ws_sc = sb([P, R], U8, "ws_sc")
         nc.vector.tensor_copy(
             ws[:].bitcast(U16).rearrange("p a (t m) -> p a t m", t=PACK),
             ws_raw[:].bitcast(U16).rearrange("p a (m t) -> p a t m", t=PACK),
         )
-        nc.vector.tensor_copy(
-            ws_sc[:].rearrange("p a (t m) -> p a t m", t=PACK),
-            ws_sc_raw[:].rearrange("p a (m t) -> p a t m", t=PACK),
-        )
-        nc.vector.tensor_copy(
-            wd[:].bitcast(U16).rearrange("p (t m) -> p t m", t=PACK),
-            wd_raw[:].bitcast(U16).rearrange("p (m t) -> p t m", t=PACK),
-        )
-        tab.append(sb([P, T], I32, "tab1"))
-        load_tab(1)
+        load_and_round_wt(0, 1, "stage1")
+        load_tab(1, "stage0")
 
-        g_words = [[sb([P, J], I32, f"g0_{a}")[:] for a in range(PASSES)]]
-        g_sc = [sb([P, J], U8, "g_sc0")]
+        g_sc = [sb([P, J], U8, f"g_sc{l}") for l in range(2)]
+        for l in range(2):
+            nc.vector.tensor_copy(g_sc[l][:], tab_sc[:].indirect(lists[l][:]))
+        nc.gpsimd.dma_start(src_sc1[0 : P - 4, :].bitcast(I32), g_sc[0][4:P, :].bitcast(I32))
+        nc.vector.tensor_copy(
+            ws_sc[:].rearrange("p (t m) -> p t m", t=PACK), ws_sc_raw[:].rearrange("p (m t) -> p t m", t=PACK)
+        )
+        nc.gpsimd.dma_start(ws_sc1[0 : P - 4, :].bitcast(I32), ws_sc[4:P, :].bitcast(I32))
+
+        load_and_round_wt(1, 0, "stage2")
+        load_and_round_wt(1, 1, "stage1")
+        g_src = sb([P, PASSES * J], I32, "g_src")
+        g_words = [[g_src[:, a * J : (a + 1) * J] for a in range(PASSES)]]
 
         def gather_words(l, a, j0, j1):
             nc.vector.tensor_copy(
                 g_words[l][a][:, j0:j1].bitcast(U32), tab[a][:].bitcast(U32).indirect(lists[l][:, j0 // 16 : j1 // 16])
             )
 
-        def gather_scales(l):
-            nc.vector.tensor_copy(g_sc[l][:], tab_sc[:].indirect(lists[l][:]))
-
-        gather_scales(0)
-        nc.gpsimd.dma_start(src_sc1[0 : P - 4, :].bitcast(I32), g_sc[0][4:P, :].bitcast(I32))
         for j0, j1 in ((0, 256), (256, 512), (512, 1024)):
             gather_words(0, 0, j0, j1)
-        nc.vector.tensor_copy(
-            wd_sc[:].rearrange("p (t m) -> p t m", t=PACK),
-            wd_sc_raw[:].rearrange("p (m t) -> p t m", t=PACK),
-        )
-        wt_raw = [[ring([P, PACK, R // 2], F32, f"wt_raw{a}_{h}") for h in range(2)] for a in range(PASSES)]
-
-        def load_wt(a, h):
-            rows = wt[a * 512 : (a + 1) * 512, :].rearrange("(p i) c -> p i c", i=PACK)
-            nc.sync.dma_start(wt_raw[a][h][:], rows[:, :, h * 256 : (h + 1) * 256])
-
         gather_words(0, 1, 0, 512)
         gather_words(0, 1, 512, 1024)
 
-        wt_bf = [sb([P, R * PACK], BF16, f"wt_bf{a}") for a in range(PASSES)]
         wt_q = [sb([P, R], I32, f"wt_q{a}") for a in range(PASSES)]
         wt_sc = [sb([P, R], U8, f"wt_sc{a}") for a in range(PASSES)]
         for a in range(PASSES):
-            for h in range(2):
-                load_wt(a, h)
-                nc.scalar.activation(
-                    wt_bf[a][:].rearrange("p (t m i) -> p m i t", t=PACK, i=PACK)[:, 64 * h : 64 * (h + 1), :, :],
-                    wt_raw[a][h][:].rearrange("p i (m t) -> p m i t", t=PACK),
-                    ACT.Copy,
-                )
             nc.vector.quantize_mx(wt_q[a][:].bitcast(FP8X4), wt_sc[a][:], wt_bf[a][:])
 
-        g_sc.append(sb([P, J], U8, "g_sc1", tag="wt_bf0"))
-        gather_scales(1)
+        edge_w = sb([P, J], F32, "edge_w", tag="stage2")
+        nc.sync.dma_start(edge_w[:], wgo)
+        wd = sb([P, 2 * N], U8, "wd", tag="stage1")
+        nc.vector.tensor_copy(
+            wd[:].bitcast(U16).rearrange("p (t m) -> p t m", t=PACK),
+            wd_raw[:].bitcast(U16).rearrange("p (m t) -> p t m", t=PACK),
+        )
+        wd_sc = sb([P, N], U8, "wd_sc", tag="wt_bf0")
+        nc.vector.tensor_copy(
+            wd_sc[:].rearrange("p (t m) -> p t m", t=PACK), wd_sc_raw[:].rearrange("p (m t) -> p t m", t=PACK)
+        )
+        page0 = sb([P, T], F32, "page0")
+        nc.gpsimd.memset(page0[:], 0.0)
         g_dst = sb([P, PASSES * J], I32, "g_dst", tag="wt_bf1")
         g_words.append([g_dst[:, a * J : (a + 1) * J] for a in range(PASSES)])
-        edge_w = ring([P, J], F32, "edge_w")
-        nc.sync.dma_start(edge_w[:], wgo)
 
         acc = [psum.tile([P, PACK, BANK_J], F32, name=f"acc{b}", tag=f"bank{b}") for b in range(BANKS)]
 
@@ -157,7 +150,7 @@ def tile_list_msg_relu_noneP_kernel(
             for t in range(PACK):
                 if l == 0:
                     lhsT = ws[:, a, 2 * P * t : 2 * P * (t + 1)].bitcast(FP4X4)
-                    lhsT_scale = ws_sc[:, a, P * t : P * (t + 1)]
+                    lhsT_scale = (ws_sc if a == 0 else ws_sc1)[:, P * t : P * (t + 1)]
                     rhs_scale = g_sc[0][:, cols] if a == 0 else src_sc1[:, cols]
                 else:
                     lhsT = wt_q[a][:, P * t : P * (t + 1)].bitcast(FP8X4)

@@ -43,17 +43,17 @@ def tile_list_msg_relu_noneP_kernel(
         lists = (src_list, dst_list)
 
         tab_sc = sb([P, T], U8, "tab_sc", tag="stage2")
-        ws_sc_raw = sb([P, R], U8, "ws_sc_raw", tag="g_src")
-        zeros = sb([P, R // 4], I32, "zeros", tag="tab0")
-        wd_sc_raw = sb([P, N], U8, "wd_sc_raw", tag="page0")
-        lowered = sb([P, J + R], U8, "lowered")
-        src_sc1 = lowered[:, 0:J]
-        ws_sc1 = lowered[:, J : J + R]
-        nc.gpsimd.memset(lowered[:].bitcast(I32), 0)
+        ws_sc_raw = sb([P, PASSES, R], U8, "ws_sc_raw", tag="g_src")
+        zeros = sb([P, PASSES * R // 4], I32, "zeros", tag="tab0")
+        wd_sc_raw = sb([P, N], U8, "wd_sc_raw")
+        src_sc1 = sb([P, J], U8, "src_sc1")
+        page0 = sb([P, T], F32, "page0")
+        nc.gpsimd.memset(wd_sc_raw[:].bitcast(I32), 0)
         nc.vector.memset(tab_sc[:].bitcast(I32), 0)
         nc.vector.memset(zeros[:], 0)
-        nc.vector.tensor_copy(wd_sc_raw[:].bitcast(I32), zeros[:])
-        nc.vector.memset(ws_sc_raw[:].bitcast(I32), 0)
+        nc.vector.tensor_copy(ws_sc_raw[:].rearrange("p a c -> p (a c)").bitcast(I32), zeros[:])
+        nc.vector.memset(src_sc1[:].bitcast(I32), 0)
+        nc.vector.memset(page0[:], 0.0)
 
         ws_raw = sb([P, PASSES, 2 * R], U8, "ws_raw", tag="stage1")
         wd_raw = sb([P, 2 * N], U8, "wd_raw")
@@ -87,10 +87,14 @@ def tile_list_msg_relu_noneP_kernel(
         load_and_round_wt(0, 0, "stage0")
         load_planes(nc.sync, tab_sc, 8, tab_scales)
         load_tab(0, "tab0")
-        load_planes(nc.sync, ws_sc_raw, 8, ws_scales)
+        for q in range(4):
+            nc.sync.dma_start(
+                ws_sc_raw[32 * q : 32 * q + 4, :, :].bitcast(I32),
+                ws_scales[:, 4 * q : 4 * q + 4, :].rearrange("a r c -> r a c").bitcast(I32),
+            )
 
         ws = sb([P, PASSES, 2 * R], U8, "ws")
-        ws_sc = sb([P, R], U8, "ws_sc")
+        ws_sc = sb([P, PASSES, R], U8, "ws_sc")
         nc.vector.tensor_copy(
             ws[:].bitcast(U16).rearrange("p a (t m) -> p a t m", t=PACK),
             ws_raw[:].bitcast(U16).rearrange("p a (m t) -> p a t m", t=PACK),
@@ -101,11 +105,10 @@ def tile_list_msg_relu_noneP_kernel(
         g_sc = [sb([P, J], U8, f"g_sc{l}") for l in range(2)]
         for l in range(2):
             nc.vector.tensor_copy(g_sc[l][:], tab_sc[:].indirect(lists[l][:]))
-        nc.gpsimd.dma_start(src_sc1[0 : P - 4, :].bitcast(I32), g_sc[0][4:P, :].bitcast(I32))
+        nc.sync.dma_start(src_sc1[0 : P - 4, :].bitcast(I32), g_sc[0][4:P, :].bitcast(I32))
         nc.vector.tensor_copy(
-            ws_sc[:].rearrange("p (t m) -> p t m", t=PACK), ws_sc_raw[:].rearrange("p (m t) -> p t m", t=PACK)
+            ws_sc[:].rearrange("p a (t m) -> p a t m", t=PACK), ws_sc_raw[:].rearrange("p a (m t) -> p a t m", t=PACK)
         )
-        nc.gpsimd.dma_start(ws_sc1[0 : P - 4, :].bitcast(I32), ws_sc[4:P, :].bitcast(I32))
 
         load_and_round_wt(1, 0, "stage2")
         load_and_round_wt(1, 1, "stage1")
@@ -138,8 +141,6 @@ def tile_list_msg_relu_noneP_kernel(
         nc.vector.tensor_copy(
             wd_sc[:].rearrange("p (t m) -> p t m", t=PACK), wd_sc_raw[:].rearrange("p (m t) -> p t m", t=PACK)
         )
-        page0 = sb([P, T], F32, "page0")
-        nc.gpsimd.memset(page0[:], 0.0)
         g_dst = sb([P, PASSES * J], I32, "g_dst", tag="wt_bf1")
         g_words.append([g_dst[:, a * J : (a + 1) * J] for a in range(PASSES)])
 
@@ -150,7 +151,7 @@ def tile_list_msg_relu_noneP_kernel(
             for t in range(PACK):
                 if l == 0:
                     lhsT = ws[:, a, 2 * P * t : 2 * P * (t + 1)].bitcast(FP4X4)
-                    lhsT_scale = (ws_sc if a == 0 else ws_sc1)[:, P * t : P * (t + 1)]
+                    lhsT_scale = ws_sc[:, a, P * t : P * (t + 1)]
                     rhs_scale = g_sc[0][:, cols] if a == 0 else src_sc1[:, cols]
                 else:
                     lhsT = wt_q[a][:, P * t : P * (t + 1)].bitcast(FP8X4)

@@ -18,13 +18,21 @@ MULT = mybir.AluOpType.mult
 
 P = 128
 PACK = 4
-PASSES = K // (P * PACK)
+K_PASS = P * PACK
+PASSES = K // K_PASS
+QUADS = 4
+LIST_ROWS = 16
+SRC, DST = 0, 1
 BANK_J = 128
 BANKS = J // BANK_J
 CHUNK_J = 256
 CHUNKS = J // CHUNK_J
+SRC_CUTS = ((0, 256, 512, 1024), (0, 512, 1024))
+LOWERED = 112
+EARLY_PAGES = 2
 OUT_C = 512
 OUT_CHUNKS = T // OUT_C
+V_CHUNKS = 2
 
 
 def tile_list_msg_relu_noneP_kernel(
@@ -38,25 +46,23 @@ def tile_list_msg_relu_noneP_kernel(
         def sb(shape, dtype, name, tag=None):
             return keep.tile(shape, dtype, name=name, tag=tag or name, align_bytes=64)
 
-        src_list = keep.tile([P, J // 16], U16, name="src_list")
-        dst_list = keep.tile([P, J // 16], U16, name="dst_list")
+        src_list = keep.tile([P, J // LIST_ROWS], U16, name="src_list")
+        dst_list = keep.tile([P, J // LIST_ROWS], U16, name="dst_list")
         lists = (src_list, dst_list)
 
         tab_sc = sb([P, T], U8, "tab_sc", tag="stage2")
         ws_sc_raw = sb([P, PASSES, R], U8, "ws_sc_raw", tag="g_src")
-        zeros = sb([P, PASSES * R // 4], I32, "zeros", tag="tab0")
-        wd_sc_raw = sb([P, N], U8, "wd_sc_raw")
+        zeros = sb([P, PASSES * R // 4], I32, "zeros", tag="stage0")
+        wd_sc_raw = sb([P, N], U8, "wd_sc_raw", tag="page0")
         src_sc1 = sb([P, J], U8, "src_sc1")
-        page0 = sb([P, T], F32, "page0")
         nc.gpsimd.memset(wd_sc_raw[:].bitcast(I32), 0)
-        nc.vector.memset(tab_sc[:].bitcast(I32), 0)
         nc.vector.memset(zeros[:], 0)
+        nc.vector.memset(tab_sc[:].bitcast(I32), 0)
         nc.vector.tensor_copy(ws_sc_raw[:].rearrange("p a c -> p (a c)").bitcast(I32), zeros[:])
         nc.vector.memset(src_sc1[:].bitcast(I32), 0)
-        nc.vector.memset(page0[:], 0.0)
 
         ws_raw = sb([P, PASSES, 2 * R], U8, "ws_raw", tag="stage1")
-        wd_raw = sb([P, 2 * N], U8, "wd_raw")
+        wd_raw = sb([P, 2 * N], U8, "wd_raw", tag="stage3")
         tab = []
 
         def load_tab(a, tag):
@@ -65,29 +71,28 @@ def tile_list_msg_relu_noneP_kernel(
 
         wt_bf = [sb([P, R * PACK], BF16, f"wt_bf{a}") for a in range(PASSES)]
 
-        def load_and_round_wt(a, h, tag):
-            rows = wt[a * 512 : (a + 1) * 512, :].rearrange("(p i) c -> p i c", i=PACK)
-            wt_raw = sb([P, PACK, R // 2], F32, f"wt_part{a}_{h}", tag=tag)
-            nc.sync.dma_start(wt_raw[:], rows[:, :, h * 256 : (h + 1) * 256])
+        def load_and_round_wt(a, c0, c1, tag):
+            rows = wt[a * K_PASS : (a + 1) * K_PASS, :].rearrange("(p i) c -> p i c", i=PACK)
+            wt_raw = sb([P, PACK, c1 - c0], F32, f"wt_part{a}_{c0}", tag=tag)
+            nc.sync.dma_start(wt_raw[:], rows[:, :, c0:c1])
             nc.scalar.activation(
-                wt_bf[a][:].rearrange("p (t m i) -> p m i t", t=PACK, i=PACK)[:, 64 * h : 64 * (h + 1), :, :],
+                wt_bf[a][:].rearrange("p (t m i) -> p m i t", t=PACK, i=PACK)[:, c0 // PACK : c1 // PACK, :, :],
                 wt_raw[:].rearrange("p i (m t) -> p m i t", t=PACK),
                 ACT.Copy,
             )
 
         def load_planes(eng, tile, rows, scales):
-            for q in range(4):
+            for q in range(QUADS):
                 eng.dma_start(tile[32 * q : 32 * q + rows, :].bitcast(I32), scales[:, 4 * q : 4 * q + 4, :].bitcast(I32))
 
-        nc.gpsimd.dma_start(wd_raw[:].bitcast(I32), wd_words[0].bitcast(I32))
         load_planes(nc.gpsimd, wd_sc_raw, 4, wd_scales)
         nc.sync.dma_start(ws_raw[:].bitcast(I32), ws_words.rearrange("a p c -> p a c").bitcast(I32))
+        nc.sync.dma_start(wd_raw[:].bitcast(I32), wd_words[0].bitcast(I32))
         nc.sync.dma_start(src_list[:], offs)
         nc.sync.dma_start(dst_list[:], offs2)
-        load_and_round_wt(0, 0, "stage0")
-        load_planes(nc.sync, tab_sc, 8, tab_scales)
-        load_tab(0, "tab0")
-        for q in range(4):
+        load_planes(nc.sync, tab_sc, 4 * PASSES, tab_scales)
+        load_and_round_wt(0, 0, R, "stage0")
+        for q in range(QUADS):
             nc.sync.dma_start(
                 ws_sc_raw[32 * q : 32 * q + 4, :, :].bitcast(I32),
                 ws_scales[:, 4 * q : 4 * q + 4, :].rearrange("a r c -> r a c").bitcast(I32),
@@ -99,102 +104,108 @@ def tile_list_msg_relu_noneP_kernel(
             ws[:].bitcast(U16).rearrange("p a (t m) -> p a t m", t=PACK),
             ws_raw[:].bitcast(U16).rearrange("p a (m t) -> p a t m", t=PACK),
         )
-        load_and_round_wt(0, 1, "stage1")
-        load_tab(1, "stage0")
+        wd = sb([P, 2 * N], U8, "wd")
+        nc.vector.tensor_copy(
+            wd[:].bitcast(U16).rearrange("p (t m) -> p t m", t=PACK),
+            wd_raw[:].bitcast(U16).rearrange("p (m t) -> p t m", t=PACK),
+        )
+        load_tab(0, "stage1")
+        load_tab(1, "stage3")
 
-        g_sc = [sb([P, J], U8, f"g_sc{l}") for l in range(2)]
-        for l in range(2):
-            nc.vector.tensor_copy(g_sc[l][:], tab_sc[:].indirect(lists[l][:]))
-        nc.sync.dma_start(src_sc1[0 : P - 4, :].bitcast(I32), g_sc[0][4:P, :].bitcast(I32))
+        g_sc = [sb([P, J], U8, f"g_sc{side}") for side in (SRC, DST)]
+        for side in (SRC, DST):
+            nc.vector.tensor_copy(g_sc[side][:], tab_sc[:].indirect(lists[side][:]))
+        nc.sync.dma_start(src_sc1[0:LOWERED, :].bitcast(I32), g_sc[SRC][4 : LOWERED + 4, :].bitcast(I32))
         nc.vector.tensor_copy(
             ws_sc[:].rearrange("p a (t m) -> p a t m", t=PACK), ws_sc_raw[:].rearrange("p a (m t) -> p a t m", t=PACK)
         )
 
-        load_and_round_wt(1, 0, "stage2")
-        load_and_round_wt(1, 1, "stage1")
+        load_and_round_wt(1, 0, R // 2, "stage2")
+        load_and_round_wt(1, R // 2, R, "stage0")
+
         g_src = sb([P, PASSES * J], I32, "g_src")
         g_words = [[g_src[:, a * J : (a + 1) * J] for a in range(PASSES)]]
 
-        def gather_words(l, a, j0, j1):
+        def gather_words(side, a, j0, j1):
             nc.vector.tensor_copy(
-                g_words[l][a][:, j0:j1].bitcast(U32), tab[a][:].bitcast(U32).indirect(lists[l][:, j0 // 16 : j1 // 16])
+                g_words[side][a][:, j0:j1].bitcast(U32),
+                tab[a][:].bitcast(U32).indirect(lists[side][:, j0 // LIST_ROWS : j1 // LIST_ROWS]),
             )
 
-        for j0, j1 in ((0, 256), (256, 512), (512, 1024)):
-            gather_words(0, 0, j0, j1)
-        gather_words(0, 1, 0, 512)
-        gather_words(0, 1, 512, 1024)
+        for a in range(PASSES):
+            for j0, j1 in zip(SRC_CUTS[a][:-1], SRC_CUTS[a][1:]):
+                gather_words(SRC, a, j0, j1)
 
         wt_q = [sb([P, R], I32, f"wt_q{a}") for a in range(PASSES)]
         wt_sc = [sb([P, R], U8, f"wt_sc{a}") for a in range(PASSES)]
         for a in range(PASSES):
             nc.vector.quantize_mx(wt_q[a][:].bitcast(FP8X4), wt_sc[a][:], wt_bf[a][:])
 
-        edge_w = sb([P, J], F32, "edge_w", tag="stage2")
+        edge_w = sb([P, J], F32, "edge_w", tag="stage0")
         nc.sync.dma_start(edge_w[:], wgo)
-        wd = sb([P, 2 * N], U8, "wd", tag="stage1")
-        nc.vector.tensor_copy(
-            wd[:].bitcast(U16).rearrange("p (t m) -> p t m", t=PACK),
-            wd_raw[:].bitcast(U16).rearrange("p (m t) -> p t m", t=PACK),
-        )
         wd_sc = sb([P, N], U8, "wd_sc", tag="wt_bf0")
         nc.vector.tensor_copy(
             wd_sc[:].rearrange("p (t m) -> p t m", t=PACK), wd_sc_raw[:].rearrange("p (m t) -> p t m", t=PACK)
         )
+        pages = [sb([P, T], F32, "page0"), sb([P, T], F32, "page1", tag="stage2")]
+        for page in pages:
+            nc.gpsimd.memset(page[:], 0.0)
         g_dst = sb([P, PASSES * J], I32, "g_dst", tag="wt_bf1")
         g_words.append([g_dst[:, a * J : (a + 1) * J] for a in range(PASSES)])
 
         acc = [psum.tile([P, PACK, BANK_J], F32, name=f"acc{b}", tag=f"bank{b}") for b in range(BANKS)]
 
-        def first_product(l, a, b):
+        def first_product(side, a, b):
             cols = slice(b * BANK_J, (b + 1) * BANK_J)
             for t in range(PACK):
-                if l == 0:
+                if side == SRC:
                     lhsT = ws[:, a, 2 * P * t : 2 * P * (t + 1)].bitcast(FP4X4)
                     lhsT_scale = ws_sc[:, a, P * t : P * (t + 1)]
-                    rhs_scale = g_sc[0][:, cols] if a == 0 else src_sc1[:, cols]
+                    rhs_scale = g_sc[SRC][:, cols] if a == 0 else src_sc1[:, cols]
                 else:
                     lhsT = wt_q[a][:, P * t : P * (t + 1)].bitcast(FP8X4)
                     lhsT_scale = wt_sc[a][:, P * t : P * (t + 1)]
-                    rhs_scale = g_sc[1][4 * a : P, cols]
+                    rhs_scale = g_sc[DST][4 * a : P, cols]
                 nc.tensor.matmul_mx(
                     acc[b][:, t, :],
                     lhsT=lhsT,
                     lhsT_scale=lhsT_scale,
-                    rhs=g_words[l][a][:, cols].bitcast(FP8X4),
+                    rhs=g_words[side][a][:, cols].bitcast(FP8X4),
                     rhs_scale=rhs_scale,
-                    start=(l == 0 and a == 0 and t == 0),
-                    stop=(l == 1 and a == PASSES - 1 and t == PACK - 1),
+                    start=(side == SRC and a == 0 and t == 0),
+                    stop=(side == DST and a == PASSES - 1 and t == PACK - 1),
                 )
 
         for a in range(PASSES):
             for b in range(BANKS):
-                first_product(0, a, b)
+                first_product(SRC, a, b)
 
-        h_bf = sb([P, J * PACK], BF16, "h_bf", tag="slot1")
-        h_q = sb([P, J], I32, "h_q", tag="slot2")
-        h_sc = sb([P, J], U8, "h_sc", tag="slot3")
+        h_bf = sb([P, J * PACK], BF16, "h_bf", tag="late_page2")
+        h_q = sb([P, J], I32, "h_q", tag="late_page3")
+        h_sc = sb([P, J], U8, "h_sc")
         y = sb([P, PACK, J], F32, "y")
 
-        def scatter(page, t, j0, j1):
+        def scatter(t, j0, j1):
             nc.vector.tensor_tensor(
-                page[:].indirect(dst_list[:, j0 // 16 : j1 // 16]), y[:, t, j0:j1], edge_w[:, j0:j1], MULT
+                pages[t][:].indirect(dst_list[:, j0 // LIST_ROWS : j1 // LIST_ROWS]),
+                y[:, t, j0:j1],
+                edge_w[:, j0:j1],
+                MULT,
             )
 
-        def finish_first(c):
-            j0, j1 = c * CHUNK_J, (c + 1) * CHUNK_J
+        def finish_first_product(c):
             for a in range(PASSES):
-                gather_words(1, a, j0, j1)
+                gather_words(DST, a, c * CHUNK_J, (c + 1) * CHUNK_J)
             for b in (2 * c, 2 * c + 1):
                 for a in range(PASSES):
-                    first_product(1, a, b)
+                    first_product(DST, a, b)
                 nc.scalar.activation(
-                    h_bf[:, b * 512 : (b + 1) * 512].rearrange("p (j t) -> p j t", t=PACK),
+                    h_bf[:, b * BANK_J * PACK : (b + 1) * BANK_J * PACK].rearrange("p (j t) -> p j t", t=PACK),
                     acc[b][:].rearrange("p t j -> p j t"),
                     ACT.Relu,
                 )
 
-        def second(c):
+        def second_product(c):
             j0, j1 = c * CHUNK_J, (c + 1) * CHUNK_J
             nc.vector.quantize_mx(h_q[:, j0:j1].bitcast(FP8X4), h_sc[:, j0:j1], h_bf[:, PACK * j0 : PACK * j1])
             for u in range(2):
@@ -212,51 +223,51 @@ def tile_list_msg_relu_noneP_kernel(
                     )
                 nc.scalar.activation(y[:, 2 * u : 2 * u + 2, j0:j1], res[:], ACT.Copy)
 
-        for c in range(CHUNKS + 2):
-            if c < CHUNKS:
-                finish_first(c)
-            if 1 <= c <= CHUNKS:
-                second(c - 1)
-            if c >= 2:
-                scatter(page0, 0, (c - 2) * CHUNK_J, (c - 1) * CHUNK_J)
+        for step in range(CHUNKS + 2):
+            if step < CHUNKS:
+                finish_first_product(step)
+            if 1 <= step <= CHUNKS:
+                second_product(step - 1)
+            if step >= 2:
+                for t in range(EARLY_PAGES):
+                    scatter(t, (step - 2) * CHUNK_J, (step - 1) * CHUNK_J)
 
-        pages = [page0] + [sb([P, T], F32, f"page{t}", tag=f"slot{t}") for t in range(1, PACK)]
-        for t in range(1, PACK):
+        for t in range(EARLY_PAGES, PACK):
+            pages.append(sb([P, T], F32, f"page{t}", tag=f"late_page{t}"))
             nc.gpsimd.memset(pages[t][:], 0.0)
 
-        o_bf = sb([P, T * PACK], BF16, "o_bf")
-        o_dealt = o_bf[:].rearrange("p (c t) -> p c t", t=PACK)
+        pairs = [sb([P, 2, OUT_C, 2], BF16, f"pairs{c}") for c in range(OUT_CHUNKS)]
+        o_bf = [sb([P, OUT_C * PACK], BF16, f"o_bf{c}") for c in range(OUT_CHUNKS)]
         o_q = [sb([P, OUT_C], I32, f"o_q{c}") for c in range(OUT_CHUNKS)]
         o_sc = sb([P, T], U8, "o_sc")
         out_rows = out_0.rearrange("(p t) c -> p t c", t=PACK)
         out_words = out_1[0].rearrange("p c i -> p (c i)").bitcast(I32)
-        V_COLS = 2 * OUT_C
+        last = PACK - 1
 
         for t in range(PACK):
-            if t > 0:
-                scatter(pages[t], t, 0, J)
+            if t >= EARLY_PAGES:
+                scatter(t, 0, J)
             nc.sync.dma_start(out_rows[:, t, :], pages[t][:])
-            if t < 2:
-                nc.scalar.activation(o_dealt[:, :, t], pages[t][:], ACT.Copy)
-            elif t == 2:
-                nc.scalar.activation(
-                    o_dealt[:, 0:V_COLS, 2:4], pages[t][:, 0:V_COLS].unsqueeze(2).to_broadcast([P, V_COLS, 2]), ACT.Copy
-                )
-                nc.scalar.activation(o_dealt[:, V_COLS:T, t], pages[t][:, V_COLS:T], ACT.Copy)
-            else:
-                for c in range(OUT_CHUNKS):
-                    cols = slice(c * OUT_C, (c + 1) * OUT_C)
-                    if c * OUT_C < V_COLS:
-                        nc.vector.tensor_copy(o_dealt[:, cols, t], pages[t][:, cols])
+            for c in range(OUT_CHUNKS):
+                part = pages[t][:, c * OUT_C : (c + 1) * OUT_C]
+                if t == last - 1 and c < V_CHUNKS:
+                    nc.scalar.activation(pairs[c][:, 1, :, :], part.unsqueeze(2).to_broadcast([P, OUT_C, 2]), ACT.Copy)
+                elif t == last and c < V_CHUNKS:
+                    nc.vector.tensor_copy(pairs[c][:, 1, :, 1], part)
+                else:
+                    nc.scalar.activation(pairs[c][:, t // 2, :, t % 2], part, ACT.Copy)
+                if t == last:
+                    woven = o_bf[c][:].bitcast(F32).rearrange("p (c u) -> p c u", u=2)
+                    words = pairs[c][:].rearrange("p u c e -> p u (c e)").bitcast(F32).rearrange("p u c -> p c u")
+                    if c < V_CHUNKS:
+                        nc.vector.tensor_copy(woven, words)
                     else:
-                        nc.scalar.activation(o_dealt[:, cols, t], pages[t][:, cols], ACT.Copy)
+                        nc.scalar.copy(woven, words)
 
         for c in range(OUT_CHUNKS):
             cols = slice(c * OUT_C, (c + 1) * OUT_C)
-            nc.vector.quantize_mx(
-                o_q[c][:].bitcast(FP8X4), o_sc[:, cols], o_bf[:, PACK * c * OUT_C : PACK * (c + 1) * OUT_C]
-            )
+            nc.vector.quantize_mx(o_q[c][:].bitcast(FP8X4), o_sc[:, cols], o_bf[c][:])
             nc.sync.dma_start(out_words[:, cols], o_q[c][:])
-        for q in range(4):
+        for q in range(QUADS):
             eng = nc.scalar if q % 2 else nc.sync
             eng.dma_start(out_2[0, 4 * q : 4 * q + 4, :].bitcast(I32), o_sc[32 * q : 32 * q + 4, :].bitcast(I32))

@@ -27,9 +27,10 @@ BANK_J = 128
 BANKS = J // BANK_J
 CHUNK_J = 256
 CHUNKS = J // CHUNK_J
-SRC_CUTS = ((0, 256, 512, 1024), (0, 512, 1024))
+HALF = J // 2
+PAGE_B = 4 * T
+PART_B = 4 * PACK * R // 2
 LOWERED = 112
-EARLY_PAGES = 2
 OUT_C = 512
 OUT_CHUNKS = T // OUT_C
 V_CHUNKS = 2
@@ -41,65 +42,73 @@ def tile_list_msg_relu_noneP_kernel(
     nc = tc.nc
     with ExitStack() as ctx:
         keep = ctx.enter_context(tc.tile_pool(name="keep", bufs=1))
+        shared = ctx.enter_context(tc.tile_pool(name="shared", bufs=1))
         psum = ctx.enter_context(tc.psum_pool(name="psum", bufs=1))
 
         def sb(shape, dtype, name, tag=None):
             return keep.tile(shape, dtype, name=name, tag=tag or name, align_bytes=64)
 
+        def placed(shape, dtype, name, offset):
+            return shared.tile(shape, dtype, name=name, tag=name, align_bytes=64, offset=offset)
+
         src_list = keep.tile([P, J // LIST_ROWS], U16, name="src_list")
         dst_list = keep.tile([P, J // LIST_ROWS], U16, name="dst_list")
         lists = (src_list, dst_list)
 
-        tab_sc = sb([P, T], U8, "tab_sc", tag="stage2")
-        ws_sc_raw = sb([P, PASSES, R], U8, "ws_sc_raw", tag="g_src")
-        zeros = sb([P, PASSES * R // 4], I32, "zeros", tag="stage0")
-        wd_sc_raw = sb([P, N], U8, "wd_sc_raw", tag="page0")
+        tab_sc = sb([P, T], U8, "tab_sc")
+        w_sc_raw = sb([P, R], U8, "w_sc_raw", tag="g_first")
+        ws_sc1 = sb([P, R], U8, "ws_sc1")
+        wd_sc_raw = sb([P, N], U8, "wd_sc_raw")
         src_sc1 = sb([P, J], U8, "src_sc1")
+        zeros_a = sb([P, R // 4], I32, "zeros_a", tag="tab")
+        zeros_b = sb([P, R // 4], I32, "zeros_b", tag="wt_raw")
+        nc.gpsimd.memset(tab_sc[:].bitcast(I32), 0)
         nc.gpsimd.memset(wd_sc_raw[:].bitcast(I32), 0)
-        nc.vector.memset(zeros[:], 0)
-        nc.vector.memset(tab_sc[:].bitcast(I32), 0)
-        nc.vector.tensor_copy(ws_sc_raw[:].rearrange("p a c -> p (a c)").bitcast(I32), zeros[:])
+        nc.vector.memset(zeros_a[:], 0)
+        nc.vector.memset(zeros_b[:], 0)
+        nc.vector.tensor_copy(w_sc_raw[:].bitcast(I32), zeros_a[:])
+        nc.vector.tensor_copy(ws_sc1[:].bitcast(I32), zeros_b[:])
         nc.vector.memset(src_sc1[:].bitcast(I32), 0)
 
-        ws_raw = sb([P, PASSES, 2 * R], U8, "ws_raw", tag="stage1")
-        wd_raw = sb([P, 2 * N], U8, "wd_raw", tag="stage3")
-        tab = []
+        ws_raw = placed([P, PASSES, 2 * R], U8, "ws_raw", PAGE_B - 2 * R)
+        wd_raw = placed([P, 2 * N], U8, "wd_raw", 2 * PAGE_B + PART_B - N)
+        tab = sb([P, PASSES * T], I32, "tab")
+        wt_bf = sb([P, PASSES * R * PACK], BF16, "wt_bf")
 
-        def load_tab(a, tag):
-            tab.append(sb([P, T], I32, f"tab{a}", tag=tag))
-            nc.sync.dma_start(tab[a][:], tab_words[a].rearrange("p t i -> p (t i)").bitcast(I32))
+        def load_tab(a):
+            nc.sync.dma_start(tab[:, a * T : (a + 1) * T], tab_words[a].rearrange("p t i -> p (t i)").bitcast(I32))
 
-        wt_bf = [sb([P, R * PACK], BF16, f"wt_bf{a}") for a in range(PASSES)]
-
-        def load_and_round_wt(a, c0, c1, tag):
+        def load_and_round_wt(a, c0, c1, part):
             rows = wt[a * K_PASS : (a + 1) * K_PASS, :].rearrange("(p i) c -> p i c", i=PACK)
-            wt_raw = sb([P, PACK, c1 - c0], F32, f"wt_part{a}_{c0}", tag=tag)
-            nc.sync.dma_start(wt_raw[:], rows[:, :, c0:c1])
+            nc.sync.dma_start(part[:], rows[:, :, c0:c1])
             nc.scalar.activation(
-                wt_bf[a][:].rearrange("p (t m i) -> p m i t", t=PACK, i=PACK)[:, c0 // PACK : c1 // PACK, :, :],
-                wt_raw[:].rearrange("p i (m t) -> p m i t", t=PACK),
+                wt_bf[:, a * PACK * R : (a + 1) * PACK * R].rearrange("p (t m i) -> p m i t", t=PACK, i=PACK)[
+                    :, c0 // PACK : c1 // PACK, :, :
+                ],
+                part[:].rearrange("p i (m t) -> p m i t", t=PACK),
                 ACT.Copy,
             )
 
-        def load_planes(eng, tile, rows, scales):
+        def load_planes(eng, tile, row0, rows, scales):
             for q in range(QUADS):
-                eng.dma_start(tile[32 * q : 32 * q + rows, :].bitcast(I32), scales[:, 4 * q : 4 * q + 4, :].bitcast(I32))
+                eng.dma_start(
+                    tile[32 * q + row0 : 32 * q + row0 + rows, :].bitcast(I32), scales[:, 4 * q : 4 * q + 4, :].bitcast(I32)
+                )
 
-        load_planes(nc.gpsimd, wd_sc_raw, 4, wd_scales)
+        nc.sync.dma_start(src_list[:], offs)
         nc.sync.dma_start(ws_raw[:].bitcast(I32), ws_words.rearrange("a p c -> p a c").bitcast(I32))
         nc.sync.dma_start(wd_raw[:].bitcast(I32), wd_words[0].bitcast(I32))
-        nc.sync.dma_start(src_list[:], offs)
         nc.sync.dma_start(dst_list[:], offs2)
-        load_planes(nc.sync, tab_sc, 4 * PASSES, tab_scales)
-        load_and_round_wt(0, 0, R, "stage0")
-        for q in range(QUADS):
-            nc.sync.dma_start(
-                ws_sc_raw[32 * q : 32 * q + 4, :, :].bitcast(I32),
-                ws_scales[:, 4 * q : 4 * q + 4, :].rearrange("a r c -> r a c").bitcast(I32),
-            )
+        load_planes(nc.sync, tab_sc, 0, 4 * PASSES, tab_scales)
+        load_tab(0)
+        load_planes(nc.sync, w_sc_raw, 0, 4 * PASSES, ws_scales)
+        load_planes(nc.gpsimd, wd_sc_raw, 0, 4, wd_scales)
+        load_and_round_wt(0, 0, R, sb([P, PACK, R], F32, "wt_raw"))
+        load_tab(1)
+        load_and_round_wt(1, 0, R // 2, placed([P, PACK, R // 2], F32, "wt_a", PAGE_B))
+        load_and_round_wt(1, R // 2, R, placed([P, PACK, R // 2], F32, "wt_b", 2 * PAGE_B + PART_B))
 
         ws = sb([P, PASSES, 2 * R], U8, "ws")
-        ws_sc = sb([P, PASSES, R], U8, "ws_sc")
         nc.vector.tensor_copy(
             ws[:].bitcast(U16).rearrange("p a (t m) -> p a t m", t=PACK),
             ws_raw[:].bitcast(U16).rearrange("p a (m t) -> p a t m", t=PACK),
@@ -109,109 +118,90 @@ def tile_list_msg_relu_noneP_kernel(
             wd[:].bitcast(U16).rearrange("p (t m) -> p t m", t=PACK),
             wd_raw[:].bitcast(U16).rearrange("p (m t) -> p t m", t=PACK),
         )
-        load_tab(0, "stage1")
-        load_tab(1, "stage3")
+        pages = [placed([P, T], F32, "page0", 0), placed([P, T], F32, "page1", PAGE_B + PART_B)]
+        for page in pages:
+            nc.gpsimd.memset(page[:], 0.0)
 
         g_sc = [sb([P, J], U8, f"g_sc{side}") for side in (SRC, DST)]
         for side in (SRC, DST):
             nc.vector.tensor_copy(g_sc[side][:], tab_sc[:].indirect(lists[side][:]))
         nc.sync.dma_start(src_sc1[0:LOWERED, :].bitcast(I32), g_sc[SRC][4 : LOWERED + 4, :].bitcast(I32))
+        w_sc = sb([P, R], U8, "w_sc")
         nc.vector.tensor_copy(
-            ws_sc[:].rearrange("p a (t m) -> p a t m", t=PACK), ws_sc_raw[:].rearrange("p a (m t) -> p a t m", t=PACK)
+            w_sc[:].rearrange("p (t m) -> p t m", t=PACK), w_sc_raw[:].rearrange("p (m t) -> p t m", t=PACK)
         )
+        nc.sync.dma_start(ws_sc1[0:LOWERED, :].bitcast(I32), w_sc[4 : LOWERED + 4, :].bitcast(I32))
+        ws_sc = [w_sc, ws_sc1]
+        edge_w = sb([P, J], F32, "edge_w", tag="tab_sc")
+        nc.sync.dma_start(edge_w[:], wgo)
 
-        load_and_round_wt(1, 0, R // 2, "stage2")
-        load_and_round_wt(1, R // 2, R, "stage0")
+        g_words = {}
 
-        g_src = sb([P, PASSES * J], I32, "g_src")
-        g_words = [[g_src[:, a * J : (a + 1) * J] for a in range(PASSES)]]
-
-        def gather_words(side, a, j0, j1):
+        def gather_words(half, side, a, dst):
+            g_words[(half, side, a)] = dst
             nc.vector.tensor_copy(
-                g_words[side][a][:, j0:j1].bitcast(U32),
-                tab[a][:].bitcast(U32).indirect(lists[side][:, j0 // LIST_ROWS : j1 // LIST_ROWS]),
+                dst.bitcast(U32),
+                tab[:, a * T : (a + 1) * T]
+                .bitcast(U32)
+                .indirect(lists[side][:, half * HALF // LIST_ROWS : (half + 1) * HALF // LIST_ROWS]),
             )
 
+        g_first = sb([P, 2 * PASSES * HALF], I32, "g_first")
         for a in range(PASSES):
-            for j0, j1 in zip(SRC_CUTS[a][:-1], SRC_CUTS[a][1:]):
-                gather_words(SRC, a, j0, j1)
+            for side in (SRC, DST):
+                k = side * PASSES + a
+                gather_words(0, side, a, g_first[:, k * HALF : (k + 1) * HALF])
 
-        wt_q = [sb([P, R], I32, f"wt_q{a}") for a in range(PASSES)]
-        wt_sc = [sb([P, R], U8, f"wt_sc{a}") for a in range(PASSES)]
-        for a in range(PASSES):
-            nc.vector.quantize_mx(wt_q[a][:].bitcast(FP8X4), wt_sc[a][:], wt_bf[a][:])
-
-        edge_w = sb([P, J], F32, "edge_w", tag="stage0")
-        nc.sync.dma_start(edge_w[:], wgo)
-        wd_sc = sb([P, N], U8, "wd_sc", tag="wt_bf0")
+        wt_q = sb([P, PASSES * R], I32, "wt_q")
+        wt_sc = sb([P, PASSES * R], U8, "wt_sc")
+        nc.vector.quantize_mx(wt_q[:].bitcast(FP8X4), wt_sc[:], wt_bf[:])
+        wd_sc = placed([P, N], U8, "wd_sc", 2 * PAGE_B + 2 * PART_B - N)
         nc.vector.tensor_copy(
             wd_sc[:].rearrange("p (t m) -> p t m", t=PACK), wd_sc_raw[:].rearrange("p (m t) -> p t m", t=PACK)
         )
-        pages = [sb([P, T], F32, "page0"), sb([P, T], F32, "page1", tag="stage2")]
-        for page in pages:
-            nc.gpsimd.memset(page[:], 0.0)
-        g_dst = sb([P, PASSES * J], I32, "g_dst", tag="wt_bf1")
-        g_words.append([g_dst[:, a * J : (a + 1) * J] for a in range(PASSES)])
 
         acc = [psum.tile([P, PACK, BANK_J], F32, name=f"acc{b}", tag=f"bank{b}") for b in range(BANKS)]
 
         def first_product(side, a, b):
             cols = slice(b * BANK_J, (b + 1) * BANK_J)
+            half, j0 = divmod(b * BANK_J, HALF)
             for t in range(PACK):
                 if side == SRC:
                     lhsT = ws[:, a, 2 * P * t : 2 * P * (t + 1)].bitcast(FP4X4)
-                    lhsT_scale = ws_sc[:, a, P * t : P * (t + 1)]
+                    lhsT_scale = ws_sc[a][:, P * t : P * (t + 1)]
                     rhs_scale = g_sc[SRC][:, cols] if a == 0 else src_sc1[:, cols]
                 else:
-                    lhsT = wt_q[a][:, P * t : P * (t + 1)].bitcast(FP8X4)
-                    lhsT_scale = wt_sc[a][:, P * t : P * (t + 1)]
+                    lhsT = wt_q[:, a * R + P * t : a * R + P * (t + 1)].bitcast(FP8X4)
+                    lhsT_scale = wt_sc[:, a * R + P * t : a * R + P * (t + 1)]
                     rhs_scale = g_sc[DST][4 * a : P, cols]
                 nc.tensor.matmul_mx(
                     acc[b][:, t, :],
                     lhsT=lhsT,
                     lhsT_scale=lhsT_scale,
-                    rhs=g_words[side][a][:, cols].bitcast(FP8X4),
+                    rhs=g_words[(half, side, a)][:, j0 : j0 + BANK_J].bitcast(FP8X4),
                     rhs_scale=rhs_scale,
                     start=(side == SRC and a == 0 and t == 0),
                     stop=(side == DST and a == PASSES - 1 and t == PACK - 1),
                 )
 
-        for a in range(PASSES):
-            for b in range(BANKS):
-                first_product(SRC, a, b)
-
-        h_bf = sb([P, J * PACK], BF16, "h_bf", tag="late_page2")
-        h_q = sb([P, J], I32, "h_q", tag="late_page3")
+        h_q = sb([P, J], I32, "h_q")
         h_sc = sb([P, J], U8, "h_sc")
         y = sb([P, PACK, J], F32, "y")
 
-        def scatter(t, j0, j1):
-            nc.vector.tensor_tensor(
-                pages[t][:].indirect(dst_list[:, j0 // LIST_ROWS : j1 // LIST_ROWS]),
-                y[:, t, j0:j1],
-                edge_w[:, j0:j1],
-                MULT,
+        def relu(b, h_bf, j0):
+            nc.scalar.activation(
+                h_bf[:, (b * BANK_J - j0) * PACK : ((b + 1) * BANK_J - j0) * PACK].rearrange("p (j t) -> p j t", t=PACK),
+                acc[b][:].rearrange("p t j -> p j t"),
+                ACT.Relu,
             )
 
-        def finish_first_product(c):
-            for a in range(PASSES):
-                gather_words(DST, a, c * CHUNK_J, (c + 1) * CHUNK_J)
-            for b in (2 * c, 2 * c + 1):
-                for a in range(PASSES):
-                    first_product(DST, a, b)
-                nc.scalar.activation(
-                    h_bf[:, b * BANK_J * PACK : (b + 1) * BANK_J * PACK].rearrange("p (j t) -> p j t", t=PACK),
-                    acc[b][:].rearrange("p t j -> p j t"),
-                    ACT.Relu,
-                )
-
-        def second_product(c):
-            j0, j1 = c * CHUNK_J, (c + 1) * CHUNK_J
-            nc.vector.quantize_mx(h_q[:, j0:j1].bitcast(FP8X4), h_sc[:, j0:j1], h_bf[:, PACK * j0 : PACK * j1])
-            for u in range(2):
-                res = psum.tile([P, 2, CHUNK_J], F32, name=f"res{c}_{u}", tag=f"bank{2 * c + u}")
-                for e in range(2):
-                    t = 2 * u + e
+        def second_product(j0, j1, h_bf):
+            nc.vector.quantize_mx(h_q[:, j0:j1].bitcast(FP8X4), h_sc[:, j0:j1], h_bf[:])
+            per_bank = BANK_J * PACK // (j1 - j0)
+            for u in range(PACK // per_bank):
+                res = psum.tile([P, per_bank, j1 - j0], F32, name=f"res{j0}_{u}", tag=f"bank{j0 // BANK_J + u}")
+                for e in range(per_bank):
+                    t = per_bank * u + e
                     nc.tensor.matmul_mx(
                         res[:, e, :],
                         lhsT=wd[:, 2 * P * t : 2 * P * (t + 1)].bitcast(FP4X4),
@@ -221,20 +211,50 @@ def tile_list_msg_relu_noneP_kernel(
                         start=True,
                         stop=True,
                     )
-                nc.scalar.activation(y[:, 2 * u : 2 * u + 2, j0:j1], res[:], ACT.Copy)
+                nc.scalar.activation(y[:, per_bank * u : per_bank * (u + 1), j0:j1], res[:], ACT.Copy)
 
-        for step in range(CHUNKS + 2):
-            if step < CHUNKS:
-                finish_first_product(step)
-            if 1 <= step <= CHUNKS:
-                second_product(step - 1)
-            if step >= 2:
-                for t in range(EARLY_PAGES):
-                    scatter(t, (step - 2) * CHUNK_J, (step - 1) * CHUNK_J)
+        def scatter(t, j0, j1):
+            nc.vector.tensor_tensor(
+                pages[t][:].indirect(dst_list[:, j0 // LIST_ROWS : j1 // LIST_ROWS]),
+                y[:, t, j0:j1],
+                edge_w[:, j0:j1],
+                MULT,
+            )
 
-        for t in range(EARLY_PAGES, PACK):
-            pages.append(sb([P, T], F32, f"page{t}", tag=f"late_page{t}"))
+        half_banks = BANKS // 2
+        for a in range(PASSES):
+            for b in range(half_banks):
+                first_product(SRC, a, b)
+        h_first = [sb([P, CHUNK_J * PACK], BF16, f"h_first{c}") for c in range(2)]
+        for b in range(half_banks):
+            for a in range(PASSES):
+                first_product(DST, a, b)
+            relu(b, h_first[b // 2], b // 2 * CHUNK_J)
+
+        g_src = sb([P, PASSES * HALF], I32, "g_src", tag="wt_bf")
+        for a in range(PASSES):
+            gather_words(1, SRC, a, g_src[:, a * HALF : (a + 1) * HALF])
+        for a in range(PASSES):
+            second_product(a * CHUNK_J, (a + 1) * CHUNK_J, h_first[a])
+            g_dst = sb([P, HALF], I32, f"g_dst{a}", tag=f"h_first{a}")
+            gather_words(1, DST, a, g_dst[:])
+        for side in (SRC, DST):
+            for a in range(PASSES):
+                for b in range(half_banks, BANKS):
+                    first_product(side, a, b)
+        h_second = sb([P, HALF * PACK], BF16, "h_second")
+        for b in range(half_banks, BANKS):
+            relu(b, h_second, HALF)
+
+        scatter(0, 0, CHUNK_J)
+        scatter(1, 0, HALF)
+        scatter(0, CHUNK_J, HALF)
+        second_product(HALF, J, h_second)
+        pages.append(sb([P, T], F32, "page2", tag="h_first1"))
+        pages.append(sb([P, T], F32, "page3", tag="h_second"))
+        for t in (2, 3):
             nc.gpsimd.memset(pages[t][:], 0.0)
+        scatter(2, 0, HALF)
 
         pairs = [sb([P, 2, OUT_C, 2], BF16, f"pairs{c}") for c in range(OUT_CHUNKS)]
         o_bf = [sb([P, OUT_C * PACK], BF16, f"o_bf{c}") for c in range(OUT_CHUNKS)]
@@ -245,8 +265,7 @@ def tile_list_msg_relu_noneP_kernel(
         last = PACK - 1
 
         for t in range(PACK):
-            if t >= EARLY_PAGES:
-                scatter(t, 0, J)
+            scatter(t, HALF if t < last else 0, J)
             nc.sync.dma_start(out_rows[:, t, :], pages[t][:])
             for c in range(OUT_CHUNKS):
                 part = pages[t][:, c * OUT_C : (c + 1) * OUT_C]

@@ -29,7 +29,6 @@ CHUNK_J = 256
 CHUNKS = J // CHUNK_J
 HALF = J // 2
 PAGE_B = 4 * T
-PART_B = 4 * PACK * R // 2
 LOWERED = 112
 OUT_C = 512
 OUT_CHUNKS = T // OUT_C
@@ -60,19 +59,20 @@ def tile_list_msg_relu_noneP_kernel(
         ws_sc1 = sb([P, R], U8, "ws_sc1")
         wd_sc_raw = sb([P, N], U8, "wd_sc_raw")
         src_sc1 = sb([P, J], U8, "src_sc1")
-        zeros_a = sb([P, R // 4], I32, "zeros_a", tag="tab")
-        zeros_b = sb([P, R // 4], I32, "zeros_b", tag="wt_raw")
+        zeros = placed([P, 6 * T], I32, "zeros", 0)
         nc.gpsimd.memset(tab_sc[:].bitcast(I32), 0)
-        nc.gpsimd.memset(wd_sc_raw[:].bitcast(I32), 0)
-        nc.vector.memset(zeros_a[:], 0)
-        nc.vector.memset(zeros_b[:], 0)
-        nc.vector.tensor_copy(w_sc_raw[:].bitcast(I32), zeros_a[:])
-        nc.vector.tensor_copy(ws_sc1[:].bitcast(I32), zeros_b[:])
+        nc.vector.memset(zeros[:, 0 : R // 4], 0)
+        nc.vector.tensor_copy(w_sc_raw[:].bitcast(I32), zeros[:, 0 : R // 4])
+        nc.vector.tensor_copy(ws_sc1[:].bitcast(I32), zeros[:, 0 : R // 4])
         nc.vector.memset(src_sc1[:].bitcast(I32), 0)
+        nc.vector.memset(wd_sc_raw[:].bitcast(I32), 0)
+        pages = [placed([P, T], F32, "page0", 0), placed([P, T], F32, "page1", 3 * PAGE_B)]
+        for page in pages:
+            nc.vector.memset(page[:].bitcast(I32), 0)
 
-        ws_raw = placed([P, PASSES, 2 * R], U8, "ws_raw", PAGE_B - 2 * R)
-        wd_raw = placed([P, 2 * N], U8, "wd_raw", 2 * PAGE_B + PART_B - N)
-        tab = sb([P, PASSES * T], I32, "tab")
+        ws_raw = sb([P, PASSES, 2 * R], U8, "ws_raw")
+        wd_raw = sb([P, 2 * N], U8, "wd_raw")
+        tab = placed([P, PASSES * T], I32, "tab", PAGE_B)
         wt_bf = sb([P, PASSES * R * PACK], BF16, "wt_bf")
 
         def load_tab(a):
@@ -102,11 +102,10 @@ def tile_list_msg_relu_noneP_kernel(
         load_planes(nc.sync, tab_sc, 0, 4 * PASSES, tab_scales)
         load_tab(0)
         load_planes(nc.sync, w_sc_raw, 0, 4 * PASSES, ws_scales)
-        load_planes(nc.gpsimd, wd_sc_raw, 0, 4, wd_scales)
-        load_and_round_wt(0, 0, R, sb([P, PACK, R], F32, "wt_raw"))
+        load_and_round_wt(0, 0, R, placed([P, PACK, R], F32, "wt_raw", 4 * PAGE_B))
         load_tab(1)
-        load_and_round_wt(1, 0, R // 2, placed([P, PACK, R // 2], F32, "wt_a", PAGE_B))
-        load_and_round_wt(1, R // 2, R, placed([P, PACK, R // 2], F32, "wt_b", 2 * PAGE_B + PART_B))
+        load_and_round_wt(1, 0, R // 2, placed([P, PACK, R // 2], F32, "wt_a", 5 * PAGE_B))
+        load_and_round_wt(1, R // 2, R, placed([P, PACK, R // 2], F32, "wt_b", 5 * PAGE_B + PAGE_B // 2))
 
         ws = sb([P, PASSES, 2 * R], U8, "ws")
         nc.vector.tensor_copy(
@@ -118,9 +117,6 @@ def tile_list_msg_relu_noneP_kernel(
             wd[:].bitcast(U16).rearrange("p (t m) -> p t m", t=PACK),
             wd_raw[:].bitcast(U16).rearrange("p (m t) -> p t m", t=PACK),
         )
-        pages = [placed([P, T], F32, "page0", 0), placed([P, T], F32, "page1", PAGE_B + PART_B)]
-        for page in pages:
-            nc.gpsimd.memset(page[:], 0.0)
 
         g_sc = [sb([P, J], U8, f"g_sc{side}") for side in (SRC, DST)]
         for side in (SRC, DST):
@@ -132,6 +128,7 @@ def tile_list_msg_relu_noneP_kernel(
         )
         nc.sync.dma_start(ws_sc1[0:LOWERED, :].bitcast(I32), w_sc[4 : LOWERED + 4, :].bitcast(I32))
         ws_sc = [w_sc, ws_sc1]
+        load_planes(nc.sync, wd_sc_raw, 0, 4, wd_scales)
         edge_w = sb([P, J], F32, "edge_w", tag="tab_sc")
         nc.sync.dma_start(edge_w[:], wgo)
 
@@ -155,7 +152,7 @@ def tile_list_msg_relu_noneP_kernel(
         wt_q = sb([P, PASSES * R], I32, "wt_q")
         wt_sc = sb([P, PASSES * R], U8, "wt_sc")
         nc.vector.quantize_mx(wt_q[:].bitcast(FP8X4), wt_sc[:], wt_bf[:])
-        wd_sc = placed([P, N], U8, "wd_sc", 2 * PAGE_B + 2 * PART_B - N)
+        wd_sc = placed([P, N], U8, "wd_sc", 5 * PAGE_B + PAGE_B // 2)
         nc.vector.tensor_copy(
             wd_sc[:].rearrange("p (t m) -> p t m", t=PACK), wd_sc_raw[:].rearrange("p (m t) -> p t m", t=PACK)
         )

@@ -30,9 +30,8 @@ CHUNKS = J // CHUNK_J
 HALF = J // 2
 PAGE_B = 4 * T
 LOWERED = 112
-OUT_C = 512
-OUT_CHUNKS = T // OUT_C
-V_CHUNKS = 2
+OUT_CUTS = ((0, 512), (512, 1024), (1024, 1536), (1536, 1792), (1792, 2048))
+V_COLS = 1024
 
 
 def tile_list_msg_relu_noneP_kernel(
@@ -59,21 +58,18 @@ def tile_list_msg_relu_noneP_kernel(
         ws_sc1 = sb([P, R], U8, "ws_sc1")
         wd_sc_raw = sb([P, N], U8, "wd_sc_raw")
         src_sc1 = sb([P, J], U8, "src_sc1")
-        zeros = placed([P, 6 * T], I32, "zeros", 0)
+        zeros = placed([P, 4 * T], I32, "zeros", 0)
         nc.gpsimd.memset(tab_sc[:].bitcast(I32), 0)
         nc.vector.memset(zeros[:, 0 : R // 4], 0)
         nc.vector.tensor_copy(w_sc_raw[:].bitcast(I32), zeros[:, 0 : R // 4])
         nc.vector.tensor_copy(ws_sc1[:].bitcast(I32), zeros[:, 0 : R // 4])
         nc.vector.memset(src_sc1[:].bitcast(I32), 0)
         nc.vector.memset(wd_sc_raw[:].bitcast(I32), 0)
-        pages = [placed([P, T], F32, "page0", 0), placed([P, T], F32, "page1", 3 * PAGE_B)]
-        for page in pages:
-            nc.vector.memset(page[:].bitcast(I32), 0)
 
-        ws_raw = sb([P, PASSES, 2 * R], U8, "ws_raw")
-        wd_raw = sb([P, 2 * N], U8, "wd_raw")
-        tab = placed([P, PASSES * T], I32, "tab", PAGE_B)
-        wt_bf = sb([P, PASSES * R * PACK], BF16, "wt_bf")
+        ws_raw = sb([P, PASSES, 2 * R], U8, "ws_raw", tag="page0")
+        wd_raw = sb([P, 2 * N], U8, "wd_raw", tag="page1")
+        tab = placed([P, PASSES * T], I32, "tab", 0)
+        wt_bf = [sb([P, R * PACK], BF16, f"wt_bf{a}") for a in range(PASSES)]
 
         def load_tab(a):
             nc.sync.dma_start(tab[:, a * T : (a + 1) * T], tab_words[a].rearrange("p t i -> p (t i)").bitcast(I32))
@@ -82,7 +78,7 @@ def tile_list_msg_relu_noneP_kernel(
             rows = wt[a * K_PASS : (a + 1) * K_PASS, :].rearrange("(p i) c -> p i c", i=PACK)
             nc.sync.dma_start(part[:], rows[:, :, c0:c1])
             nc.scalar.activation(
-                wt_bf[:, a * PACK * R : (a + 1) * PACK * R].rearrange("p (t m i) -> p m i t", t=PACK, i=PACK)[
+                wt_bf[a][:].rearrange("p (t m i) -> p m i t", t=PACK, i=PACK)[
                     :, c0 // PACK : c1 // PACK, :, :
                 ],
                 part[:].rearrange("p i (m t) -> p m i t", t=PACK),
@@ -102,10 +98,10 @@ def tile_list_msg_relu_noneP_kernel(
         load_planes(nc.sync, tab_sc, 0, 4 * PASSES, tab_scales)
         load_tab(0)
         load_planes(nc.sync, w_sc_raw, 0, 4 * PASSES, ws_scales)
-        load_and_round_wt(0, 0, R, placed([P, PACK, R], F32, "wt_raw", 4 * PAGE_B))
+        load_and_round_wt(0, 0, R, placed([P, PACK, R], F32, "wt_raw", 2 * PAGE_B))
         load_tab(1)
-        load_and_round_wt(1, 0, R // 2, placed([P, PACK, R // 2], F32, "wt_a", 5 * PAGE_B))
-        load_and_round_wt(1, R // 2, R, placed([P, PACK, R // 2], F32, "wt_b", 5 * PAGE_B + PAGE_B // 2))
+        load_and_round_wt(1, 0, R // 2, placed([P, PACK, R // 2], F32, "wt_a", 3 * PAGE_B))
+        load_and_round_wt(1, R // 2, R, placed([P, PACK, R // 2], F32, "wt_b", 3 * PAGE_B + PAGE_B // 2))
 
         ws = sb([P, PASSES, 2 * R], U8, "ws")
         nc.vector.tensor_copy(
@@ -117,6 +113,10 @@ def tile_list_msg_relu_noneP_kernel(
             wd[:].bitcast(U16).rearrange("p (t m) -> p t m", t=PACK),
             wd_raw[:].bitcast(U16).rearrange("p (m t) -> p t m", t=PACK),
         )
+
+        pages = [sb([P, T], F32, "page0"), sb([P, T], F32, "page1")]
+        for page in pages:
+            nc.gpsimd.memset(page[:], 0.0)
 
         g_sc = [sb([P, J], U8, f"g_sc{side}") for side in (SRC, DST)]
         for side in (SRC, DST):
@@ -143,16 +143,23 @@ def tile_list_msg_relu_noneP_kernel(
                 .indirect(lists[side][:, half * HALF // LIST_ROWS : (half + 1) * HALF // LIST_ROWS]),
             )
 
-        g_first = sb([P, 2 * PASSES * HALF], I32, "g_first")
-        for a in range(PASSES):
-            for side in (SRC, DST):
-                k = side * PASSES + a
-                gather_words(0, side, a, g_first[:, k * HALF : (k + 1) * HALF])
+        def gather_run(name, tag, pieces):
+            tile = sb([P, len(pieces) * HALF], I32, name, tag=tag)
+            for k, (half, side, a) in enumerate(pieces):
+                gather_words(half, side, a, tile[:, k * HALF : (k + 1) * HALF])
 
         wt_q = sb([P, PASSES * R], I32, "wt_q")
         wt_sc = sb([P, PASSES * R], U8, "wt_sc")
-        nc.vector.quantize_mx(wt_q[:].bitcast(FP8X4), wt_sc[:], wt_bf[:])
-        wd_sc = placed([P, N], U8, "wd_sc", 5 * PAGE_B + PAGE_B // 2)
+
+        def quantize_wt(a):
+            cols = slice(a * R, (a + 1) * R)
+            nc.vector.quantize_mx(wt_q[:, cols].bitcast(FP8X4), wt_sc[:, cols], wt_bf[a][:])
+
+        gather_run("g_first", "g_first", [(0, SRC, 0), (1, SRC, 0), (0, DST, 0)])
+        quantize_wt(0)
+        gather_run("g_second", "wt_bf0", [(0, SRC, 1), (0, DST, 1)])
+        quantize_wt(1)
+        wd_sc = placed([P, N], U8, "wd_sc", 3 * PAGE_B + PAGE_B // 2)
         nc.vector.tensor_copy(
             wd_sc[:].rearrange("p (t m) -> p t m", t=PACK), wd_sc_raw[:].rearrange("p (m t) -> p t m", t=PACK)
         )
@@ -219,43 +226,41 @@ def tile_list_msg_relu_noneP_kernel(
             )
 
         half_banks = BANKS // 2
-        for a in range(PASSES):
+        for b in range(BANKS):
+            first_product(SRC, 0, b)
+        for side, a in ((DST, 0), (SRC, 1)):
             for b in range(half_banks):
-                first_product(SRC, a, b)
+                first_product(side, a, b)
         h_first = [sb([P, CHUNK_J * PACK], BF16, f"h_first{c}") for c in range(2)]
         for b in range(half_banks):
-            for a in range(PASSES):
-                first_product(DST, a, b)
+            first_product(DST, 1, b)
             relu(b, h_first[b // 2], b // 2 * CHUNK_J)
 
-        g_src = sb([P, PASSES * HALF], I32, "g_src", tag="wt_bf")
-        for a in range(PASSES):
-            gather_words(1, SRC, a, g_src[:, a * HALF : (a + 1) * HALF])
-        for a in range(PASSES):
-            second_product(a * CHUNK_J, (a + 1) * CHUNK_J, h_first[a])
-            g_dst = sb([P, HALF], I32, f"g_dst{a}", tag=f"h_first{a}")
-            gather_words(1, DST, a, g_dst[:])
-        for side in (SRC, DST):
-            for a in range(PASSES):
-                for b in range(half_banks, BANKS):
-                    first_product(side, a, b)
+        gather_run("g_third", "wt_bf1", [(1, SRC, 1), (1, DST, 0)])
+        second_product(0, CHUNK_J, h_first[0])
+        gather_run("g_last", "h_first0", [(1, DST, 1)])
+        second_product(CHUNK_J, HALF, h_first[1])
+        for side, a in ((SRC, 1), (DST, 0), (DST, 1)):
+            for b in range(half_banks, BANKS):
+                first_product(side, a, b)
         h_second = sb([P, HALF * PACK], BF16, "h_second")
         for b in range(half_banks, BANKS):
             relu(b, h_second, HALF)
 
-        scatter(0, 0, CHUNK_J)
-        scatter(1, 0, HALF)
-        scatter(0, CHUNK_J, HALF)
+        for j0 in range(0, HALF, CHUNK_J):
+            for t in range(2):
+                scatter(t, j0, j0 + CHUNK_J)
         second_product(HALF, J, h_second)
-        pages.append(sb([P, T], F32, "page2", tag="h_first1"))
+        pages.append(sb([P, T], F32, "page2", tag="h_first0"))
         pages.append(sb([P, T], F32, "page3", tag="h_second"))
         for t in (2, 3):
             nc.gpsimd.memset(pages[t][:], 0.0)
         scatter(2, 0, HALF)
 
-        pairs = [sb([P, 2, OUT_C, 2], BF16, f"pairs{c}") for c in range(OUT_CHUNKS)]
-        o_bf = [sb([P, OUT_C * PACK], BF16, f"o_bf{c}") for c in range(OUT_CHUNKS)]
-        o_q = [sb([P, OUT_C], I32, f"o_q{c}") for c in range(OUT_CHUNKS)]
+        pairs_v = sb([P, 2, V_COLS, 2], BF16, "pairs_v")
+        pairs_s = sb([P, 2, T - V_COLS, 2], BF16, "pairs_s")
+        o_bf = [sb([P, (c1 - c0) * PACK], BF16, f"o_bf{c0}") for c0, c1 in OUT_CUTS]
+        o_q = sb([P, T], I32, "o_q")
         o_sc = sb([P, T], U8, "o_sc")
         out_rows = out_0.rearrange("(p t) c -> p t c", t=PACK)
         out_words = out_1[0].rearrange("p c i -> p (c i)").bitcast(I32)
@@ -263,27 +268,30 @@ def tile_list_msg_relu_noneP_kernel(
 
         for t in range(PACK):
             scatter(t, HALF if t < last else 0, J)
-            nc.sync.dma_start(out_rows[:, t, :], pages[t][:])
-            for c in range(OUT_CHUNKS):
-                part = pages[t][:, c * OUT_C : (c + 1) * OUT_C]
-                if t == last - 1 and c < V_CHUNKS:
-                    nc.scalar.activation(pairs[c][:, 1, :, :], part.unsqueeze(2).to_broadcast([P, OUT_C, 2]), ACT.Copy)
-                elif t == last and c < V_CHUNKS:
-                    nc.vector.tensor_copy(pairs[c][:, 1, :, 1], part)
-                else:
-                    nc.scalar.activation(pairs[c][:, t // 2, :, t % 2], part, ACT.Copy)
-                if t == last:
-                    woven = o_bf[c][:].bitcast(F32).rearrange("p (c u) -> p c u", u=2)
-                    words = pairs[c][:].rearrange("p u c e -> p u (c e)").bitcast(F32).rearrange("p u c -> p c u")
-                    if c < V_CHUNKS:
-                        nc.vector.tensor_copy(woven, words)
-                    else:
-                        nc.scalar.copy(woven, words)
+            page = pages[t]
+            nc.sync.dma_start(out_rows[:, t, :], page[:])
+            if t < 2:
+                nc.scalar.activation(pairs_v[:, 0, :, t], page[:, 0:V_COLS], ACT.Copy)
+            if t == 2:
+                nc.scalar.activation(
+                    pairs_v[:, 1, :, :], page[:, 0:V_COLS].unsqueeze(2).to_broadcast([P, V_COLS, 2]), ACT.Copy
+                )
+            if t < last:
+                nc.scalar.activation(pairs_s[:, t // 2, :, t % 2], page[:, V_COLS:T], ACT.Copy)
 
-        for c in range(OUT_CHUNKS):
-            cols = slice(c * OUT_C, (c + 1) * OUT_C)
-            nc.vector.quantize_mx(o_q[c][:].bitcast(FP8X4), o_sc[:, cols], o_bf[c][:])
-            nc.sync.dma_start(out_words[:, cols], o_q[c][:])
+        for k, (c0, c1) in enumerate(OUT_CUTS):
+            pairs, first = (pairs_v, 0) if c0 < V_COLS else (pairs_s, V_COLS)
+            words = pairs[:].rearrange("p u c e -> p u (c e)").bitcast(F32)[:, :, c0 - first : c1 - first]
+            woven = o_bf[k][:].bitcast(F32).rearrange("p (c u) -> p c u", u=2)
+            if c0 < V_COLS:
+                nc.vector.tensor_copy(pairs[:, 1, c0:c1, 1], pages[last][:, c0:c1])
+                nc.vector.tensor_copy(woven, words.rearrange("p u c -> p c u"))
+            else:
+                nc.scalar.activation(pairs[:, 1, c0 - first : c1 - first, 1], pages[last][:, c0:c1], ACT.Copy)
+                nc.scalar.copy(woven, words.rearrange("p u c -> p c u"))
+        for k, (c0, c1) in enumerate(OUT_CUTS):
+            nc.vector.quantize_mx(o_q[:, c0:c1].bitcast(FP8X4), o_sc[:, c0:c1], o_bf[k][:])
+            nc.sync.dma_start(out_words[:, c0:c1], o_q[:, c0:c1])
         for q in range(QUADS):
             eng = nc.scalar if q % 2 else nc.sync
             eng.dma_start(out_2[0, 4 * q : 4 * q + 4, :].bitcast(I32), o_sc[32 * q : 32 * q + 4, :].bitcast(I32))

@@ -54,7 +54,7 @@ def tile_list_msg_relu_noneP_kernel(
         lists = (src_list, dst_list)
 
         tab_sc = sb([P, T], U8, "tab_sc")
-        w_sc_raw = sb([P, R], U8, "w_sc_raw", tag="g_first")
+        w_sc_raw = sb([P, R], U8, "w_sc_raw")
         ws_sc1 = sb([P, R], U8, "ws_sc1")
         wd_sc_raw = sb([P, N], U8, "wd_sc_raw")
         src_sc1 = sb([P, J], U8, "src_sc1")
@@ -69,7 +69,7 @@ def tile_list_msg_relu_noneP_kernel(
         ws_raw = sb([P, PASSES, 2 * R], U8, "ws_raw", tag="page0")
         wd_raw = sb([P, 2 * N], U8, "wd_raw", tag="page1")
         tab = placed([P, PASSES * T], I32, "tab", 0)
-        wt_bf = [sb([P, R * PACK], BF16, f"wt_bf{a}") for a in range(PASSES)]
+        wt_bf = [sb([P, R * PACK], BF16, "wt_bf0"), placed([P, R * PACK], BF16, "wt_bf1", 4 * PAGE_B + N)]
 
         def load_tab(a):
             nc.sync.dma_start(tab[:, a * T : (a + 1) * T], tab_words[a].rearrange("p t i -> p (t i)").bitcast(I32))
@@ -99,8 +99,8 @@ def tile_list_msg_relu_noneP_kernel(
         load_tab(0)
         load_planes(nc.sync, w_sc_raw, 0, 4 * PASSES, ws_scales)
         load_and_round_wt(0, 0, R, placed([P, PACK, R], F32, "wt_raw", 2 * PAGE_B))
-        load_tab(1)
         load_and_round_wt(1, 0, R // 2, placed([P, PACK, R // 2], F32, "wt_a", 3 * PAGE_B))
+        load_tab(1)
         load_and_round_wt(1, R // 2, R, placed([P, PACK, R // 2], F32, "wt_b", 3 * PAGE_B + PAGE_B // 2))
 
         ws = sb([P, PASSES, 2 * R], U8, "ws")
@@ -123,7 +123,7 @@ def tile_list_msg_relu_noneP_kernel(
             nc.vector.tensor_copy(g_sc[side][:], tab_sc[:].indirect(lists[side][:]))
         nc.sync.dma_start(src_sc1[0:LOWERED, :].bitcast(I32), g_sc[SRC][4 : LOWERED + 4, :].bitcast(I32))
         w_sc = sb([P, R], U8, "w_sc")
-        nc.vector.tensor_copy(
+        nc.gpsimd.tensor_copy(
             w_sc[:].rearrange("p (t m) -> p t m", t=PACK), w_sc_raw[:].rearrange("p (m t) -> p t m", t=PACK)
         )
         nc.sync.dma_start(ws_sc1[0:LOWERED, :].bitcast(I32), w_sc[4 : LOWERED + 4, :].bitcast(I32))
@@ -143,8 +143,7 @@ def tile_list_msg_relu_noneP_kernel(
                 .indirect(lists[side][:, half * HALF // LIST_ROWS : (half + 1) * HALF // LIST_ROWS]),
             )
 
-        def gather_run(name, tag, pieces):
-            tile = sb([P, len(pieces) * HALF], I32, name, tag=tag)
+        def gather_run(tile, pieces):
             for k, (half, side, a) in enumerate(pieces):
                 gather_words(half, side, a, tile[:, k * HALF : (k + 1) * HALF])
 
@@ -155,12 +154,12 @@ def tile_list_msg_relu_noneP_kernel(
             cols = slice(a * R, (a + 1) * R)
             nc.vector.quantize_mx(wt_q[:, cols].bitcast(FP8X4), wt_sc[:, cols], wt_bf[a][:])
 
-        gather_run("g_first", "g_first", [(0, SRC, 0), (1, SRC, 0), (0, DST, 0)])
+        gather_run(sb([P, 3 * HALF], I32, "g_first"), [(0, SRC, 0), (1, SRC, 0), (0, DST, 0)])
         quantize_wt(0)
-        gather_run("g_second", "wt_bf0", [(0, SRC, 1), (0, DST, 1)])
+        gather_run(sb([P, 2 * HALF], I32, "g_second"), [(0, SRC, 1), (0, DST, 1)])
         quantize_wt(1)
-        wd_sc = placed([P, N], U8, "wd_sc", 3 * PAGE_B + PAGE_B // 2)
-        nc.vector.tensor_copy(
+        wd_sc = placed([P, N], U8, "wd_sc", 4 * PAGE_B + PAGE_B // 2)
+        nc.gpsimd.tensor_copy(
             wd_sc[:].rearrange("p (t m) -> p t m", t=PACK), wd_sc_raw[:].rearrange("p (m t) -> p t m", t=PACK)
         )
 
@@ -236,9 +235,9 @@ def tile_list_msg_relu_noneP_kernel(
             first_product(DST, 1, b)
             relu(b, h_first[b // 2], b // 2 * CHUNK_J)
 
-        gather_run("g_third", "wt_bf1", [(1, SRC, 1), (1, DST, 0)])
+        gather_run(placed([P, 2 * HALF], I32, "g_third", 4 * PAGE_B), [(1, SRC, 1), (1, DST, 0)])
         second_product(0, CHUNK_J, h_first[0])
-        gather_run("g_last", "h_first0", [(1, DST, 1)])
+        gather_run(sb([P, HALF], I32, "g_last", tag="h_first0"), [(1, DST, 1)])
         second_product(CHUNK_J, HALF, h_first[1])
         for side, a in ((SRC, 1), (DST, 0), (DST, 1)):
             for b in range(half_banks, BANKS):

@@ -54,22 +54,24 @@ def tile_list_msg_relu_noneP_kernel(
         lists = (src_list, dst_list)
 
         tab_sc = sb([P, T], U8, "tab_sc")
-        w_sc_raw = sb([P, R], U8, "w_sc_raw")
+        w_sc_raw = sb([P, R], U8, "w_sc_raw", tag="page1")
         ws_sc1 = sb([P, R], U8, "ws_sc1")
         wd_sc_raw = sb([P, N], U8, "wd_sc_raw")
         src_sc1 = sb([P, J], U8, "src_sc1")
-        zeros = placed([P, 4 * T], I32, "zeros", 0)
-        nc.gpsimd.memset(tab_sc[:].bitcast(I32), 0)
+        zeros = placed([P, 7 * T], I32, "zeros", 0)
+        nc.vector.memset(tab_sc[:].bitcast(I32), 0)
         nc.vector.memset(zeros[:, 0 : R // 4], 0)
         nc.vector.tensor_copy(w_sc_raw[:].bitcast(I32), zeros[:, 0 : R // 4])
         nc.vector.tensor_copy(ws_sc1[:].bitcast(I32), zeros[:, 0 : R // 4])
         nc.vector.memset(src_sc1[:].bitcast(I32), 0)
         nc.vector.memset(wd_sc_raw[:].bitcast(I32), 0)
+        pages = [placed([P, T], F32, "page0", 4 * PAGE_B), ]
+        nc.vector.memset(pages[0][:], 0.0)
 
-        ws_raw = sb([P, PASSES, 2 * R], U8, "ws_raw", tag="page0")
-        wd_raw = sb([P, 2 * N], U8, "wd_raw", tag="page1")
+        ws_raw = placed([P, PASSES, 2 * R], U8, "ws_raw", 6 * PAGE_B)
+        wd_raw = placed([P, 2 * N], U8, "wd_raw", 6 * PAGE_B + PAGE_B // 2)
         tab = placed([P, PASSES * T], I32, "tab", 0)
-        wt_bf = [sb([P, R * PACK], BF16, "wt_bf0"), placed([P, R * PACK], BF16, "wt_bf1", 4 * PAGE_B + N)]
+        wt_bf = [sb([P, R * PACK], BF16, "wt_bf0"), sb([P, R * PACK], BF16, "wt_bf1")]
 
         def load_tab(a):
             nc.sync.dma_start(tab[:, a * T : (a + 1) * T], tab_words[a].rearrange("p t i -> p (t i)").bitcast(I32))
@@ -92,31 +94,28 @@ def tile_list_msg_relu_noneP_kernel(
                 )
 
         nc.sync.dma_start(src_list[:], offs)
-        nc.sync.dma_start(ws_raw[:].bitcast(I32), ws_words.rearrange("a p c -> p a c").bitcast(I32))
-        nc.sync.dma_start(wd_raw[:].bitcast(I32), wd_words[0].bitcast(I32))
         nc.sync.dma_start(dst_list[:], offs2)
         load_planes(nc.sync, tab_sc, 0, 4 * PASSES, tab_scales)
+        nc.sync.dma_start(ws_raw[:].bitcast(I32), ws_words.rearrange("a p c -> p a c").bitcast(I32))
         load_tab(0)
         load_planes(nc.sync, w_sc_raw, 0, 4 * PASSES, ws_scales)
         load_and_round_wt(0, 0, R, placed([P, PACK, R], F32, "wt_raw", 2 * PAGE_B))
         load_and_round_wt(1, 0, R // 2, placed([P, PACK, R // 2], F32, "wt_a", 3 * PAGE_B))
         load_tab(1)
+        nc.sync.dma_start(wd_raw[:].bitcast(I32), wd_words[0].bitcast(I32))
         load_and_round_wt(1, R // 2, R, placed([P, PACK, R // 2], F32, "wt_b", 3 * PAGE_B + PAGE_B // 2))
 
         ws = sb([P, PASSES, 2 * R], U8, "ws")
-        nc.vector.tensor_copy(
+        nc.gpsimd.tensor_copy(
             ws[:].bitcast(U16).rearrange("p a (t m) -> p a t m", t=PACK),
             ws_raw[:].bitcast(U16).rearrange("p a (m t) -> p a t m", t=PACK),
         )
         wd = sb([P, 2 * N], U8, "wd")
-        nc.vector.tensor_copy(
+        nc.gpsimd.tensor_copy(
             wd[:].bitcast(U16).rearrange("p (t m) -> p t m", t=PACK),
             wd_raw[:].bitcast(U16).rearrange("p (m t) -> p t m", t=PACK),
         )
 
-        pages = [sb([P, T], F32, "page0"), sb([P, T], F32, "page1")]
-        for page in pages:
-            nc.gpsimd.memset(page[:], 0.0)
 
         g_sc = [sb([P, J], U8, f"g_sc{side}") for side in (SRC, DST)]
         for side in (SRC, DST):
@@ -129,6 +128,8 @@ def tile_list_msg_relu_noneP_kernel(
         nc.sync.dma_start(ws_sc1[0:LOWERED, :].bitcast(I32), w_sc[4 : LOWERED + 4, :].bitcast(I32))
         ws_sc = [w_sc, ws_sc1]
         load_planes(nc.sync, wd_sc_raw, 0, 4, wd_scales)
+        pages.append(sb([P, T], F32, "page1"))
+        nc.gpsimd.memset(pages[1][:], 0.0)
         edge_w = sb([P, J], F32, "edge_w", tag="tab_sc")
         nc.sync.dma_start(edge_w[:], wgo)
 
@@ -158,7 +159,7 @@ def tile_list_msg_relu_noneP_kernel(
         quantize_wt(0)
         gather_run(sb([P, 2 * HALF], I32, "g_second"), [(0, SRC, 1), (0, DST, 1)])
         quantize_wt(1)
-        wd_sc = placed([P, N], U8, "wd_sc", 4 * PAGE_B + PAGE_B // 2)
+        wd_sc = sb([P, N], U8, "wd_sc", tag="wt_bf1")
         nc.gpsimd.tensor_copy(
             wd_sc[:].rearrange("p (t m) -> p t m", t=PACK), wd_sc_raw[:].rearrange("p (m t) -> p t m", t=PACK)
         )
@@ -235,7 +236,7 @@ def tile_list_msg_relu_noneP_kernel(
             first_product(DST, 1, b)
             relu(b, h_first[b // 2], b // 2 * CHUNK_J)
 
-        gather_run(placed([P, 2 * HALF], I32, "g_third", 4 * PAGE_B), [(1, SRC, 1), (1, DST, 0)])
+        gather_run(placed([P, 2 * HALF], I32, "g_third", 3 * PAGE_B + PAGE_B // 2), [(1, SRC, 1), (1, DST, 0)])
         second_product(0, CHUNK_J, h_first[0])
         gather_run(sb([P, HALF], I32, "g_last", tag="h_first0"), [(1, DST, 1)])
         second_product(CHUNK_J, HALF, h_first[1])
@@ -292,5 +293,4 @@ def tile_list_msg_relu_noneP_kernel(
             nc.vector.quantize_mx(o_q[:, c0:c1].bitcast(FP8X4), o_sc[:, c0:c1], o_bf[k][:])
             nc.sync.dma_start(out_words[:, c0:c1], o_q[:, c0:c1])
         for q in range(QUADS):
-            eng = nc.scalar if q % 2 else nc.sync
-            eng.dma_start(out_2[0, 4 * q : 4 * q + 4, :].bitcast(I32), o_sc[32 * q : 32 * q + 4, :].bitcast(I32))
+            nc.scalar.dma_start(out_2[0, 4 * q : 4 * q + 4, :].bitcast(I32), o_sc[32 * q : 32 * q + 4, :].bitcast(I32))

@@ -28,8 +28,8 @@ BANKS = J // BANK_J
 CHUNK_J = 256
 CHUNKS = J // CHUNK_J
 HALF = J // 2
-PAGE_B = 4 * T
-LOWERED = 112
+KB = 1024
+ROW_B = 2 * J + R
 OUT_CUTS = ((0, 512), (512, 1024), (1024, 1536), (1536, 1792), (1792, 2048))
 V_COLS = 1024
 
@@ -54,84 +54,75 @@ def tile_list_msg_relu_noneP_kernel(
         lists = (src_list, dst_list)
 
         tab_sc = sb([P, T], U8, "tab_sc")
-        w_sc_raw = sb([P, R], U8, "w_sc_raw", tag="page1")
-        ws_sc1 = sb([P, R], U8, "ws_sc1")
-        wd_sc_raw = sb([P, N], U8, "wd_sc_raw")
-        src_sc1 = sb([P, J], U8, "src_sc1")
-        zeros = placed([P, 7 * T], I32, "zeros", 0)
-        nc.vector.memset(tab_sc[:].bitcast(I32), 0)
-        nc.vector.memset(zeros[:, 0 : R // 4], 0)
-        nc.vector.tensor_copy(w_sc_raw[:].bitcast(I32), zeros[:, 0 : R // 4])
-        nc.vector.tensor_copy(ws_sc1[:].bitcast(I32), zeros[:, 0 : R // 4])
-        nc.vector.memset(src_sc1[:].bitcast(I32), 0)
-        nc.vector.memset(wd_sc_raw[:].bitcast(I32), 0)
-        pages = [placed([P, T], F32, "page0", 4 * PAGE_B), ]
-        nc.vector.memset(pages[0][:], 0.0)
+        nc.vector.memset(tab_sc[32:64, :].bitcast(I32), 0)
+        nc.vector.memset(tab_sc[64:P, :].bitcast(I32), 0)
+        ws_sc_raw = sb([P, R], U8, "ws_sc_raw")
+        nc.gpsimd.memset(ws_sc_raw[32:64, :].bitcast(I32), 0)
+        nc.gpsimd.memset(ws_sc_raw[64:P, :].bitcast(I32), 0)
+        planes = [sb([P, ROW_B], U8, "planes0")]
+        nc.gpsimd.memset(planes[0][:].bitcast(I32), 0)
 
-        ws_raw = placed([P, PASSES, 2 * R], U8, "ws_raw", 6 * PAGE_B)
-        wd_raw = placed([P, 2 * N], U8, "wd_raw", 6 * PAGE_B + PAGE_B // 2)
-        tab = placed([P, PASSES * T], I32, "tab", 0)
-        wt_bf = [sb([P, R * PACK], BF16, "wt_bf0"), sb([P, R * PACK], BF16, "wt_bf1")]
+        tab = [sb([P, T], I32, f"tab{a}") for a in range(PASSES)]
+        ws_raw = placed([P, PASSES, 2 * R], U8, "ws_raw", 10 * KB + 512)
+        wt_bf = [placed([P, R * PACK], BF16, "wt_bf0", 62 * KB), placed([P, R * PACK], BF16, "wt_bf1", 24 * KB)]
 
         def load_tab(a):
-            nc.sync.dma_start(tab[:, a * T : (a + 1) * T], tab_words[a].rearrange("p t i -> p (t i)").bitcast(I32))
+            nc.sync.dma_start(tab[a][:], tab_words[a].rearrange("p t i -> p (t i)").bitcast(I32))
 
         def load_and_round_wt(a, c0, c1, part):
             rows = wt[a * K_PASS : (a + 1) * K_PASS, :].rearrange("(p i) c -> p i c", i=PACK)
-            nc.sync.dma_start(part[:], rows[:, :, c0:c1])
+            nc.sync.dma_start(part, rows[:, :, c0:c1])
             nc.scalar.activation(
                 wt_bf[a][:].rearrange("p (t m i) -> p m i t", t=PACK, i=PACK)[
                     :, c0 // PACK : c1 // PACK, :, :
                 ],
-                part[:].rearrange("p i (m t) -> p m i t", t=PACK),
+                part.rearrange("p i (m t) -> p m i t", t=PACK),
                 ACT.Copy,
             )
 
-        def load_planes(eng, tile, row0, rows, scales):
-            for q in range(QUADS):
-                eng.dma_start(
-                    tile[32 * q + row0 : 32 * q + row0 + rows, :].bitcast(I32), scales[:, 4 * q : 4 * q + 4, :].bitcast(I32)
-                )
-
         nc.sync.dma_start(src_list[:], offs)
         nc.sync.dma_start(dst_list[:], offs2)
-        load_planes(nc.sync, tab_sc, 0, 4 * PASSES, tab_scales)
-        nc.sync.dma_start(ws_raw[:].bitcast(I32), ws_words.rearrange("a p c -> p a c").bitcast(I32))
+        nc.sync.dma_start(tab_sc[0:32, :].bitcast(I32), tab_scales.rearrange("a q t -> (a q) t").bitcast(I32))
+        nc.sync.dma_start(ws_sc_raw[0:32, :].bitcast(I32), ws_scales.rearrange("a q c -> (a q) c").bitcast(I32))
+        load_and_round_wt(0, 0, P, sb([P, PACK, P], F32, "wt_head")[:])
         load_tab(0)
-        load_planes(nc.sync, w_sc_raw, 0, 4 * PASSES, ws_scales)
-        load_and_round_wt(0, 0, R, placed([P, PACK, R], F32, "wt_raw", 2 * PAGE_B))
-        load_and_round_wt(1, 0, R // 2, placed([P, PACK, R // 2], F32, "wt_a", 3 * PAGE_B))
+        nc.sync.dma_start(ws_raw[:].bitcast(I32), ws_words.rearrange("a p c -> p a c").bitcast(I32))
+        load_and_round_wt(0, P, R, sb([P, PACK, R - P], F32, "wt_rest")[:])
         load_tab(1)
-        nc.sync.dma_start(wd_raw[:].bitcast(I32), wd_words[0].bitcast(I32))
-        load_and_round_wt(1, R // 2, R, placed([P, PACK, R // 2], F32, "wt_b", 3 * PAGE_B + PAGE_B // 2))
+        load_and_round_wt(1, 0, R // 2, sb([P, PACK, R // 2], F32, "wt_a")[:])
 
+        rows_sc = sb([P, ROW_B], U8, "rows_sc")
+        nc.gpsimd.tensor_copy(
+            rows_sc[:, 2 * J :].rearrange("p (t m) -> p t m", t=PACK), ws_sc_raw[:].rearrange("p (m t) -> p t m", t=PACK)
+        )
+        wd_sc_raw = placed([P, N], U8, "wd_sc_raw", 11 * KB)
         ws = sb([P, PASSES, 2 * R], U8, "ws")
         nc.gpsimd.tensor_copy(
             ws[:].bitcast(U16).rearrange("p a (t m) -> p a t m", t=PACK),
             ws_raw[:].bitcast(U16).rearrange("p a (m t) -> p a t m", t=PACK),
         )
-        wd = sb([P, 2 * N], U8, "wd")
-        nc.gpsimd.tensor_copy(
-            wd[:].bitcast(U16).rearrange("p (t m) -> p t m", t=PACK),
-            wd_raw[:].bitcast(U16).rearrange("p (m t) -> p t m", t=PACK),
-        )
-
-
-        g_sc = [sb([P, J], U8, f"g_sc{side}") for side in (SRC, DST)]
+        g_sc = [placed([P, J], U8, f"g_sc{side}", side * KB) for side in (SRC, DST)]
         for side in (SRC, DST):
             nc.vector.tensor_copy(g_sc[side][:], tab_sc[:].indirect(lists[side][:]))
-        nc.sync.dma_start(src_sc1[0:LOWERED, :].bitcast(I32), g_sc[SRC][4 : LOWERED + 4, :].bitcast(I32))
-        w_sc = sb([P, R], U8, "w_sc")
-        nc.gpsimd.tensor_copy(
-            w_sc[:].rearrange("p (t m) -> p t m", t=PACK), w_sc_raw[:].rearrange("p (m t) -> p t m", t=PACK)
-        )
-        nc.sync.dma_start(ws_sc1[0:LOWERED, :].bitcast(I32), w_sc[4 : LOWERED + 4, :].bitcast(I32))
-        ws_sc = [w_sc, ws_sc1]
-        load_planes(nc.sync, wd_sc_raw, 0, 4, wd_scales)
-        pages.append(sb([P, T], F32, "page1"))
-        nc.gpsimd.memset(pages[1][:], 0.0)
-        edge_w = sb([P, J], F32, "edge_w", tag="tab_sc")
-        nc.sync.dma_start(edge_w[:], wgo)
+        for side in (SRC, DST):
+            nc.vector.tensor_copy(rows_sc[:, side * J : (side + 1) * J].bitcast(I32), g_sc[side][:].bitcast(I32))
+
+        def move_planes(a, eng):
+            for q in range(QUADS):
+                row = 16 * a + 4 * q
+                eng.dma_start(planes[a][32 * q : 32 * q + 4, :].bitcast(I32), rows_sc[row : row + 4, :].bitcast(I32))
+
+        move_planes(0, nc.scalar)
+        load_and_round_wt(1, R // 2, R, placed([P, PACK, R // 2], F32, "wt_b", 7 * KB)[:])
+        planes.append(sb([P, ROW_B], U8, "planes1", tag="wt_rest"))
+        nc.gpsimd.memset(planes[1][:].bitcast(I32), 0)
+        move_planes(1, nc.sync)
+        nc.gpsimd.memset(wd_sc_raw[:].bitcast(I32), 0)
+
+        for q in range(QUADS):
+            nc.sync.dma_start(wd_sc_raw[32 * q : 32 * q + 4, :].bitcast(I32), wd_scales[0, 4 * q : 4 * q + 4, :].bitcast(I32))
+        wd_raw = placed([P, 2 * N], U8, "wd_raw", 11 * KB + 512)
+        nc.sync.dma_start(wd_raw[:].bitcast(I32), wd_words[0].bitcast(I32))
 
         g_words = {}
 
@@ -139,9 +130,7 @@ def tile_list_msg_relu_noneP_kernel(
             g_words[(half, side, a)] = dst
             nc.vector.tensor_copy(
                 dst.bitcast(U32),
-                tab[:, a * T : (a + 1) * T]
-                .bitcast(U32)
-                .indirect(lists[side][:, half * HALF // LIST_ROWS : (half + 1) * HALF // LIST_ROWS]),
+                tab[a][:].bitcast(U32).indirect(lists[side][:, half * HALF // LIST_ROWS : (half + 1) * HALF // LIST_ROWS]),
             )
 
         def gather_run(tile, pieces):
@@ -155,11 +144,20 @@ def tile_list_msg_relu_noneP_kernel(
             cols = slice(a * R, (a + 1) * R)
             nc.vector.quantize_mx(wt_q[:, cols].bitcast(FP8X4), wt_sc[:, cols], wt_bf[a][:])
 
-        gather_run(sb([P, 3 * HALF], I32, "g_first"), [(0, SRC, 0), (1, SRC, 0), (0, DST, 0)])
+        gather_run(placed([P, 3 * HALF], I32, "g_first", 0), [(0, SRC, 0), (0, DST, 0), (1, SRC, 0)])
         quantize_wt(0)
+        pages = [placed([P, T], F32, "page0", 62 * KB)]
+        nc.gpsimd.memset(pages[0][:], 0.0)
         gather_run(sb([P, 2 * HALF], I32, "g_second"), [(0, SRC, 1), (0, DST, 1)])
         quantize_wt(1)
-        wd_sc = sb([P, N], U8, "wd_sc", tag="wt_bf1")
+        edge_w = placed([P, J], F32, "edge_w", 26 * KB + 512)
+        nc.sync.dma_start(edge_w[:], wgo)
+        wd = placed([P, 2 * N], U8, "wd", 24 * KB)
+        nc.gpsimd.tensor_copy(
+            wd[:].bitcast(U16).rearrange("p (t m) -> p t m", t=PACK),
+            wd_raw[:].bitcast(U16).rearrange("p (m t) -> p t m", t=PACK),
+        )
+        wd_sc = placed([P, N], U8, "wd_sc", 26 * KB)
         nc.gpsimd.tensor_copy(
             wd_sc[:].rearrange("p (t m) -> p t m", t=PACK), wd_sc_raw[:].rearrange("p (m t) -> p t m", t=PACK)
         )
@@ -167,30 +165,29 @@ def tile_list_msg_relu_noneP_kernel(
         acc = [psum.tile([P, PACK, BANK_J], F32, name=f"acc{b}", tag=f"bank{b}") for b in range(BANKS)]
 
         def first_product(side, a, b):
-            cols = slice(b * BANK_J, (b + 1) * BANK_J)
+            cols = slice(side * J + b * BANK_J, side * J + (b + 1) * BANK_J)
             half, j0 = divmod(b * BANK_J, HALF)
             for t in range(PACK):
                 if side == SRC:
                     lhsT = ws[:, a, 2 * P * t : 2 * P * (t + 1)].bitcast(FP4X4)
-                    lhsT_scale = ws_sc[a][:, P * t : P * (t + 1)]
-                    rhs_scale = g_sc[SRC][:, cols] if a == 0 else src_sc1[:, cols]
+                    lhsT_scale = planes[a][:, 2 * J + P * t : 2 * J + P * (t + 1)]
                 else:
                     lhsT = wt_q[:, a * R + P * t : a * R + P * (t + 1)].bitcast(FP8X4)
                     lhsT_scale = wt_sc[:, a * R + P * t : a * R + P * (t + 1)]
-                    rhs_scale = g_sc[DST][4 * a : P, cols]
                 nc.tensor.matmul_mx(
                     acc[b][:, t, :],
                     lhsT=lhsT,
                     lhsT_scale=lhsT_scale,
                     rhs=g_words[(half, side, a)][:, j0 : j0 + BANK_J].bitcast(FP8X4),
-                    rhs_scale=rhs_scale,
-                    start=(side == SRC and a == 0 and t == 0),
+                    rhs_scale=planes[a][:, cols],
+                    start=((side, a) == (SRC, half) and t == 0),
                     stop=(side == DST and a == PASSES - 1 and t == PACK - 1),
                 )
 
         h_q = sb([P, J], I32, "h_q")
         h_sc = sb([P, J], U8, "h_sc")
         y = sb([P, PACK, J], F32, "y")
+        late = []
 
         def relu(b, h_bf, j0):
             nc.scalar.activation(
@@ -215,47 +212,54 @@ def tile_list_msg_relu_noneP_kernel(
                         start=True,
                         stop=True,
                     )
-                nc.scalar.activation(y[:, per_bank * u : per_bank * (u + 1), j0:j1], res[:], ACT.Copy)
+                if j0 < HALF and u == 1:
+                    late.append(res)
+                else:
+                    nc.scalar.activation(y[:, per_bank * u : per_bank * (u + 1), j0:j1], res[:], ACT.Copy)
 
-        def scatter(t, j0, j1):
+        def scatter(t, j0, j1, src=None):
             nc.vector.tensor_tensor(
                 pages[t][:].indirect(dst_list[:, j0 // LIST_ROWS : j1 // LIST_ROWS]),
-                y[:, t, j0:j1],
+                y[:, t, j0:j1] if src is None else src,
                 edge_w[:, j0:j1],
                 MULT,
             )
 
         half_banks = BANKS // 2
-        for b in range(BANKS):
-            first_product(SRC, 0, b)
-        for side, a in ((DST, 0), (SRC, 1)):
+        for side in (SRC, DST):
             for b in range(half_banks):
-                first_product(side, a, b)
-        h_first = [sb([P, CHUNK_J * PACK], BF16, f"h_first{c}") for c in range(2)]
+                first_product(side, 0, b)
+        h_first = [sb([P, CHUNK_J * PACK], BF16, "h_first0"), placed([P, CHUNK_J * PACK], BF16, "h_first1", 43 * KB)]
         for b in range(half_banks):
+            first_product(SRC, 1, b)
             first_product(DST, 1, b)
             relu(b, h_first[b // 2], b // 2 * CHUNK_J)
 
-        gather_run(placed([P, 2 * HALF], I32, "g_third", 3 * PAGE_B + PAGE_B // 2), [(1, SRC, 1), (1, DST, 0)])
+        gather_run(placed([P, 2 * HALF], I32, "g_third", 7 * KB), [(1, SRC, 1), (1, DST, 0)])
         second_product(0, CHUNK_J, h_first[0])
         gather_run(sb([P, HALF], I32, "g_last", tag="h_first0"), [(1, DST, 1)])
         second_product(CHUNK_J, HALF, h_first[1])
-        for side, a in ((SRC, 1), (DST, 0), (DST, 1)):
+        for t in (1, 2):
+            pages.append(placed([P, T], F32, f"page{t}", (36 + 8 * (t - 1)) * KB))
+            nc.gpsimd.memset(pages[t][:], 0.0)
+        for side, a in ((SRC, 1), (SRC, 0), (DST, 0), (DST, 1)):
             for b in range(half_banks, BANKS):
                 first_product(side, a, b)
         h_second = sb([P, HALF * PACK], BF16, "h_second")
         for b in range(half_banks, BANKS):
             relu(b, h_second, HALF)
 
-        for j0 in range(0, HALF, CHUNK_J):
-            for t in range(2):
+        for t in range(2):
+            for j0 in range(0, HALF, CHUNK_J):
                 scatter(t, j0, j0 + CHUNK_J)
+        y_late = sb([P, 2, HALF], F32, "y_late", tag="h_first0")
+        for c, res in enumerate(late):
+            nc.scalar.activation(y_late[:, :, c * CHUNK_J : (c + 1) * CHUNK_J], res[:], ACT.Copy)
         second_product(HALF, J, h_second)
-        pages.append(sb([P, T], F32, "page2", tag="h_first0"))
         pages.append(sb([P, T], F32, "page3", tag="h_second"))
-        for t in (2, 3):
-            nc.gpsimd.memset(pages[t][:], 0.0)
-        scatter(2, 0, HALF)
+        nc.gpsimd.memset(pages[3][:], 0.0)
+        for j0 in range(0, HALF, CHUNK_J):
+            scatter(2, j0, j0 + CHUNK_J, y_late[:, 0, j0 : j0 + CHUNK_J])
 
         pairs_v = sb([P, 2, V_COLS, 2], BF16, "pairs_v")
         pairs_s = sb([P, 2, T - V_COLS, 2], BF16, "pairs_s")
@@ -267,7 +271,9 @@ def tile_list_msg_relu_noneP_kernel(
         last = PACK - 1
 
         for t in range(PACK):
-            scatter(t, HALF if t < last else 0, J)
+            if t == last:
+                scatter(t, 0, HALF, y_late[:, 1, :])
+            scatter(t, HALF, J)
             page = pages[t]
             nc.sync.dma_start(out_rows[:, t, :], page[:])
             if t < 2:

@@ -61,81 +61,91 @@ def tile_list_msg_relu_noneP_kernel(
         nc.gpsimd.memset(ws_sc_raw[64:P, :].bitcast(I32), 0)
         planes = [sb([P, ROW_B], U8, "planes0")]
         nc.gpsimd.memset(planes[0][:].bitcast(I32), 0)
+        pages = [sb([P, T], F32, "page0")]
+        nc.gpsimd.memset(pages[0][:], 0.0)
 
-        tab = [sb([P, T], I32, f"tab{a}") for a in range(PASSES)]
-        ws_raw = placed([P, PASSES, 2 * R], U8, "ws_raw", 10 * KB + 512)
-        wt_bf = [placed([P, R * PACK], BF16, "wt_bf0", 62 * KB), placed([P, R * PACK], BF16, "wt_bf1", 24 * KB)]
+        ws_raw = placed([P, PASSES, 2 * R], U8, "ws_raw", 23 * KB)
+        wt_bf = [sb([P, R * PACK], BF16, "wt_bf0"), sb([P, R * PACK], BF16, "wt_bf1")]
+        tab = []
 
-        def load_tab(a):
-            nc.sync.dma_start(tab[a][:], tab_words[a].rearrange("p t i -> p (t i)").bitcast(I32))
+        def load_tab(tile):
+            nc.sync.dma_start(tile[:], tab_words[len(tab)].rearrange("p t i -> p (t i)").bitcast(I32))
+            tab.append(tile)
 
         def load_and_round_wt(a, c0, c1, part):
             rows = wt[a * K_PASS : (a + 1) * K_PASS, :].rearrange("(p i) c -> p i c", i=PACK)
-            nc.sync.dma_start(part, rows[:, :, c0:c1])
+            nc.sync.dma_start(part[:], rows[:, :, c0:c1])
             nc.scalar.activation(
                 wt_bf[a][:].rearrange("p (t m i) -> p m i t", t=PACK, i=PACK)[
                     :, c0 // PACK : c1 // PACK, :, :
                 ],
-                part.rearrange("p i (m t) -> p m i t", t=PACK),
+                part[:].rearrange("p i (m t) -> p m i t", t=PACK),
                 ACT.Copy,
             )
 
         nc.sync.dma_start(src_list[:], offs)
-        nc.sync.dma_start(dst_list[:], offs2)
         nc.sync.dma_start(tab_sc[0:32, :].bitcast(I32), tab_scales.rearrange("a q t -> (a q) t").bitcast(I32))
+        nc.sync.dma_start(dst_list[:], offs2)
         nc.sync.dma_start(ws_sc_raw[0:32, :].bitcast(I32), ws_scales.rearrange("a q c -> (a q) c").bitcast(I32))
-        load_and_round_wt(0, 0, P, sb([P, PACK, P], F32, "wt_head")[:])
-        load_tab(0)
+        load_tab(sb([P, T], I32, "tab0"))
         nc.sync.dma_start(ws_raw[:].bitcast(I32), ws_words.rearrange("a p c -> p a c").bitcast(I32))
-        load_and_round_wt(0, P, R, sb([P, PACK, R - P], F32, "wt_rest")[:])
-        load_tab(1)
-        load_and_round_wt(1, 0, R // 2, sb([P, PACK, R // 2], F32, "wt_a")[:])
+        load_and_round_wt(0, 0, R, placed([P, PACK, R], F32, "wt_raw", 40 * KB))
+        load_and_round_wt(1, 0, R // 2, sb([P, PACK, R // 2], F32, "wt_a"))
+        load_and_round_wt(1, R // 2, R, sb([P, PACK, R // 2], F32, "wt_b"))
 
         rows_sc = sb([P, ROW_B], U8, "rows_sc")
         nc.gpsimd.tensor_copy(
-            rows_sc[:, 2 * J :].rearrange("p (t m) -> p t m", t=PACK), ws_sc_raw[:].rearrange("p (m t) -> p t m", t=PACK)
+            rows_sc[:, 2 * J : ROW_B].rearrange("p (t m) -> p t m", t=PACK),
+            ws_sc_raw[:].rearrange("p (m t) -> p t m", t=PACK),
         )
-        wd_sc_raw = placed([P, N], U8, "wd_sc_raw", 11 * KB)
         ws = sb([P, PASSES, 2 * R], U8, "ws")
         nc.gpsimd.tensor_copy(
             ws[:].bitcast(U16).rearrange("p a (t m) -> p a t m", t=PACK),
             ws_raw[:].bitcast(U16).rearrange("p a (m t) -> p a t m", t=PACK),
         )
-        g_sc = [placed([P, J], U8, f"g_sc{side}", side * KB) for side in (SRC, DST)]
+        g_sc = [sb([P, J], U8, "g_src"), placed([P, J], U8, "g_dst", 16 * KB - 512)]
         for side in (SRC, DST):
             nc.vector.tensor_copy(g_sc[side][:], tab_sc[:].indirect(lists[side][:]))
         for side in (SRC, DST):
             nc.vector.tensor_copy(rows_sc[:, side * J : (side + 1) * J].bitcast(I32), g_sc[side][:].bitcast(I32))
 
-        def move_planes(a, eng):
+        def move_planes(a):
             for q in range(QUADS):
                 row = 16 * a + 4 * q
-                eng.dma_start(planes[a][32 * q : 32 * q + 4, :].bitcast(I32), rows_sc[row : row + 4, :].bitcast(I32))
+                nc.sync.dma_start(
+                    planes[a][32 * q : 32 * q + 4, :].bitcast(I32), rows_sc[row : row + 4, :].bitcast(I32)
+                )
 
-        move_planes(0, nc.scalar)
-        load_and_round_wt(1, R // 2, R, placed([P, PACK, R // 2], F32, "wt_b", 7 * KB)[:])
-        planes.append(sb([P, ROW_B], U8, "planes1", tag="wt_rest"))
+        move_planes(0)
+        load_tab(placed([P, T], I32, "tab1", 24 * KB))
+        planes.append(placed([P, ROW_B], U8, "planes1", 40 * KB))
         nc.gpsimd.memset(planes[1][:].bitcast(I32), 0)
-        move_planes(1, nc.sync)
+        wd_sc_raw = placed([P, N], U8, "wd_sc_raw", 42 * KB + 512)
         nc.gpsimd.memset(wd_sc_raw[:].bitcast(I32), 0)
-
+        move_planes(1)
+        wd_raw = placed([P, 2 * N], U8, "wd_raw", 43 * KB)
+        nc.sync.dma_start(wd_raw[:].bitcast(I32), wd_words[0].bitcast(I32))
         for q in range(QUADS):
             nc.sync.dma_start(wd_sc_raw[32 * q : 32 * q + 4, :].bitcast(I32), wd_scales[0, 4 * q : 4 * q + 4, :].bitcast(I32))
-        wd_raw = placed([P, 2 * N], U8, "wd_raw", 11 * KB + 512)
-        nc.sync.dma_start(wd_raw[:].bitcast(I32), wd_words[0].bitcast(I32))
+        edge_w = placed([P, J], F32, "edge_w", 44 * KB)
+        nc.sync.dma_start(edge_w[:], wgo)
+        pages.append(placed([P, T], F32, "page1", 16 * KB))
+        nc.gpsimd.memset(pages[1][:], 0.0)
 
         g_words = {}
 
-        def gather_words(half, side, a, dst):
-            g_words[(half, side, a)] = dst
+        def gather_words(side, a, j0, j1, dst):
+            for j in range(j0, j1, BANK_J):
+                g_words[(side, a, j // BANK_J)] = dst[:, j - j0 : j - j0 + BANK_J]
             nc.vector.tensor_copy(
-                dst.bitcast(U32),
-                tab[a][:].bitcast(U32).indirect(lists[side][:, half * HALF // LIST_ROWS : (half + 1) * HALF // LIST_ROWS]),
+                dst.bitcast(U32), tab[a][:].bitcast(U32).indirect(lists[side][:, j0 // LIST_ROWS : j1 // LIST_ROWS])
             )
 
         def gather_run(tile, pieces):
-            for k, (half, side, a) in enumerate(pieces):
-                gather_words(half, side, a, tile[:, k * HALF : (k + 1) * HALF])
+            at = 0
+            for side, a, j0, j1 in pieces:
+                gather_words(side, a, j0, j1, tile[:, at : at + j1 - j0])
+                at = at + j1 - j0
 
         wt_q = sb([P, PASSES * R], I32, "wt_q")
         wt_sc = sb([P, PASSES * R], U8, "wt_sc")
@@ -144,20 +154,22 @@ def tile_list_msg_relu_noneP_kernel(
             cols = slice(a * R, (a + 1) * R)
             nc.vector.quantize_mx(wt_q[:, cols].bitcast(FP8X4), wt_sc[:, cols], wt_bf[a][:])
 
-        gather_run(placed([P, 3 * HALF], I32, "g_first", 0), [(0, SRC, 0), (0, DST, 0), (1, SRC, 0)])
+        gather_run(
+            placed([P, 2 * J], I32, "g_first", 8 * KB),
+            [(SRC, 0, 0, HALF), (DST, 0, 0, HALF), (SRC, 0, HALF, J), (DST, 0, HALF, J)],
+        )
         quantize_wt(0)
-        pages = [placed([P, T], F32, "page0", 62 * KB)]
-        nc.gpsimd.memset(pages[0][:], 0.0)
-        gather_run(sb([P, 2 * HALF], I32, "g_second"), [(0, SRC, 1), (0, DST, 1)])
         quantize_wt(1)
-        edge_w = placed([P, J], F32, "edge_w", 26 * KB + 512)
-        nc.sync.dma_start(edge_w[:], wgo)
-        wd = placed([P, 2 * N], U8, "wd", 24 * KB)
+        gather_run(
+            sb([P, 3 * HALF], I32, "g_second"),
+            [(SRC, 1, 0, CHUNK_J), (DST, 1, 0, CHUNK_J), (SRC, 1, CHUNK_J, HALF), (DST, 1, CHUNK_J, HALF), (SRC, 1, HALF, J)],
+        )
+        wd = sb([P, 2 * N], U8, "wd", tag="wt_bf1")
         nc.gpsimd.tensor_copy(
             wd[:].bitcast(U16).rearrange("p (t m) -> p t m", t=PACK),
             wd_raw[:].bitcast(U16).rearrange("p (m t) -> p t m", t=PACK),
         )
-        wd_sc = placed([P, N], U8, "wd_sc", 26 * KB)
+        wd_sc = sb([P, N], U8, "wd_sc")
         nc.gpsimd.tensor_copy(
             wd_sc[:].rearrange("p (t m) -> p t m", t=PACK), wd_sc_raw[:].rearrange("p (m t) -> p t m", t=PACK)
         )
@@ -166,7 +178,7 @@ def tile_list_msg_relu_noneP_kernel(
 
         def first_product(side, a, b):
             cols = slice(side * J + b * BANK_J, side * J + (b + 1) * BANK_J)
-            half, j0 = divmod(b * BANK_J, HALF)
+            half = b * BANK_J // HALF
             for t in range(PACK):
                 if side == SRC:
                     lhsT = ws[:, a, 2 * P * t : 2 * P * (t + 1)].bitcast(FP4X4)
@@ -178,15 +190,15 @@ def tile_list_msg_relu_noneP_kernel(
                     acc[b][:, t, :],
                     lhsT=lhsT,
                     lhsT_scale=lhsT_scale,
-                    rhs=g_words[(half, side, a)][:, j0 : j0 + BANK_J].bitcast(FP8X4),
+                    rhs=g_words[(side, a, b)].bitcast(FP8X4),
                     rhs_scale=planes[a][:, cols],
                     start=((side, a) == (SRC, half) and t == 0),
-                    stop=(side == DST and a == PASSES - 1 and t == PACK - 1),
+                    stop=((side, a) == (DST, 1 - half) and t == PACK - 1),
                 )
 
         h_q = sb([P, J], I32, "h_q")
         h_sc = sb([P, J], U8, "h_sc")
-        y = sb([P, PACK, J], F32, "y")
+        y = [sb([P, 2, J], F32, "y01")]
         late = []
 
         def relu(b, h_bf, j0):
@@ -215,12 +227,13 @@ def tile_list_msg_relu_noneP_kernel(
                 if j0 < HALF and u == 1:
                     late.append(res)
                 else:
-                    nc.scalar.activation(y[:, per_bank * u : per_bank * (u + 1), j0:j1], res[:], ACT.Copy)
+                    t0 = per_bank * u
+                    nc.scalar.activation(y[t0 // 2][:, t0 % 2 : t0 % 2 + per_bank, j0:j1], res[:], ACT.Copy)
 
-        def scatter(t, j0, j1, src=None):
+        def scatter(t, j0, j1):
             nc.vector.tensor_tensor(
                 pages[t][:].indirect(dst_list[:, j0 // LIST_ROWS : j1 // LIST_ROWS]),
-                y[:, t, j0:j1] if src is None else src,
+                y[t // 2][:, t % 2, j0:j1],
                 edge_w[:, j0:j1],
                 MULT,
             )
@@ -229,37 +242,34 @@ def tile_list_msg_relu_noneP_kernel(
         for side in (SRC, DST):
             for b in range(half_banks):
                 first_product(side, 0, b)
-        h_first = [sb([P, CHUNK_J * PACK], BF16, "h_first0"), placed([P, CHUNK_J * PACK], BF16, "h_first1", 43 * KB)]
+        h_first = [sb([P, CHUNK_J * PACK], BF16, f"h_first{c}") for c in range(2)]
         for b in range(half_banks):
             first_product(SRC, 1, b)
             first_product(DST, 1, b)
             relu(b, h_first[b // 2], b // 2 * CHUNK_J)
 
-        gather_run(placed([P, 2 * HALF], I32, "g_third", 7 * KB), [(1, SRC, 1), (1, DST, 0)])
         second_product(0, CHUNK_J, h_first[0])
-        gather_run(sb([P, HALF], I32, "g_last", tag="h_first0"), [(1, DST, 1)])
+        gather_run(sb([P, HALF], I32, "g_last", tag="h_first0"), [(DST, 1, HALF, J)])
         second_product(CHUNK_J, HALF, h_first[1])
-        for t in (1, 2):
-            pages.append(placed([P, T], F32, f"page{t}", (36 + 8 * (t - 1)) * KB))
-            nc.gpsimd.memset(pages[t][:], 0.0)
-        for side, a in ((SRC, 1), (SRC, 0), (DST, 0), (DST, 1)):
+        pages.append(sb([P, T], F32, "page2", tag="h_first1"))
+        nc.gpsimd.memset(pages[2][:], 0.0)
+        for side, a in ((SRC, 1), (DST, 1), (SRC, 0), (DST, 0)):
             for b in range(half_banks, BANKS):
                 first_product(side, a, b)
         h_second = sb([P, HALF * PACK], BF16, "h_second")
         for b in range(half_banks, BANKS):
             relu(b, h_second, HALF)
 
-        for t in range(2):
-            for j0 in range(0, HALF, CHUNK_J):
+        for j0 in range(0, HALF, CHUNK_J):
+            for t in range(2):
                 scatter(t, j0, j0 + CHUNK_J)
-        y_late = sb([P, 2, HALF], F32, "y_late", tag="h_first0")
+        y.append(placed([P, 2, J], F32, "y23", 8 * KB))
         for c, res in enumerate(late):
-            nc.scalar.activation(y_late[:, :, c * CHUNK_J : (c + 1) * CHUNK_J], res[:], ACT.Copy)
+            nc.scalar.activation(y[1][:, :, c * CHUNK_J : (c + 1) * CHUNK_J], res[:], ACT.Copy)
         second_product(HALF, J, h_second)
         pages.append(sb([P, T], F32, "page3", tag="h_second"))
         nc.gpsimd.memset(pages[3][:], 0.0)
-        for j0 in range(0, HALF, CHUNK_J):
-            scatter(2, j0, j0 + CHUNK_J, y_late[:, 0, j0 : j0 + CHUNK_J])
+        scatter(2, 0, HALF)
 
         pairs_v = sb([P, 2, V_COLS, 2], BF16, "pairs_v")
         pairs_s = sb([P, 2, T - V_COLS, 2], BF16, "pairs_s")
@@ -271,9 +281,7 @@ def tile_list_msg_relu_noneP_kernel(
         last = PACK - 1
 
         for t in range(PACK):
-            if t == last:
-                scatter(t, 0, HALF, y_late[:, 1, :])
-            scatter(t, HALF, J)
+            scatter(t, HALF if t < last else 0, J)
             page = pages[t]
             nc.sync.dma_start(out_rows[:, t, :], page[:])
             if t < 2:
@@ -285,12 +293,14 @@ def tile_list_msg_relu_noneP_kernel(
             if t < last:
                 nc.scalar.activation(pairs_s[:, t // 2, :, t % 2], page[:, V_COLS:T], ACT.Copy)
 
+        for c0, c1 in OUT_CUTS:
+            if c0 < V_COLS:
+                nc.vector.tensor_copy(pairs_v[:, 1, c0:c1, 1], pages[last][:, c0:c1])
         for k, (c0, c1) in enumerate(OUT_CUTS):
             pairs, first = (pairs_v, 0) if c0 < V_COLS else (pairs_s, V_COLS)
             words = pairs[:].rearrange("p u c e -> p u (c e)").bitcast(F32)[:, :, c0 - first : c1 - first]
             woven = o_bf[k][:].bitcast(F32).rearrange("p (c u) -> p c u", u=2)
             if c0 < V_COLS:
-                nc.vector.tensor_copy(pairs[:, 1, c0:c1, 1], pages[last][:, c0:c1])
                 nc.vector.tensor_copy(woven, words.rearrange("p u c -> p c u"))
             else:
                 nc.scalar.activation(pairs[:, 1, c0 - first : c1 - first, 1], pages[last][:, c0:c1], ACT.Copy)

@@ -56,6 +56,8 @@ def tile_list_msg_relu_noneP_kernel(
         tab_sc = sb([P, T], U8, "tab_sc")
         nc.vector.memset(tab_sc[32:64, :].bitcast(I32), 0)
         nc.vector.memset(tab_sc[64:P, :].bitcast(I32), 0)
+        wd_sc_raw = sb([P, N], U8, "wd_sc_raw")
+        nc.gpsimd.memset(wd_sc_raw[:].bitcast(I32), 0)
         ws_sc_raw = sb([P, R], U8, "ws_sc_raw")
         nc.gpsimd.memset(ws_sc_raw[32:64, :].bitcast(I32), 0)
         nc.gpsimd.memset(ws_sc_raw[64:P, :].bitcast(I32), 0)
@@ -65,7 +67,7 @@ def tile_list_msg_relu_noneP_kernel(
         nc.gpsimd.memset(pages[0][:], 0.0)
 
         ws_raw = placed([P, PASSES, 2 * R], U8, "ws_raw", 23 * KB)
-        wt_bf = [sb([P, R * PACK], BF16, "wt_bf0"), sb([P, R * PACK], BF16, "wt_bf1")]
+        wt_bf = [placed([P, R * PACK], BF16, "wt_bf0", KB), sb([P, R * PACK], BF16, "wt_bf1")]
         tab = []
 
         def load_tab(tile):
@@ -90,6 +92,10 @@ def tile_list_msg_relu_noneP_kernel(
         load_tab(sb([P, T], I32, "tab0"))
         nc.sync.dma_start(ws_raw[:].bitcast(I32), ws_words.rearrange("a p c -> p a c").bitcast(I32))
         load_and_round_wt(0, 0, R, placed([P, PACK, R], F32, "wt_raw", 40 * KB))
+        wd_raw = sb([P, 2 * N], U8, "wd_raw")
+        nc.sync.dma_start(wd_raw[:].bitcast(I32), wd_words[0].bitcast(I32))
+        for q in range(QUADS):
+            nc.sync.dma_start(wd_sc_raw[32 * q : 32 * q + 4, :].bitcast(I32), wd_scales[0, 4 * q : 4 * q + 4, :].bitcast(I32))
         load_and_round_wt(1, 0, R // 2, sb([P, PACK, R // 2], F32, "wt_a"))
         load_and_round_wt(1, R // 2, R, sb([P, PACK, R // 2], F32, "wt_b"))
 
@@ -103,7 +109,7 @@ def tile_list_msg_relu_noneP_kernel(
             ws[:].bitcast(U16).rearrange("p a (t m) -> p a t m", t=PACK),
             ws_raw[:].bitcast(U16).rearrange("p a (m t) -> p a t m", t=PACK),
         )
-        g_sc = [sb([P, J], U8, "g_src"), placed([P, J], U8, "g_dst", 16 * KB - 512)]
+        g_sc = [sb([P, J], U8, "g_src"), placed([P, J], U8, "g_dst", 12 * KB)]
         for side in (SRC, DST):
             nc.vector.tensor_copy(g_sc[side][:], tab_sc[:].indirect(lists[side][:]))
         for side in (SRC, DST):
@@ -118,19 +124,11 @@ def tile_list_msg_relu_noneP_kernel(
 
         move_planes(0)
         load_tab(placed([P, T], I32, "tab1", 24 * KB))
-        planes.append(placed([P, ROW_B], U8, "planes1", 40 * KB))
+        planes.append(placed([P, ROW_B], U8, "planes1", 21 * KB))
         nc.gpsimd.memset(planes[1][:].bitcast(I32), 0)
-        wd_sc_raw = placed([P, N], U8, "wd_sc_raw", 42 * KB + 512)
-        nc.gpsimd.memset(wd_sc_raw[:].bitcast(I32), 0)
         move_planes(1)
-        wd_raw = placed([P, 2 * N], U8, "wd_raw", 43 * KB)
-        nc.sync.dma_start(wd_raw[:].bitcast(I32), wd_words[0].bitcast(I32))
-        for q in range(QUADS):
-            nc.sync.dma_start(wd_sc_raw[32 * q : 32 * q + 4, :].bitcast(I32), wd_scales[0, 4 * q : 4 * q + 4, :].bitcast(I32))
         edge_w = placed([P, J], F32, "edge_w", 44 * KB)
         nc.sync.dma_start(edge_w[:], wgo)
-        pages.append(placed([P, T], F32, "page1", 16 * KB))
-        nc.gpsimd.memset(pages[1][:], 0.0)
 
         g_words = {}
 
@@ -154,24 +152,24 @@ def tile_list_msg_relu_noneP_kernel(
             cols = slice(a * R, (a + 1) * R)
             nc.vector.quantize_mx(wt_q[:, cols].bitcast(FP8X4), wt_sc[:, cols], wt_bf[a][:])
 
-        gather_run(
-            placed([P, 2 * J], I32, "g_first", 8 * KB),
-            [(SRC, 0, 0, HALF), (DST, 0, 0, HALF), (SRC, 0, HALF, J), (DST, 0, HALF, J)],
-        )
+        gather_run(placed([P, J], I32, "g_first", 12 * KB), [(SRC, 0, 0, HALF), (DST, 0, 0, HALF)])
         quantize_wt(0)
-        quantize_wt(1)
-        gather_run(
-            sb([P, 3 * HALF], I32, "g_second"),
-            [(SRC, 1, 0, CHUNK_J), (DST, 1, 0, CHUNK_J), (SRC, 1, CHUNK_J, HALF), (DST, 1, CHUNK_J, HALF), (SRC, 1, HALF, J)],
-        )
-        wd = sb([P, 2 * N], U8, "wd", tag="wt_bf1")
+        wd = placed([P, 2 * N], U8, "wd", 512)
         nc.gpsimd.tensor_copy(
             wd[:].bitcast(U16).rearrange("p (t m) -> p t m", t=PACK),
             wd_raw[:].bitcast(U16).rearrange("p (m t) -> p t m", t=PACK),
         )
-        wd_sc = sb([P, N], U8, "wd_sc")
+        wd_sc = placed([P, N], U8, "wd_sc", KB + 512)
         nc.gpsimd.tensor_copy(
             wd_sc[:].rearrange("p (t m) -> p t m", t=PACK), wd_sc_raw[:].rearrange("p (m t) -> p t m", t=PACK)
+        )
+        gather_run(placed([P, J], I32, "g_rest", 2 * KB), [(SRC, 0, HALF, J), (DST, 0, HALF, J)])
+        quantize_wt(1)
+        pages.append(sb([P, T], F32, "page1", tag="wt_bf1"))
+        nc.gpsimd.memset(pages[1][:], 0.0)
+        gather_run(
+            sb([P, 3 * HALF], I32, "g_second"),
+            [(SRC, 1, 0, CHUNK_J), (DST, 1, 0, CHUNK_J), (SRC, 1, CHUNK_J, HALF), (DST, 1, CHUNK_J, HALF), (SRC, 1, HALF, J)],
         )
 
         acc = [psum.tile([P, PACK, BANK_J], F32, name=f"acc{b}", tag=f"bank{b}") for b in range(BANKS)]
@@ -192,7 +190,7 @@ def tile_list_msg_relu_noneP_kernel(
                     lhsT_scale=lhsT_scale,
                     rhs=g_words[(side, a, b)].bitcast(FP8X4),
                     rhs_scale=planes[a][:, cols],
-                    start=((side, a) == (SRC, half) and t == 0),
+                    start=((side, a) == (SRC, 0) and t == 0),
                     stop=((side, a) == (DST, 1 - half) and t == PACK - 1),
                 )
 
@@ -253,7 +251,7 @@ def tile_list_msg_relu_noneP_kernel(
         second_product(CHUNK_J, HALF, h_first[1])
         pages.append(sb([P, T], F32, "page2", tag="h_first1"))
         nc.gpsimd.memset(pages[2][:], 0.0)
-        for side, a in ((SRC, 1), (DST, 1), (SRC, 0), (DST, 0)):
+        for side, a in ((SRC, 0), (DST, 1), (SRC, 1), (DST, 0)):
             for b in range(half_banks, BANKS):
                 first_product(side, a, b)
         h_second = sb([P, HALF * PACK], BF16, "h_second")
@@ -263,7 +261,7 @@ def tile_list_msg_relu_noneP_kernel(
         for j0 in range(0, HALF, CHUNK_J):
             for t in range(2):
                 scatter(t, j0, j0 + CHUNK_J)
-        y.append(placed([P, 2, J], F32, "y23", 8 * KB))
+        y.append(placed([P, 2, J], F32, "y23", 2 * KB))
         for c, res in enumerate(late):
             nc.scalar.activation(y[1][:, :, c * CHUNK_J : (c + 1) * CHUNK_J], res[:], ACT.Copy)
         second_product(HALF, J, h_second)

@@ -54,8 +54,8 @@ def tile_list_msg_relu_noneP_kernel(
         lists = (src_list, dst_list)
 
         tab_sc = sb([P, T], U8, "tab_sc")
-        nc.vector.memset(tab_sc[32:64, :].bitcast(I32), 0)
-        nc.vector.memset(tab_sc[64:P, :].bitcast(I32), 0)
+        nc.gpsimd.memset(tab_sc[32:64, :].bitcast(I32), 0)
+        nc.gpsimd.memset(tab_sc[64:P, :].bitcast(I32), 0)
         wd_sc_raw = sb([P, N], U8, "wd_sc_raw")
         nc.gpsimd.memset(wd_sc_raw[:].bitcast(I32), 0)
         ws_sc_raw = sb([P, R], U8, "ws_sc_raw")

@@ -29,9 +29,11 @@ CHUNK_J = 256
 CHUNKS = J // CHUNK_J
 HALF = J // 2
 KB = 1024
-ROW_B = 2 * J + R
+STAGED = 96
 OUT_CUTS = ((0, 512), (512, 1024), (1024, 1536), (1536, 1792), (1792, 2048))
 V_COLS = 1024
+PLANE_C = 512
+CALL_C = 256
 
 
 def tile_list_msg_relu_noneP_kernel(
@@ -54,20 +56,16 @@ def tile_list_msg_relu_noneP_kernel(
         lists = (src_list, dst_list)
 
         tab_sc = sb([P, T], U8, "tab_sc")
-        nc.gpsimd.memset(tab_sc[32:64, :].bitcast(I32), 0)
-        nc.gpsimd.memset(tab_sc[64:P, :].bitcast(I32), 0)
-        wd_sc_raw = sb([P, N], U8, "wd_sc_raw")
-        nc.gpsimd.memset(wd_sc_raw[:].bitcast(I32), 0)
-        ws_sc_raw = sb([P, R], U8, "ws_sc_raw")
-        nc.gpsimd.memset(ws_sc_raw[32:64, :].bitcast(I32), 0)
-        nc.gpsimd.memset(ws_sc_raw[64:P, :].bitcast(I32), 0)
-        planes = [sb([P, ROW_B], U8, "planes0")]
+        ws_sc_raw = sb([P, PASSES, R], U8, "ws_sc_raw")
+        nc.gpsimd.memset(ws_sc_raw[:].bitcast(I32), 0)
+        nc.gpsimd.memset(tab_sc[0:STAGED, :].bitcast(I32), 0)
+        planes = [sb([P, 2 * J], U8, "planes0")]
         nc.gpsimd.memset(planes[0][:].bitcast(I32), 0)
         pages = [sb([P, T], F32, "page0")]
         nc.gpsimd.memset(pages[0][:], 0.0)
 
-        ws_raw = placed([P, PASSES, 2 * R], U8, "ws_raw", 23 * KB)
-        wt_bf = [placed([P, R * PACK], BF16, "wt_bf0", KB), sb([P, R * PACK], BF16, "wt_bf1")]
+        ws_raw = sb([P, PASSES, 2 * R], U8, "ws_raw")
+        wt_bf = [placed([P, R * PACK], BF16, "wt_bf0", KB), placed([P, R * PACK], BF16, "wt_bf1", 48 * KB)]
         tab = []
 
         def load_tab(tile):
@@ -85,49 +83,51 @@ def tile_list_msg_relu_noneP_kernel(
                 ACT.Copy,
             )
 
+        def deal(dst, src):
+            nc.gpsimd.tensor_copy(dst.rearrange("p (t m) -> p t m", t=PACK), src.rearrange("p (m t) -> p t m", t=PACK))
+
         nc.sync.dma_start(src_list[:], offs)
-        nc.sync.dma_start(tab_sc[0:32, :].bitcast(I32), tab_scales.rearrange("a q t -> (a q) t").bitcast(I32))
+        nc.sync.dma_start(tab_sc[STAGED:P, :].bitcast(I32), tab_scales.rearrange("a q t -> (a q) t").bitcast(I32))
         nc.sync.dma_start(dst_list[:], offs2)
-        nc.sync.dma_start(ws_sc_raw[0:32, :].bitcast(I32), ws_scales.rearrange("a q c -> (a q) c").bitcast(I32))
         load_tab(sb([P, T], I32, "tab0"))
         nc.sync.dma_start(ws_raw[:].bitcast(I32), ws_words.rearrange("a p c -> p a c").bitcast(I32))
-        load_and_round_wt(0, 0, R, placed([P, PACK, R], F32, "wt_raw", 40 * KB))
+        load_and_round_wt(0, 0, R // 2, placed([P, PACK, R // 2], F32, "wt0a", 16 * KB))
+        load_and_round_wt(0, R // 2, R, placed([P, PACK, R // 2], F32, "wt0b", 28 * KB))
+        for q in range(QUADS):
+            nc.sync.dma_start(
+                ws_sc_raw[32 * q : 32 * q + 4, :, :].bitcast(I32),
+                ws_scales[:, 4 * q : 4 * q + 4, :].rearrange("a r c -> r a c").bitcast(I32),
+            )
+        load_and_round_wt(1, 0, R // 2, sb([P, PACK, R // 2], F32, "wt1a"))
         wd_raw = sb([P, 2 * N], U8, "wd_raw")
         nc.sync.dma_start(wd_raw[:].bitcast(I32), wd_words[0].bitcast(I32))
+
+        ws = [sb([P, 2 * R], U8, f"ws{a}") for a in range(PASSES)]
+        ws_sc = [sb([P, R], U8, "ws_sc0"), placed([P, R], U8, "ws_sc1", KB + 512)]
+        deal(ws[0][:].bitcast(U16), ws_raw[:, 0, :].bitcast(U16))
+        deal(ws[1][:].bitcast(U16), ws_raw[:, 1, :].bitcast(U16))
+        deal(ws_sc[0][:], ws_sc_raw[:, 0, :])
+
+        g_sc = sb([P, 2 * J], U8, "g_sc")
+        for side in (SRC, DST):
+            nc.vector.tensor_copy(g_sc[:, side * J : (side + 1) * J], tab_sc[:].indirect(lists[side][:]))
+
+        def move_rows(a):
+            for q in range(QUADS):
+                row = STAGED + 16 * a + 4 * q
+                nc.sync.dma_start(planes[a][32 * q : 32 * q + 4, :].bitcast(I32), g_sc[row : row + 4, :].bitcast(I32))
+
+        move_rows(0)
+        load_and_round_wt(1, R // 2, R, placed([P, PACK, R // 2], F32, "wt1b", 13 * KB))
+        planes.append(placed([P, 2 * J], U8, "planes1", 17 * KB))
+        nc.gpsimd.memset(planes[1][:].bitcast(I32), 0)
+        move_rows(1)
+        load_tab(placed([P, T], I32, "tab1", 21 * KB))
+        wd_sc_raw = placed([P, N], U8, "wd_sc_raw", 19 * KB)
+        nc.gpsimd.memset(wd_sc_raw[:].bitcast(I32), 0)
         for q in range(QUADS):
             nc.sync.dma_start(wd_sc_raw[32 * q : 32 * q + 4, :].bitcast(I32), wd_scales[0, 4 * q : 4 * q + 4, :].bitcast(I32))
-        load_and_round_wt(1, 0, R // 2, sb([P, PACK, R // 2], F32, "wt_a"))
-        load_and_round_wt(1, R // 2, R, sb([P, PACK, R // 2], F32, "wt_b"))
-
-        rows_sc = sb([P, ROW_B], U8, "rows_sc")
-        nc.gpsimd.tensor_copy(
-            rows_sc[:, 2 * J : ROW_B].rearrange("p (t m) -> p t m", t=PACK),
-            ws_sc_raw[:].rearrange("p (m t) -> p t m", t=PACK),
-        )
-        ws = sb([P, PASSES, 2 * R], U8, "ws")
-        nc.gpsimd.tensor_copy(
-            ws[:].bitcast(U16).rearrange("p a (t m) -> p a t m", t=PACK),
-            ws_raw[:].bitcast(U16).rearrange("p a (m t) -> p a t m", t=PACK),
-        )
-        g_sc = [sb([P, J], U8, "g_src"), placed([P, J], U8, "g_dst", 12 * KB)]
-        for side in (SRC, DST):
-            nc.vector.tensor_copy(g_sc[side][:], tab_sc[:].indirect(lists[side][:]))
-        for side in (SRC, DST):
-            nc.vector.tensor_copy(rows_sc[:, side * J : (side + 1) * J].bitcast(I32), g_sc[side][:].bitcast(I32))
-
-        def move_planes(a):
-            for q in range(QUADS):
-                row = 16 * a + 4 * q
-                nc.sync.dma_start(
-                    planes[a][32 * q : 32 * q + 4, :].bitcast(I32), rows_sc[row : row + 4, :].bitcast(I32)
-                )
-
-        move_planes(0)
-        load_tab(placed([P, T], I32, "tab1", 24 * KB))
-        planes.append(placed([P, ROW_B], U8, "planes1", 21 * KB))
-        nc.gpsimd.memset(planes[1][:].bitcast(I32), 0)
-        move_planes(1)
-        edge_w = placed([P, J], F32, "edge_w", 44 * KB)
+        edge_w = placed([P, J], F32, "edge_w", 10 * KB)
         nc.sync.dma_start(edge_w[:], wgo)
 
         g_words = {}
@@ -152,20 +152,16 @@ def tile_list_msg_relu_noneP_kernel(
             cols = slice(a * R, (a + 1) * R)
             nc.vector.quantize_mx(wt_q[:, cols].bitcast(FP8X4), wt_sc[:, cols], wt_bf[a][:])
 
-        gather_run(placed([P, J], I32, "g_first", 12 * KB), [(SRC, 0, 0, HALF), (DST, 0, 0, HALF)])
+        gather_run(sb([P, J], I32, "g_first"), [(SRC, 0, 0, HALF), (DST, 0, 0, HALF)])
         quantize_wt(0)
+        deal(ws_sc[1][:], ws_sc_raw[:, 1, :])
         wd = placed([P, 2 * N], U8, "wd", 512)
-        nc.gpsimd.tensor_copy(
-            wd[:].bitcast(U16).rearrange("p (t m) -> p t m", t=PACK),
-            wd_raw[:].bitcast(U16).rearrange("p (m t) -> p t m", t=PACK),
-        )
-        wd_sc = placed([P, N], U8, "wd_sc", KB + 512)
-        nc.gpsimd.tensor_copy(
-            wd_sc[:].rearrange("p (t m) -> p t m", t=PACK), wd_sc_raw[:].rearrange("p (m t) -> p t m", t=PACK)
-        )
-        gather_run(placed([P, J], I32, "g_rest", 2 * KB), [(SRC, 0, HALF, J), (DST, 0, HALF, J)])
+        deal(wd[:].bitcast(U16), wd_raw[:].bitcast(U16))
+        gather_run(placed([P, J], I32, "g_rest", 30 * KB), [(SRC, 0, HALF, J), (DST, 0, HALF, J)])
         quantize_wt(1)
-        pages.append(sb([P, T], F32, "page1", tag="wt_bf1"))
+        wd_sc = placed([P, N], U8, "wd_sc", 48 * KB)
+        deal(wd_sc[:], wd_sc_raw[:])
+        pages.append(placed([P, T], F32, "page1", 49 * KB))
         nc.gpsimd.memset(pages[1][:], 0.0)
         gather_run(
             sb([P, 3 * HALF], I32, "g_second"),
@@ -179,8 +175,8 @@ def tile_list_msg_relu_noneP_kernel(
             half = b * BANK_J // HALF
             for t in range(PACK):
                 if side == SRC:
-                    lhsT = ws[:, a, 2 * P * t : 2 * P * (t + 1)].bitcast(FP4X4)
-                    lhsT_scale = planes[a][:, 2 * J + P * t : 2 * J + P * (t + 1)]
+                    lhsT = ws[a][:, 2 * P * t : 2 * P * (t + 1)].bitcast(FP4X4)
+                    lhsT_scale = ws_sc[a][:, P * t : P * (t + 1)]
                 else:
                     lhsT = wt_q[:, a * R + P * t : a * R + P * (t + 1)].bitcast(FP8X4)
                     lhsT_scale = wt_sc[:, a * R + P * t : a * R + P * (t + 1)]
@@ -261,7 +257,7 @@ def tile_list_msg_relu_noneP_kernel(
         for j0 in range(0, HALF, CHUNK_J):
             for t in range(2):
                 scatter(t, j0, j0 + CHUNK_J)
-        y.append(placed([P, 2, J], F32, "y23", 2 * KB))
+        y.append(placed([P, 2, J], F32, "y23", 32 * KB))
         for c, res in enumerate(late):
             nc.scalar.activation(y[1][:, :, c * CHUNK_J : (c + 1) * CHUNK_J], res[:], ACT.Copy)
         second_product(HALF, J, h_second)
@@ -273,7 +269,7 @@ def tile_list_msg_relu_noneP_kernel(
         pairs_s = sb([P, 2, T - V_COLS, 2], BF16, "pairs_s")
         o_bf = [sb([P, (c1 - c0) * PACK], BF16, f"o_bf{c0}") for c0, c1 in OUT_CUTS]
         o_q = sb([P, T], I32, "o_q")
-        o_sc = sb([P, T], U8, "o_sc")
+        o_sc = sb([P, PLANE_C], U8, "o_sc")
         out_rows = out_0.rearrange("(p t) c -> p t c", t=PACK)
         out_words = out_1[0].rearrange("p c i -> p (c i)").bitcast(I32)
         last = PACK - 1
@@ -304,7 +300,17 @@ def tile_list_msg_relu_noneP_kernel(
                 nc.scalar.activation(pairs[:, 1, c0 - first : c1 - first, 1], pages[last][:, c0:c1], ACT.Copy)
                 nc.scalar.copy(woven, words.rearrange("p u c -> p c u"))
         for k, (c0, c1) in enumerate(OUT_CUTS):
-            nc.vector.quantize_mx(o_q[:, c0:c1].bitcast(FP8X4), o_sc[:, c0:c1], o_bf[k][:])
+            for c in range(c0, c1, CALL_C):
+                row, at = QUADS * (c // PLANE_C), c % PLANE_C
+                nc.vector.quantize_mx(
+                    o_q[:, c : c + CALL_C].bitcast(FP8X4),
+                    o_sc[row:P, at : at + CALL_C],
+                    o_bf[k][:, (c - c0) * PACK : (c - c0 + CALL_C) * PACK],
+                )
             nc.sync.dma_start(out_words[:, c0:c1], o_q[:, c0:c1])
         for q in range(QUADS):
-            nc.scalar.dma_start(out_2[0, 4 * q : 4 * q + 4, :].bitcast(I32), o_sc[32 * q : 32 * q + 4, :].bitcast(I32))
+            queue = nc.scalar if q % 2 == 0 else nc.sync
+            queue.dma_start(
+                out_2[0, 4 * q : 4 * q + 4, :].rearrange("r (k c) -> k r c", c=PLANE_C).bitcast(I32),
+                o_sc[32 * q : 32 * q + 16, :].bitcast(I32),
+            )

@@ -56,6 +56,8 @@ def tile_list_msg_relu_noneP_kernel(
         lists = (src_list, dst_list)
 
         tab_sc = sb([P, T], U8, "tab_sc")
+        wd_sc_raw = sb([P, N], U8, "wd_sc_raw")
+        nc.gpsimd.memset(wd_sc_raw[:].bitcast(I32), 0)
         ws_sc_raw = sb([P, PASSES, R], U8, "ws_sc_raw")
         nc.gpsimd.memset(ws_sc_raw[:].bitcast(I32), 0)
         nc.gpsimd.memset(tab_sc[0:STAGED, :].bitcast(I32), 0)
@@ -65,7 +67,7 @@ def tile_list_msg_relu_noneP_kernel(
         nc.gpsimd.memset(pages[0][:], 0.0)
 
         ws_raw = sb([P, PASSES, 2 * R], U8, "ws_raw")
-        wt_bf = [placed([P, R * PACK], BF16, "wt_bf0", KB), placed([P, R * PACK], BF16, "wt_bf1", 48 * KB)]
+        wt_bf = [placed([P, R * PACK], BF16, "wt_bf0", 4 * KB), placed([P, R * PACK], BF16, "wt_bf1", 48 * KB)]
         tab = []
 
         def load_tab(tile):
@@ -89,24 +91,19 @@ def tile_list_msg_relu_noneP_kernel(
         nc.sync.dma_start(src_list[:], offs)
         nc.sync.dma_start(tab_sc[STAGED:P, :].bitcast(I32), tab_scales.rearrange("a q t -> (a q) t").bitcast(I32))
         nc.sync.dma_start(dst_list[:], offs2)
+        load_and_round_wt(0, 0, R, placed([P, PACK, R], F32, "wt0", 20 * KB))
+        for q in range(QUADS):
+            nc.sync.dma_start(wd_sc_raw[32 * q : 32 * q + 4, :].bitcast(I32), wd_scales[0, 4 * q : 4 * q + 4, :].bitcast(I32))
         load_tab(sb([P, T], I32, "tab0"))
         nc.sync.dma_start(ws_raw[:].bitcast(I32), ws_words.rearrange("a p c -> p a c").bitcast(I32))
-        load_and_round_wt(0, 0, R // 2, placed([P, PACK, R // 2], F32, "wt0a", 16 * KB))
-        load_and_round_wt(0, R // 2, R, placed([P, PACK, R // 2], F32, "wt0b", 28 * KB))
         for q in range(QUADS):
             nc.sync.dma_start(
                 ws_sc_raw[32 * q : 32 * q + 4, :, :].bitcast(I32),
                 ws_scales[:, 4 * q : 4 * q + 4, :].rearrange("a r c -> r a c").bitcast(I32),
             )
         load_and_round_wt(1, 0, R // 2, sb([P, PACK, R // 2], F32, "wt1a"))
-        wd_raw = sb([P, 2 * N], U8, "wd_raw")
-        nc.sync.dma_start(wd_raw[:].bitcast(I32), wd_words[0].bitcast(I32))
-
-        ws = [sb([P, 2 * R], U8, f"ws{a}") for a in range(PASSES)]
-        ws_sc = [sb([P, R], U8, "ws_sc0"), placed([P, R], U8, "ws_sc1", KB + 512)]
-        deal(ws[0][:].bitcast(U16), ws_raw[:, 0, :].bitcast(U16))
-        deal(ws[1][:].bitcast(U16), ws_raw[:, 1, :].bitcast(U16))
-        deal(ws_sc[0][:], ws_sc_raw[:, 0, :])
+        wd_sc = sb([P, N], U8, "wd_sc")
+        deal(wd_sc[:], wd_sc_raw[:])
 
         g_sc = sb([P, 2 * J], U8, "g_sc")
         for side in (SRC, DST):
@@ -118,17 +115,10 @@ def tile_list_msg_relu_noneP_kernel(
                 nc.sync.dma_start(planes[a][32 * q : 32 * q + 4, :].bitcast(I32), g_sc[row : row + 4, :].bitcast(I32))
 
         move_rows(0)
-        load_and_round_wt(1, R // 2, R, placed([P, PACK, R // 2], F32, "wt1b", 13 * KB))
-        planes.append(placed([P, 2 * J], U8, "planes1", 17 * KB))
-        nc.gpsimd.memset(planes[1][:].bitcast(I32), 0)
-        move_rows(1)
-        load_tab(placed([P, T], I32, "tab1", 21 * KB))
-        wd_sc_raw = placed([P, N], U8, "wd_sc_raw", 19 * KB)
-        nc.gpsimd.memset(wd_sc_raw[:].bitcast(I32), 0)
-        for q in range(QUADS):
-            nc.sync.dma_start(wd_sc_raw[32 * q : 32 * q + 4, :].bitcast(I32), wd_scales[0, 4 * q : 4 * q + 4, :].bitcast(I32))
-        edge_w = placed([P, J], F32, "edge_w", 10 * KB)
-        nc.sync.dma_start(edge_w[:], wgo)
+        load_and_round_wt(1, R // 2, R, placed([P, PACK, R // 2], F32, "wt1b", 21 * KB))
+        wd_raw = placed([P, 2 * N], U8, "wd_raw", 25 * KB)
+        nc.sync.dma_start(wd_raw[:].bitcast(I32), wd_words[0].bitcast(I32))
+        load_tab(placed([P, T], I32, "tab1", 27 * KB))
 
         g_words = {}
 
@@ -152,15 +142,24 @@ def tile_list_msg_relu_noneP_kernel(
             cols = slice(a * R, (a + 1) * R)
             nc.vector.quantize_mx(wt_q[:, cols].bitcast(FP8X4), wt_sc[:, cols], wt_bf[a][:])
 
-        gather_run(sb([P, J], I32, "g_first"), [(SRC, 0, 0, HALF), (DST, 0, 0, HALF)])
         quantize_wt(0)
-        deal(ws_sc[1][:], ws_sc_raw[:, 1, :])
-        wd = placed([P, 2 * N], U8, "wd", 512)
+        g_pass0 = placed([P, 2 * J], I32, "g_pass0", 12 * KB + 64)
+        gather_run(g_pass0[:, 0:J], [(DST, 0, 0, HALF), (SRC, 0, 0, HALF)])
+        ws = [placed([P, 2 * R], U8, "ws0", 4 * KB), placed([P, 2 * R], U8, "ws1", 5 * KB)]
+        ws_sc = [placed([P, R], U8, "ws_sc0", 6 * KB), placed([P, R], U8, "ws_sc1", 48 * KB)]
+        deal(ws[0][:].bitcast(U16), ws_raw[:, 0, :].bitcast(U16))
+        deal(ws_sc[0][:], ws_sc_raw[:, 0, :])
+        planes.append(placed([P, 2 * J], U8, "planes1", 7 * KB + 512))
+        nc.gpsimd.memset(planes[1][:].bitcast(I32), 0)
+        move_rows(1)
+        edge_w = placed([P, J], F32, "edge_w", 21 * KB)
+        nc.sync.dma_start(edge_w[:], wgo)
+        deal(ws[1][:].bitcast(U16), ws_raw[:, 1, :].bitcast(U16))
+        wd = placed([P, 2 * N], U8, "wd", 6 * KB + 512)
         deal(wd[:].bitcast(U16), wd_raw[:].bitcast(U16))
-        gather_run(placed([P, J], I32, "g_rest", 30 * KB), [(SRC, 0, HALF, J), (DST, 0, HALF, J)])
+        gather_run(g_pass0[:, J : 2 * J], [(SRC, 0, HALF, J), (DST, 0, HALF, J)])
         quantize_wt(1)
-        wd_sc = placed([P, N], U8, "wd_sc", 48 * KB)
-        deal(wd_sc[:], wd_sc_raw[:])
+        deal(ws_sc[1][:], ws_sc_raw[:, 1, :])
         pages.append(placed([P, T], F32, "page1", 49 * KB))
         nc.gpsimd.memset(pages[1][:], 0.0)
         gather_run(
@@ -186,7 +185,7 @@ def tile_list_msg_relu_noneP_kernel(
                     lhsT_scale=lhsT_scale,
                     rhs=g_words[(side, a, b)].bitcast(FP8X4),
                     rhs_scale=planes[a][:, cols],
-                    start=((side, a) == (SRC, 0) and t == 0),
+                    start=((side, a) == ((DST, SRC)[half], 0) and t == 0),
                     stop=((side, a) == (DST, 1 - half) and t == PACK - 1),
                 )
 
@@ -233,7 +232,7 @@ def tile_list_msg_relu_noneP_kernel(
             )
 
         half_banks = BANKS // 2
-        for side in (SRC, DST):
+        for side in (DST, SRC):
             for b in range(half_banks):
                 first_product(side, 0, b)
         h_first = [sb([P, CHUNK_J * PACK], BF16, f"h_first{c}") for c in range(2)]
@@ -257,7 +256,7 @@ def tile_list_msg_relu_noneP_kernel(
         for j0 in range(0, HALF, CHUNK_J):
             for t in range(2):
                 scatter(t, j0, j0 + CHUNK_J)
-        y.append(placed([P, 2, J], F32, "y23", 32 * KB))
+        y.append(placed([P, 2, J], F32, "y23", 10 * KB))
         for c, res in enumerate(late):
             nc.scalar.activation(y[1][:, :, c * CHUNK_J : (c + 1) * CHUNK_J], res[:], ACT.Copy)
         second_product(HALF, J, h_second)

@@ -30,6 +30,7 @@ CHUNKS = J // CHUNK_J
 HALF = J // 2
 KB = 1024
 STAGED = 96
+EARLY_BANKS = 2
 OUT_CUTS = ((0, 512), (512, 1024), (1024, 1536), (1536, 1792), (1792, 2048))
 V_COLS = 1024
 PLANE_C = 512
@@ -58,7 +59,7 @@ def tile_list_msg_relu_noneP_kernel(
         tab_sc = sb([P, T], U8, "tab_sc")
         wd_sc_raw = sb([P, N], U8, "wd_sc_raw")
         nc.gpsimd.memset(wd_sc_raw[:].bitcast(I32), 0)
-        ws_sc_raw = sb([P, PASSES, R], U8, "ws_sc_raw")
+        ws_sc_raw = placed([P, PASSES, R], U8, "ws_sc_raw", 76 * KB)
         nc.gpsimd.memset(ws_sc_raw[:].bitcast(I32), 0)
         nc.gpsimd.memset(tab_sc[0:STAGED, :].bitcast(I32), 0)
         planes = [sb([P, 2 * J], U8, "planes0")]
@@ -116,8 +117,6 @@ def tile_list_msg_relu_noneP_kernel(
 
         move_rows(0)
         load_and_round_wt(1, R // 2, R, placed([P, PACK, R // 2], F32, "wt1b", 21 * KB))
-        wd_raw = placed([P, 2 * N], U8, "wd_raw", 25 * KB)
-        nc.sync.dma_start(wd_raw[:].bitcast(I32), wd_words[0].bitcast(I32))
         load_tab(placed([P, T], I32, "tab1", 27 * KB))
 
         g_words = {}
@@ -146,7 +145,7 @@ def tile_list_msg_relu_noneP_kernel(
         g_pass0 = placed([P, 2 * J], I32, "g_pass0", 12 * KB + 64)
         gather_run(g_pass0[:, 0:J], [(DST, 0, 0, HALF), (SRC, 0, 0, HALF)])
         ws = [placed([P, 2 * R], U8, "ws0", 4 * KB), placed([P, 2 * R], U8, "ws1", 5 * KB)]
-        ws_sc = [placed([P, R], U8, "ws_sc0", 6 * KB), placed([P, R], U8, "ws_sc1", 48 * KB)]
+        ws_sc = [placed([P, R], U8, "ws_sc0", 6 * KB), placed([P, R], U8, "ws_sc1", 6 * KB + 512)]
         deal(ws[0][:].bitcast(U16), ws_raw[:, 0, :].bitcast(U16))
         deal(ws_sc[0][:], ws_sc_raw[:, 0, :])
         planes.append(placed([P, 2 * J], U8, "planes1", 7 * KB + 512))
@@ -155,12 +154,14 @@ def tile_list_msg_relu_noneP_kernel(
         edge_w = placed([P, J], F32, "edge_w", 21 * KB)
         nc.sync.dma_start(edge_w[:], wgo)
         deal(ws[1][:].bitcast(U16), ws_raw[:, 1, :].bitcast(U16))
-        wd = placed([P, 2 * N], U8, "wd", 6 * KB + 512)
-        deal(wd[:].bitcast(U16), wd_raw[:].bitcast(U16))
+        deal(ws_sc[1][:], ws_sc_raw[:, 1, :])
+        wd_raw = placed([P, 2 * N], U8, "wd_raw", 76 * KB)
+        nc.sync.dma_start(wd_raw[:].bitcast(I32), wd_words[0].bitcast(I32))
         gather_run(g_pass0[:, J : 2 * J], [(SRC, 0, HALF, J), (DST, 0, HALF, J)])
         quantize_wt(1)
-        deal(ws_sc[1][:], ws_sc_raw[:, 1, :])
-        pages.append(placed([P, T], F32, "page1", 49 * KB))
+        wd = placed([P, 2 * N], U8, "wd", 48 * KB)
+        deal(wd[:].bitcast(U16), wd_raw[:].bitcast(U16))
+        pages.append(placed([P, T], F32, "page1", 76 * KB))
         nc.gpsimd.memset(pages[1][:], 0.0)
         gather_run(
             sb([P, 3 * HALF], I32, "g_second"),
@@ -169,9 +170,15 @@ def tile_list_msg_relu_noneP_kernel(
 
         acc = [psum.tile([P, PACK, BANK_J], F32, name=f"acc{b}", tag=f"bank{b}") for b in range(BANKS)]
 
+        def bank_order(b):
+            if b < BANKS // 2:
+                return ((DST, 0), (SRC, 0), (SRC, 1), (DST, 1))
+            if b < BANKS // 2 + EARLY_BANKS:
+                return ((SRC, 0), (DST, 1), (SRC, 1), (DST, 0))
+            return ((DST, 1), (SRC, 0), (SRC, 1), (DST, 0))
+
         def first_product(side, a, b):
             cols = slice(side * J + b * BANK_J, side * J + (b + 1) * BANK_J)
-            half = b * BANK_J // HALF
             for t in range(PACK):
                 if side == SRC:
                     lhsT = ws[a][:, 2 * P * t : 2 * P * (t + 1)].bitcast(FP4X4)
@@ -185,8 +192,8 @@ def tile_list_msg_relu_noneP_kernel(
                     lhsT_scale=lhsT_scale,
                     rhs=g_words[(side, a, b)].bitcast(FP8X4),
                     rhs_scale=planes[a][:, cols],
-                    start=((side, a) == ((DST, SRC)[half], 0) and t == 0),
-                    stop=((side, a) == (DST, 1 - half) and t == PACK - 1),
+                    start=((side, a) == bank_order(b)[0] and t == 0),
+                    stop=((side, a) == bank_order(b)[-1] and t == PACK - 1),
                 )
 
         h_q = sb([P, J], I32, "h_q")
@@ -246,11 +253,10 @@ def tile_list_msg_relu_noneP_kernel(
         second_product(CHUNK_J, HALF, h_first[1])
         pages.append(sb([P, T], F32, "page2", tag="h_first1"))
         nc.gpsimd.memset(pages[2][:], 0.0)
-        for side, a in ((SRC, 0), (DST, 1), (SRC, 1), (DST, 0)):
-            for b in range(half_banks, BANKS):
-                first_product(side, a, b)
         h_second = sb([P, HALF * PACK], BF16, "h_second")
         for b in range(half_banks, BANKS):
+            for side, a in bank_order(b):
+                first_product(side, a, b)
             relu(b, h_second, HALF)
 
         for j0 in range(0, HALF, CHUNK_J):

@@ -33,6 +33,7 @@ STAGED = 96
 EARLY_BANKS = 2
 OUT_CUTS = ((0, 512), (512, 1024), (1024, 1536), (1536, 1792), (1792, 2048))
 V_COLS = 1024
+ROUND_CUTS = ((0, 512), (512, 1024), (1024, 1536), (1536, 2048))
 PLANE_C = 512
 CALL_C = 256
 
@@ -64,8 +65,9 @@ def tile_list_msg_relu_noneP_kernel(
         nc.gpsimd.memset(tab_sc[0:STAGED, :].bitcast(I32), 0)
         planes = [sb([P, 2 * J], U8, "planes0")]
         nc.gpsimd.memset(planes[0][:].bitcast(I32), 0)
-        pages = [sb([P, T], F32, "page0")]
-        nc.gpsimd.memset(pages[0][:], 0.0)
+        pages = [sb([P, T], F32, f"page{t}") for t in range(2)]
+        for page in pages:
+            nc.gpsimd.memset(page[:], 0.0)
 
         ws_raw = sb([P, PASSES, 2 * R], U8, "ws_raw")
         wt_bf = [placed([P, R * PACK], BF16, "wt_bf0", 4 * KB), placed([P, R * PACK], BF16, "wt_bf1", 48 * KB)]
@@ -103,8 +105,6 @@ def tile_list_msg_relu_noneP_kernel(
                 ws_scales[:, 4 * q : 4 * q + 4, :].rearrange("a r c -> r a c").bitcast(I32),
             )
         load_and_round_wt(1, 0, R // 2, sb([P, PACK, R // 2], F32, "wt1a"))
-        wd_sc = sb([P, N], U8, "wd_sc")
-        deal(wd_sc[:], wd_sc_raw[:])
 
         g_sc = sb([P, 2 * J], U8, "g_sc")
         for side in (SRC, DST):
@@ -151,18 +151,18 @@ def tile_list_msg_relu_noneP_kernel(
         planes.append(placed([P, 2 * J], U8, "planes1", 7 * KB + 512))
         nc.gpsimd.memset(planes[1][:].bitcast(I32), 0)
         move_rows(1)
-        edge_w = placed([P, J], F32, "edge_w", 21 * KB)
-        nc.sync.dma_start(edge_w[:], wgo)
         deal(ws[1][:].bitcast(U16), ws_raw[:, 1, :].bitcast(U16))
         deal(ws_sc[1][:], ws_sc_raw[:, 1, :])
         wd_raw = placed([P, 2 * N], U8, "wd_raw", 76 * KB)
         nc.sync.dma_start(wd_raw[:].bitcast(I32), wd_words[0].bitcast(I32))
         gather_run(g_pass0[:, J : 2 * J], [(SRC, 0, HALF, J), (DST, 0, HALF, J)])
         quantize_wt(1)
+        wd_sc = placed([P, N], U8, "wd_sc", 49 * KB)
+        deal(wd_sc[:], wd_sc_raw[:])
         wd = placed([P, 2 * N], U8, "wd", 48 * KB)
         deal(wd[:].bitcast(U16), wd_raw[:].bitcast(U16))
-        pages.append(placed([P, T], F32, "page1", 76 * KB))
-        nc.gpsimd.memset(pages[1][:], 0.0)
+        edge_w = placed([P, J], F32, "edge_w", 51 * KB)
+        nc.sync.dma_start(edge_w[:], wgo)
         gather_run(
             sb([P, 3 * HALF], I32, "g_second"),
             [(SRC, 1, 0, CHUNK_J), (DST, 1, 0, CHUNK_J), (SRC, 1, CHUNK_J, HALF), (DST, 1, CHUNK_J, HALF), (SRC, 1, HALF, J)],
@@ -292,9 +292,11 @@ def tile_list_msg_relu_noneP_kernel(
             if t < last:
                 nc.scalar.activation(pairs_s[:, t // 2, :, t % 2], page[:, V_COLS:T], ACT.Copy)
 
-        for c0, c1 in OUT_CUTS:
+        for c0, c1 in ROUND_CUTS:
             if c0 < V_COLS:
                 nc.vector.tensor_copy(pairs_v[:, 1, c0:c1, 1], pages[last][:, c0:c1])
+            else:
+                nc.scalar.activation(pairs_s[:, 1, c0 - V_COLS : c1 - V_COLS, 1], pages[last][:, c0:c1], ACT.Copy)
         for k, (c0, c1) in enumerate(OUT_CUTS):
             pairs, first = (pairs_v, 0) if c0 < V_COLS else (pairs_s, V_COLS)
             words = pairs[:].rearrange("p u c e -> p u (c e)").bitcast(F32)[:, :, c0 - first : c1 - first]
@@ -302,7 +304,6 @@ def tile_list_msg_relu_noneP_kernel(
             if c0 < V_COLS:
                 nc.vector.tensor_copy(woven, words.rearrange("p u c -> p c u"))
             else:
-                nc.scalar.activation(pairs[:, 1, c0 - first : c1 - first, 1], pages[last][:, c0:c1], ACT.Copy)
                 nc.scalar.copy(woven, words.rearrange("p u c -> p c u"))
         for k, (c0, c1) in enumerate(OUT_CUTS):
             for c in range(c0, c1, CALL_C):

@@ -30,7 +30,7 @@ CHUNKS = J // CHUNK_J
 HALF = J // 2
 KB = 1024
 STAGED = 96
-EARLY_BANKS = 2
+EARLY_BANKS = 0
 OUT_CUTS = ((0, 512), (512, 1024), (1024, 1536), (1536, 1792), (1792, 2048))
 V_COLS = 1024
 ROUND_CUTS = ((0, 512), (512, 1024), (1024, 1536), (1536, 2048))
@@ -60,16 +60,14 @@ def tile_list_msg_relu_noneP_kernel(
         tab_sc = sb([P, T], U8, "tab_sc")
         wd_sc_raw = sb([P, N], U8, "wd_sc_raw")
         nc.gpsimd.memset(wd_sc_raw[:].bitcast(I32), 0)
-        ws_sc_raw = placed([P, PASSES, R], U8, "ws_sc_raw", 76 * KB)
+        ws_sc_raw = placed([P, PASSES, R], U8, "ws_sc_raw", 47 * KB)
         nc.gpsimd.memset(ws_sc_raw[:].bitcast(I32), 0)
         nc.gpsimd.memset(tab_sc[0:STAGED, :].bitcast(I32), 0)
         planes = [sb([P, 2 * J], U8, "planes0")]
         nc.gpsimd.memset(planes[0][:].bitcast(I32), 0)
-        pages = [sb([P, T], F32, f"page{t}") for t in range(2)]
-        for page in pages:
-            nc.gpsimd.memset(page[:], 0.0)
+        pages = [sb([P, T], F32, "page0")]
+        nc.gpsimd.memset(pages[0][:], 0.0)
 
-        ws_raw = sb([P, PASSES, 2 * R], U8, "ws_raw")
         wt_bf = [placed([P, R * PACK], BF16, "wt_bf0", 4 * KB), placed([P, R * PACK], BF16, "wt_bf1", 48 * KB)]
         tab = []
 
@@ -88,6 +86,11 @@ def tile_list_msg_relu_noneP_kernel(
                 ACT.Copy,
             )
 
+        def deal_words(dst, src):
+            nc.scalar.copy(
+                dst.bitcast(U16).rearrange("p (t m) -> p t m", t=PACK), src.bitcast(U16).rearrange("p (m t) -> p t m", t=PACK)
+            )
+
         def deal(dst, src):
             nc.gpsimd.tensor_copy(dst.rearrange("p (t m) -> p t m", t=PACK), src.rearrange("p (m t) -> p t m", t=PACK))
 
@@ -98,13 +101,14 @@ def tile_list_msg_relu_noneP_kernel(
         for q in range(QUADS):
             nc.sync.dma_start(wd_sc_raw[32 * q : 32 * q + 4, :].bitcast(I32), wd_scales[0, 4 * q : 4 * q + 4, :].bitcast(I32))
         load_tab(sb([P, T], I32, "tab0"))
-        nc.sync.dma_start(ws_raw[:].bitcast(I32), ws_words.rearrange("a p c -> p a c").bitcast(I32))
         for q in range(QUADS):
             nc.sync.dma_start(
                 ws_sc_raw[32 * q : 32 * q + 4, :, :].bitcast(I32),
                 ws_scales[:, 4 * q : 4 * q + 4, :].rearrange("a r c -> r a c").bitcast(I32),
             )
-        load_and_round_wt(1, 0, R // 2, sb([P, PACK, R // 2], F32, "wt1a"))
+        wd_sc = sb([P, N], U8, "wd_sc")
+        deal(wd_sc[:], wd_sc_raw[:])
+        load_and_round_wt(1, 0, R, placed([P, PACK, R], F32, "wt1", 60 * KB))
 
         g_sc = sb([P, 2 * J], U8, "g_sc")
         for side in (SRC, DST):
@@ -116,7 +120,8 @@ def tile_list_msg_relu_noneP_kernel(
                 nc.sync.dma_start(planes[a][32 * q : 32 * q + 4, :].bitcast(I32), g_sc[row : row + 4, :].bitcast(I32))
 
         move_rows(0)
-        load_and_round_wt(1, R // 2, R, placed([P, PACK, R // 2], F32, "wt1b", 21 * KB))
+        ws_raw = placed([P, PASSES, 2 * R], U8, "ws_raw", 21 * KB)
+        nc.sync.dma_start(ws_raw[:].bitcast(I32), ws_words.rearrange("a p c -> p a c").bitcast(I32))
         load_tab(placed([P, T], I32, "tab1", 27 * KB))
 
         g_words = {}
@@ -144,27 +149,27 @@ def tile_list_msg_relu_noneP_kernel(
         quantize_wt(0)
         g_pass0 = placed([P, 2 * J], I32, "g_pass0", 12 * KB + 64)
         gather_run(g_pass0[:, 0:J], [(DST, 0, 0, HALF), (SRC, 0, 0, HALF)])
-        ws = [placed([P, 2 * R], U8, "ws0", 4 * KB), placed([P, 2 * R], U8, "ws1", 5 * KB)]
         ws_sc = [placed([P, R], U8, "ws_sc0", 6 * KB), placed([P, R], U8, "ws_sc1", 6 * KB + 512)]
-        deal(ws[0][:].bitcast(U16), ws_raw[:, 0, :].bitcast(U16))
         deal(ws_sc[0][:], ws_sc_raw[:, 0, :])
         planes.append(placed([P, 2 * J], U8, "planes1", 7 * KB + 512))
         nc.gpsimd.memset(planes[1][:].bitcast(I32), 0)
         move_rows(1)
-        deal(ws[1][:].bitcast(U16), ws_raw[:, 1, :].bitcast(U16))
+        ws = [placed([P, 2 * R], U8, f"ws{a}", (4 + a) * KB) for a in range(PASSES)]
+        deal(ws[0][:].bitcast(U16), ws_raw[:, 0, :].bitcast(U16))
         deal(ws_sc[1][:], ws_sc_raw[:, 1, :])
-        wd_raw = placed([P, 2 * N], U8, "wd_raw", 76 * KB)
+        deal(ws[1][:].bitcast(U16), ws_raw[:, 1, :].bitcast(U16))
+        wd_raw = placed([P, 2 * N], U8, "wd_raw", 47 * KB)
         nc.sync.dma_start(wd_raw[:].bitcast(I32), wd_words[0].bitcast(I32))
+        wd = sb([P, 2 * N], U8, "wd")
+        deal_words(wd[:], wd_raw[:])
         gather_run(g_pass0[:, J : 2 * J], [(SRC, 0, HALF, J), (DST, 0, HALF, J)])
         quantize_wt(1)
-        wd_sc = placed([P, N], U8, "wd_sc", 49 * KB)
-        deal(wd_sc[:], wd_sc_raw[:])
-        wd = placed([P, 2 * N], U8, "wd", 48 * KB)
-        deal(wd[:].bitcast(U16), wd_raw[:].bitcast(U16))
+        pages.append(placed([P, T], F32, "page1", 41 * KB))
+        nc.gpsimd.memset(pages[1][:], 0.0)
         edge_w = placed([P, J], F32, "edge_w", 51 * KB)
         nc.sync.dma_start(edge_w[:], wgo)
         gather_run(
-            sb([P, 3 * HALF], I32, "g_second"),
+            placed([P, 3 * HALF], I32, "g_second", 67 * KB),
             [(SRC, 1, 0, CHUNK_J), (DST, 1, 0, CHUNK_J), (SRC, 1, CHUNK_J, HALF), (DST, 1, CHUNK_J, HALF), (SRC, 1, HALF, J)],
         )
 
@@ -230,10 +235,10 @@ def tile_list_msg_relu_noneP_kernel(
                     t0 = per_bank * u
                     nc.scalar.activation(y[t0 // 2][:, t0 % 2 : t0 % 2 + per_bank, j0:j1], res[:], ACT.Copy)
 
-        def scatter(t, j0, j1):
+        def scatter(t, j0, j1, values=None):
             nc.vector.tensor_tensor(
                 pages[t][:].indirect(dst_list[:, j0 // LIST_ROWS : j1 // LIST_ROWS]),
-                y[t // 2][:, t % 2, j0:j1],
+                y[t // 2][:, t % 2, j0:j1] if values is None else values,
                 edge_w[:, j0:j1],
                 MULT,
             )
@@ -242,7 +247,7 @@ def tile_list_msg_relu_noneP_kernel(
         for side in (DST, SRC):
             for b in range(half_banks):
                 first_product(side, 0, b)
-        h_first = [sb([P, CHUNK_J * PACK], BF16, f"h_first{c}") for c in range(2)]
+        h_first = [sb([P, CHUNK_J * PACK], BF16, "h_first0"), placed([P, CHUNK_J * PACK], BF16, "h_first1", 87 * KB + 512)]
         for b in range(half_banks):
             first_product(SRC, 1, b)
             first_product(DST, 1, b)
@@ -251,8 +256,9 @@ def tile_list_msg_relu_noneP_kernel(
         second_product(0, CHUNK_J, h_first[0])
         gather_run(sb([P, HALF], I32, "g_last", tag="h_first0"), [(DST, 1, HALF, J)])
         second_product(CHUNK_J, HALF, h_first[1])
-        pages.append(sb([P, T], F32, "page2", tag="h_first1"))
-        nc.gpsimd.memset(pages[2][:], 0.0)
+        for t in (2, 3):
+            pages.append(placed([P, T], F32, f"page{t}", (80 + 9 * (t - 2)) * KB))
+            nc.gpsimd.memset(pages[t][:], 0.0)
         h_second = sb([P, HALF * PACK], BF16, "h_second")
         for b in range(half_banks, BANKS):
             for side, a in bank_order(b):
@@ -263,12 +269,15 @@ def tile_list_msg_relu_noneP_kernel(
             for t in range(2):
                 scatter(t, j0, j0 + CHUNK_J)
         y.append(placed([P, 2, J], F32, "y23", 10 * KB))
+        y_early = sb([P, CHUNK_J], F32, "y_early")
+        nc.scalar.activation(y_early[:], late[0][:, 0, :], ACT.Copy)
+        scatter(2, 0, CHUNK_J, y_early[:])
+        nc.scalar.activation(y[1][:, 0, CHUNK_J:HALF], late[1][:, 0, :], ACT.Copy)
         for c, res in enumerate(late):
-            nc.scalar.activation(y[1][:, :, c * CHUNK_J : (c + 1) * CHUNK_J], res[:], ACT.Copy)
+            nc.scalar.activation(y[1][:, 1, c * CHUNK_J : (c + 1) * CHUNK_J], res[:, 1, :], ACT.Copy)
         second_product(HALF, J, h_second)
-        pages.append(sb([P, T], F32, "page3", tag="h_second"))
-        nc.gpsimd.memset(pages[3][:], 0.0)
-        scatter(2, 0, HALF)
+        scatter(2, CHUNK_J, HALF)
+        scatter(3, 0, CHUNK_J)
 
         pairs_v = sb([P, 2, V_COLS, 2], BF16, "pairs_v")
         pairs_s = sb([P, 2, T - V_COLS, 2], BF16, "pairs_s")
@@ -280,7 +289,7 @@ def tile_list_msg_relu_noneP_kernel(
         last = PACK - 1
 
         for t in range(PACK):
-            scatter(t, HALF if t < last else 0, J)
+            scatter(t, HALF if t < last else CHUNK_J, J)
             page = pages[t]
             nc.sync.dma_start(out_rows[:, t, :], page[:])
             if t < 2:

@@ -33,7 +33,7 @@ STAGED = 96
 EARLY_BANKS = 0
 OUT_CUTS = ((0, 512), (512, 1024), (1024, 1536), (1536, 1792), (1792, 2048))
 V_COLS = 1024
-ROUND_CUTS = ((0, 512), (512, 1024), (1024, 1536), (1536, 2048))
+ROUND_C = 512
 PLANE_C = 512
 CALL_C = 256
 
@@ -203,8 +203,7 @@ def tile_list_msg_relu_noneP_kernel(
 
         h_q = sb([P, J], I32, "h_q")
         h_sc = sb([P, J], U8, "h_sc")
-        y = [sb([P, 2, J], F32, "y01")]
-        late = []
+        y = [sb([P, 2, J], F32, "y01"), placed([P, 2, J], F32, "y23", 10 * KB)]
 
         def relu(b, h_bf, j0):
             nc.scalar.activation(
@@ -213,32 +212,31 @@ def tile_list_msg_relu_noneP_kernel(
                 ACT.Relu,
             )
 
-        def second_product(j0, j1, h_bf):
-            nc.vector.quantize_mx(h_q[:, j0:j1].bitcast(FP8X4), h_sc[:, j0:j1], h_bf[:])
-            per_bank = BANK_J * PACK // (j1 - j0)
-            for u in range(PACK // per_bank):
-                res = psum.tile([P, per_bank, j1 - j0], F32, name=f"res{j0}_{u}", tag=f"bank{j0 // BANK_J + u}")
-                for e in range(per_bank):
-                    t = per_bank * u + e
-                    nc.tensor.matmul_mx(
-                        res[:, e, :],
-                        lhsT=wd[:, 2 * P * t : 2 * P * (t + 1)].bitcast(FP4X4),
-                        lhsT_scale=wd_sc[:, P * t : P * (t + 1)],
-                        rhs=h_q[:, j0:j1].bitcast(FP8X4),
-                        rhs_scale=h_sc[:, j0:j1],
-                        start=True,
-                        stop=True,
-                    )
-                if j0 < HALF and u == 1:
-                    late.append(res)
-                else:
-                    t0 = per_bank * u
-                    nc.scalar.activation(y[t0 // 2][:, t0 % 2 : t0 % 2 + per_bank, j0:j1], res[:], ACT.Copy)
+        def second_product(c, h_bf, groups):
+            cols = slice(c * CHUNK_J, (c + 1) * CHUNK_J)
+            nc.vector.quantize_mx(h_q[:, cols].bitcast(FP8X4), h_sc[:, cols], h_bf[:])
+            for t0, t1, bank in groups:
+                slices(c, t0, t1, bank)
 
-        def scatter(t, j0, j1, values=None):
+        def slices(c, t0, t1, bank):
+            cols = slice(c * CHUNK_J, (c + 1) * CHUNK_J)
+            res = psum.tile([P, t1 - t0, CHUNK_J], F32, name=f"res{c}_{t0}", tag=f"bank{bank}")
+            for t in range(t0, t1):
+                nc.tensor.matmul_mx(
+                    res[:, t - t0, :],
+                    lhsT=wd[:, 2 * P * t : 2 * P * (t + 1)].bitcast(FP4X4),
+                    lhsT_scale=wd_sc[:, P * t : P * (t + 1)],
+                    rhs=h_q[:, cols].bitcast(FP8X4),
+                    rhs_scale=h_sc[:, cols],
+                    start=True,
+                    stop=True,
+                )
+            nc.scalar.activation(y[t0 // 2][:, t0 % 2 : t0 % 2 + t1 - t0, cols], res[:], ACT.Copy)
+
+        def scatter(t, j0, j1):
             nc.vector.tensor_tensor(
                 pages[t][:].indirect(dst_list[:, j0 // LIST_ROWS : j1 // LIST_ROWS]),
-                y[t // 2][:, t % 2, j0:j1] if values is None else values,
+                y[t // 2][:, t % 2, j0:j1],
                 edge_w[:, j0:j1],
                 MULT,
             )
@@ -253,74 +251,75 @@ def tile_list_msg_relu_noneP_kernel(
             first_product(DST, 1, b)
             relu(b, h_first[b // 2], b // 2 * CHUNK_J)
 
-        second_product(0, CHUNK_J, h_first[0])
+        second_product(0, h_first[0], ((0, 2, 0),))
         gather_run(sb([P, HALF], I32, "g_last", tag="h_first0"), [(DST, 1, HALF, J)])
-        second_product(CHUNK_J, HALF, h_first[1])
+        second_product(1, h_first[1], ((0, 1, 2),))
         for t in (2, 3):
             pages.append(placed([P, T], F32, f"page{t}", (80 + 9 * (t - 2)) * KB))
             nc.gpsimd.memset(pages[t][:], 0.0)
-        h_second = sb([P, HALF * PACK], BF16, "h_second")
+        for t, c in ((0, 0), (1, 0), (0, 1)):
+            scatter(t, c * CHUNK_J, (c + 1) * CHUNK_J)
+        h_second = [sb([P, CHUNK_J * PACK], BF16, f"h_second{c}") for c in (2, 3)]
         for b in range(half_banks, BANKS):
             for side, a in bank_order(b):
                 first_product(side, a, b)
-            relu(b, h_second, HALF)
+            relu(b, h_second[b // 2 - 2], b // 2 * CHUNK_J)
+            if b == 5:
+                slices(1, 1, 2, b)
+        second_product(2, h_second[0], ((0, 2, 4),))
+        scatter(1, CHUNK_J, HALF)
+        second_product(3, h_second[1], ((0, 2, 6),))
+        for t in range(2):
+            scatter(t, HALF, HALF + CHUNK_J)
+        for c in (2, 3):
+            slices(c, 2, 4, 2 * c - 4)
+        for c in (0, 1):
+            slices(c, 2, 4, 2 * c + 1)
 
-        for j0 in range(0, HALF, CHUNK_J):
-            for t in range(2):
-                scatter(t, j0, j0 + CHUNK_J)
-        y.append(placed([P, 2, J], F32, "y23", 10 * KB))
-        y_early = sb([P, CHUNK_J], F32, "y_early")
-        nc.scalar.activation(y_early[:], late[0][:, 0, :], ACT.Copy)
-        scatter(2, 0, CHUNK_J, y_early[:])
-        nc.scalar.activation(y[1][:, 0, CHUNK_J:HALF], late[1][:, 0, :], ACT.Copy)
-        for c, res in enumerate(late):
-            nc.scalar.activation(y[1][:, 1, c * CHUNK_J : (c + 1) * CHUNK_J], res[:, 1, :], ACT.Copy)
-        second_product(HALF, J, h_second)
-        scatter(2, CHUNK_J, HALF)
-        scatter(3, 0, CHUNK_J)
-
-        pairs_v = sb([P, 2, V_COLS, 2], BF16, "pairs_v")
-        pairs_s = sb([P, 2, T - V_COLS, 2], BF16, "pairs_s")
-        o_bf = [sb([P, (c1 - c0) * PACK], BF16, f"o_bf{c0}") for c0, c1 in OUT_CUTS]
+        S_COLS = T - V_COLS
+        pairs01 = sb([P, V_COLS, 2], BF16, "pairs01")
+        pairs_s = sb([P, 2, S_COLS, 2], BF16, "pairs_s")
+        woven = sb([P, V_COLS, PACK], BF16, "woven")
+        o_bf = [woven[:, c0:c1, :] if c0 < V_COLS else sb([P, c1 - c0, PACK], BF16, f"o_bf{c0}")[:] for c0, c1 in OUT_CUTS]
+        v_cuts = [(k, c0, c1) for k, (c0, c1) in enumerate(OUT_CUTS) if c0 < V_COLS]
+        s_cuts = [(k, c0, c1) for k, (c0, c1) in enumerate(OUT_CUTS) if c0 >= V_COLS]
         o_q = sb([P, T], I32, "o_q")
         o_sc = sb([P, PLANE_C], U8, "o_sc")
         out_rows = out_0.rearrange("(p t) c -> p t c", t=PACK)
         out_words = out_1[0].rearrange("p c i -> p (c i)").bitcast(I32)
         last = PACK - 1
 
-        for t in range(PACK):
-            scatter(t, HALF if t < last else CHUNK_J, J)
+        def as_words(tile):
+            return tile.rearrange("p c i -> p (c i)").bitcast(F32).rearrange("p (c u) -> p c u", u=2)
+
+        for t, j0 in ((0, J - CHUNK_J), (1, J - CHUNK_J), (2, 0), (last, 0)):
+            scatter(t, j0, J)
             page = pages[t]
             nc.sync.dma_start(out_rows[:, t, :], page[:])
             if t < 2:
-                nc.scalar.activation(pairs_v[:, 0, :, t], page[:, 0:V_COLS], ACT.Copy)
+                nc.scalar.activation(pairs01[:, :, t], page[:, 0:V_COLS], ACT.Copy)
             if t == 2:
-                nc.scalar.activation(
-                    pairs_v[:, 1, :, :], page[:, 0:V_COLS].unsqueeze(2).to_broadcast([P, V_COLS, 2]), ACT.Copy
-                )
+                nc.scalar.activation(woven[:, :, 2:4], page[:, 0:V_COLS].unsqueeze(2).to_broadcast([P, V_COLS, 2]), ACT.Copy)
             if t < last:
                 nc.scalar.activation(pairs_s[:, t // 2, :, t % 2], page[:, V_COLS:T], ACT.Copy)
+            if t == 1:
+                words01 = pairs01[:].rearrange("p c e -> p (c e)").bitcast(F32)
+                nc.scalar.copy(as_words(woven[:]), words01.unsqueeze(2).to_broadcast([P, V_COLS, 2]))
 
-        for c0, c1 in ROUND_CUTS:
-            if c0 < V_COLS:
-                nc.vector.tensor_copy(pairs_v[:, 1, c0:c1, 1], pages[last][:, c0:c1])
-            else:
-                nc.scalar.activation(pairs_s[:, 1, c0 - V_COLS : c1 - V_COLS, 1], pages[last][:, c0:c1], ACT.Copy)
-        for k, (c0, c1) in enumerate(OUT_CUTS):
-            pairs, first = (pairs_v, 0) if c0 < V_COLS else (pairs_s, V_COLS)
-            words = pairs[:].rearrange("p u c e -> p u (c e)").bitcast(F32)[:, :, c0 - first : c1 - first]
-            woven = o_bf[k][:].bitcast(F32).rearrange("p (c u) -> p c u", u=2)
-            if c0 < V_COLS:
-                nc.vector.tensor_copy(woven, words.rearrange("p u c -> p c u"))
-            else:
-                nc.scalar.copy(woven, words.rearrange("p u c -> p c u"))
+        for k, c0, c1 in v_cuts:
+            nc.vector.tensor_copy(o_bf[k][:, :, last], pages[last][:, c0:c1])
+        for c0 in range(V_COLS, T, ROUND_C):
+            nc.scalar.activation(pairs_s[:, 1, c0 - V_COLS : c0 - V_COLS + ROUND_C, 1], pages[last][:, c0 : c0 + ROUND_C], ACT.Copy)
+        for k, c0, c1 in s_cuts:
+            words = pairs_s[:].rearrange("p u c e -> p u (c e)").bitcast(F32)[:, :, c0 - V_COLS : c1 - V_COLS]
+            nc.scalar.copy(as_words(o_bf[k]), words.rearrange("p u c -> p c u"))
         for k, (c0, c1) in enumerate(OUT_CUTS):
             for c in range(c0, c1, CALL_C):
                 row, at = QUADS * (c // PLANE_C), c % PLANE_C
                 nc.vector.quantize_mx(
                     o_q[:, c : c + CALL_C].bitcast(FP8X4),
                     o_sc[row:P, at : at + CALL_C],
-                    o_bf[k][:, (c - c0) * PACK : (c - c0 + CALL_C) * PACK],
+                    o_bf[k][:, c - c0 : c - c0 + CALL_C, :].rearrange("p c i -> p (c i)"),
                 )
             nc.sync.dma_start(out_words[:, c0:c1], o_q[:, c0:c1])
         for q in range(QUADS):

@@ -108,6 +108,11 @@ def tile_list_msg_relu_noneP_kernel(
             )
         wd_sc = sb([P, N], U8, "wd_sc")
         deal(wd_sc[:], wd_sc_raw[:])
+        ws_raw = sb([P, PASSES, 2 * R], U8, "ws_raw")
+        nc.sync.dma_start(ws_raw[:].bitcast(I32), ws_words.rearrange("a p c -> p a c").bitcast(I32))
+        ws = [sb([P, 2 * R], U8, f"ws{a}") for a in range(PASSES)]
+        for a in range(PASSES):
+            deal_words(ws[a][:], ws_raw[:, a, :])
         load_and_round_wt(1, 0, R, placed([P, PACK, R], F32, "wt1", 60 * KB))
 
         g_sc = sb([P, 2 * J], U8, "g_sc")
@@ -120,8 +125,6 @@ def tile_list_msg_relu_noneP_kernel(
                 nc.sync.dma_start(planes[a][32 * q : 32 * q + 4, :].bitcast(I32), g_sc[row : row + 4, :].bitcast(I32))
 
         move_rows(0)
-        ws_raw = placed([P, PASSES, 2 * R], U8, "ws_raw", 21 * KB)
-        nc.sync.dma_start(ws_raw[:].bitcast(I32), ws_words.rearrange("a p c -> p a c").bitcast(I32))
         load_tab(placed([P, T], I32, "tab1", 27 * KB))
 
         g_words = {}
@@ -154,10 +157,7 @@ def tile_list_msg_relu_noneP_kernel(
         planes.append(placed([P, 2 * J], U8, "planes1", 7 * KB + 512))
         nc.gpsimd.memset(planes[1][:].bitcast(I32), 0)
         move_rows(1)
-        ws = [placed([P, 2 * R], U8, f"ws{a}", (4 + a) * KB) for a in range(PASSES)]
-        deal(ws[0][:].bitcast(U16), ws_raw[:, 0, :].bitcast(U16))
         deal(ws_sc[1][:], ws_sc_raw[:, 1, :])
-        deal(ws[1][:].bitcast(U16), ws_raw[:, 1, :].bitcast(U16))
         wd_raw = placed([P, 2 * N], U8, "wd_raw", 47 * KB)
         nc.sync.dma_start(wd_raw[:].bitcast(I32), wd_words[0].bitcast(I32))
         wd = sb([P, 2 * N], U8, "wd")
@@ -245,7 +245,7 @@ def tile_list_msg_relu_noneP_kernel(
         for side in (DST, SRC):
             for b in range(half_banks):
                 first_product(side, 0, b)
-        h_first = [sb([P, CHUNK_J * PACK], BF16, "h_first0"), placed([P, CHUNK_J * PACK], BF16, "h_first1", 87 * KB + 512)]
+        h_first = [sb([P, CHUNK_J * PACK], BF16, "h_first0"), sb([P, CHUNK_J * PACK], BF16, "h_first1")]
         for b in range(half_banks):
             first_product(SRC, 1, b)
             first_product(DST, 1, b)
@@ -254,12 +254,9 @@ def tile_list_msg_relu_noneP_kernel(
         second_product(0, h_first[0], ((0, 2, 0),))
         gather_run(sb([P, HALF], I32, "g_last", tag="h_first0"), [(DST, 1, HALF, J)])
         second_product(1, h_first[1], ((0, 1, 2),))
-        for t in (2, 3):
-            pages.append(placed([P, T], F32, f"page{t}", (80 + 9 * (t - 2)) * KB))
-            nc.gpsimd.memset(pages[t][:], 0.0)
         for t, c in ((0, 0), (1, 0), (0, 1)):
             scatter(t, c * CHUNK_J, (c + 1) * CHUNK_J)
-        h_second = [sb([P, CHUNK_J * PACK], BF16, f"h_second{c}") for c in (2, 3)]
+        h_second = [sb([P, CHUNK_J * PACK], BF16, "h_second2"), placed([P, CHUNK_J * PACK], BF16, "h_second3", 87 * KB + 512)]
         for b in range(half_banks, BANKS):
             for side, a in bank_order(b):
                 first_product(side, a, b)
@@ -269,6 +266,9 @@ def tile_list_msg_relu_noneP_kernel(
         second_product(2, h_second[0], ((0, 2, 4),))
         scatter(1, CHUNK_J, HALF)
         second_product(3, h_second[1], ((0, 2, 6),))
+        for t in (2, 3):
+            pages.append(placed([P, T], F32, f"page{t}", (80 + 9 * (t - 2)) * KB))
+            nc.gpsimd.memset(pages[t][:], 0.0)
         for t in range(2):
             scatter(t, HALF, HALF + CHUNK_J)
         for c in (2, 3):

@@ -63,8 +63,9 @@ def tile_list_msg_relu_noneP_kernel(
         ws_sc_raw = placed([P, PASSES, R], U8, "ws_sc_raw", 47 * KB)
         nc.gpsimd.memset(ws_sc_raw[:].bitcast(I32), 0)
         nc.gpsimd.memset(tab_sc[0:STAGED, :].bitcast(I32), 0)
-        planes = [sb([P, 2 * J], U8, "planes0")]
-        nc.gpsimd.memset(planes[0][:].bitcast(I32), 0)
+        planes = [sb([P, 2 * J], U8, f"planes{a}") for a in range(PASSES)]
+        for plane in planes:
+            nc.gpsimd.memset(plane[:].bitcast(I32), 0)
         pages = [sb([P, T], F32, "page0")]
         nc.gpsimd.memset(pages[0][:], 0.0)
 
@@ -75,13 +76,11 @@ def tile_list_msg_relu_noneP_kernel(
             nc.sync.dma_start(tile[:], tab_words[len(tab)].rearrange("p t i -> p (t i)").bitcast(I32))
             tab.append(tile)
 
-        def load_and_round_wt(a, c0, c1, part):
+        def load_and_round_wt(a, i0, i1, part):
             rows = wt[a * K_PASS : (a + 1) * K_PASS, :].rearrange("(p i) c -> p i c", i=PACK)
-            nc.sync.dma_start(part[:], rows[:, :, c0:c1])
+            nc.sync.dma_start(part[:], rows[:, i0:i1, :])
             nc.scalar.activation(
-                wt_bf[a][:].rearrange("p (t m i) -> p m i t", t=PACK, i=PACK)[
-                    :, c0 // PACK : c1 // PACK, :, :
-                ],
+                wt_bf[a][:].rearrange("p (t m i) -> p m i t", t=PACK, i=PACK)[:, :, i0:i1, :],
                 part[:].rearrange("p i (m t) -> p m i t", t=PACK),
                 ACT.Copy,
             )
@@ -97,10 +96,11 @@ def tile_list_msg_relu_noneP_kernel(
         nc.sync.dma_start(src_list[:], offs)
         nc.sync.dma_start(tab_sc[STAGED:P, :].bitcast(I32), tab_scales.rearrange("a q t -> (a q) t").bitcast(I32))
         nc.sync.dma_start(dst_list[:], offs2)
-        load_and_round_wt(0, 0, R, placed([P, PACK, R], F32, "wt0", 20 * KB))
+        load_and_round_wt(0, 0, 2, placed([P, 2, R], F32, "wt0_low", 24 * KB))
         for q in range(QUADS):
             nc.sync.dma_start(wd_sc_raw[32 * q : 32 * q + 4, :].bitcast(I32), wd_scales[0, 4 * q : 4 * q + 4, :].bitcast(I32))
         load_tab(sb([P, T], I32, "tab0"))
+        load_and_round_wt(0, 2, PACK, placed([P, 2, R], F32, "wt0_high", 20 * KB))
         for q in range(QUADS):
             nc.sync.dma_start(
                 ws_sc_raw[32 * q : 32 * q + 4, :, :].bitcast(I32),
@@ -108,12 +108,19 @@ def tile_list_msg_relu_noneP_kernel(
             )
         wd_sc = sb([P, N], U8, "wd_sc")
         deal(wd_sc[:], wd_sc_raw[:])
-        ws_raw = sb([P, PASSES, 2 * R], U8, "ws_raw")
-        nc.sync.dma_start(ws_raw[:].bitcast(I32), ws_words.rearrange("a p c -> p a c").bitcast(I32))
-        ws = [sb([P, 2 * R], U8, f"ws{a}") for a in range(PASSES)]
+        ws_sc = [sb([P, R], U8, f"ws_sc{a}") for a in range(PASSES)]
         for a in range(PASSES):
-            deal_words(ws[a][:], ws_raw[:, a, :])
-        load_and_round_wt(1, 0, R, placed([P, PACK, R], F32, "wt1", 60 * KB))
+            deal(ws_sc[a][:], ws_sc_raw[:, a, :])
+        ws = []
+
+        def load_and_deal_ws(a):
+            raw = sb([P, 2 * R], U8, f"ws_raw{a}")
+            nc.sync.dma_start(raw[:].bitcast(I32), ws_words[a].bitcast(I32))
+            ws.append(sb([P, 2 * R], U8, f"ws{a}"))
+            deal_words(ws[a][:], raw[:])
+
+        load_and_deal_ws(0)
+        load_and_round_wt(1, 0, PACK, placed([P, PACK, R], F32, "wt1", 60 * KB))
 
         g_sc = sb([P, 2 * J], U8, "g_sc")
         for side in (SRC, DST):
@@ -125,7 +132,9 @@ def tile_list_msg_relu_noneP_kernel(
                 nc.sync.dma_start(planes[a][32 * q : 32 * q + 4, :].bitcast(I32), g_sc[row : row + 4, :].bitcast(I32))
 
         move_rows(0)
-        load_tab(placed([P, T], I32, "tab1", 27 * KB))
+        load_tab(sb([P, T], I32, "tab1"))
+        load_and_deal_ws(1)
+        move_rows(1)
 
         g_words = {}
 
@@ -149,20 +158,14 @@ def tile_list_msg_relu_noneP_kernel(
             cols = slice(a * R, (a + 1) * R)
             nc.vector.quantize_mx(wt_q[:, cols].bitcast(FP8X4), wt_sc[:, cols], wt_bf[a][:])
 
+        gather_run(sb([P, J], I32, "g_first"), [(SRC, 0, 0, HALF), (DST, 0, 0, HALF)])
         quantize_wt(0)
-        g_pass0 = placed([P, 2 * J], I32, "g_pass0", 12 * KB + 64)
-        gather_run(g_pass0[:, 0:J], [(DST, 0, 0, HALF), (SRC, 0, 0, HALF)])
-        ws_sc = [placed([P, R], U8, "ws_sc0", 6 * KB), placed([P, R], U8, "ws_sc1", 6 * KB + 512)]
-        deal(ws_sc[0][:], ws_sc_raw[:, 0, :])
-        planes.append(placed([P, 2 * J], U8, "planes1", 7 * KB + 512))
-        nc.gpsimd.memset(planes[1][:].bitcast(I32), 0)
-        move_rows(1)
-        deal(ws_sc[1][:], ws_sc_raw[:, 1, :])
-        wd_raw = placed([P, 2 * N], U8, "wd_raw", 47 * KB)
+        g_pass0 = placed([P, J], I32, "g_pass0", 16 * KB + 64)
+        wd_raw = placed([P, 2 * N], U8, "wd_raw", 21 * KB)
         nc.sync.dma_start(wd_raw[:].bitcast(I32), wd_words[0].bitcast(I32))
         wd = sb([P, 2 * N], U8, "wd")
         deal_words(wd[:], wd_raw[:])
-        gather_run(g_pass0[:, J : 2 * J], [(SRC, 0, HALF, J), (DST, 0, HALF, J)])
+        gather_run(g_pass0[:], [(SRC, 0, HALF, J), (DST, 0, HALF, J)])
         quantize_wt(1)
         pages.append(placed([P, T], F32, "page1", 41 * KB))
         nc.gpsimd.memset(pages[1][:], 0.0)
@@ -177,7 +180,7 @@ def tile_list_msg_relu_noneP_kernel(
 
         def bank_order(b):
             if b < BANKS // 2:
-                return ((DST, 0), (SRC, 0), (SRC, 1), (DST, 1))
+                return ((SRC, 0), (DST, 0), (SRC, 1), (DST, 1))
             if b < BANKS // 2 + EARLY_BANKS:
                 return ((SRC, 0), (DST, 1), (SRC, 1), (DST, 0))
             return ((DST, 1), (SRC, 0), (SRC, 1), (DST, 0))
@@ -242,7 +245,7 @@ def tile_list_msg_relu_noneP_kernel(
             )
 
         half_banks = BANKS // 2
-        for side in (DST, SRC):
+        for side in (SRC, DST):
             for b in range(half_banks):
                 first_product(side, 0, b)
         h_first = [sb([P, CHUNK_J * PACK], BF16, "h_first0"), sb([P, CHUNK_J * PACK], BF16, "h_first1")]

@@ -86,9 +86,7 @@ def tile_list_msg_relu_noneP_kernel(
             )
 
         def deal_words(dst, src):
-            nc.scalar.copy(
-                dst.bitcast(U16).rearrange("p (t m) -> p t m", t=PACK), src.bitcast(U16).rearrange("p (m t) -> p t m", t=PACK)
-            )
+            nc.scalar.copy(dst.rearrange("p (t m) -> p t m", t=PACK), src.rearrange("p (m t) -> p t m", t=PACK))
 
         def deal(dst, src):
             nc.gpsimd.tensor_copy(dst.rearrange("p (t m) -> p t m", t=PACK), src.rearrange("p (m t) -> p t m", t=PACK))
@@ -96,11 +94,10 @@ def tile_list_msg_relu_noneP_kernel(
         nc.sync.dma_start(src_list[:], offs)
         nc.sync.dma_start(tab_sc[STAGED:P, :].bitcast(I32), tab_scales.rearrange("a q t -> (a q) t").bitcast(I32))
         nc.sync.dma_start(dst_list[:], offs2)
-        load_and_round_wt(0, 0, 2, placed([P, 2, R], F32, "wt0_low", 24 * KB))
+        load_tab(sb([P, T], I32, "tab0"))
         for q in range(QUADS):
             nc.sync.dma_start(wd_sc_raw[32 * q : 32 * q + 4, :].bitcast(I32), wd_scales[0, 4 * q : 4 * q + 4, :].bitcast(I32))
-        load_tab(sb([P, T], I32, "tab0"))
-        load_and_round_wt(0, 2, PACK, placed([P, 2, R], F32, "wt0_high", 20 * KB))
+        load_and_round_wt(0, 0, PACK, placed([P, PACK, R], F32, "wt0", 20 * KB))
         for q in range(QUADS):
             nc.sync.dma_start(
                 ws_sc_raw[32 * q : 32 * q + 4, :, :].bitcast(I32),
@@ -113,13 +110,13 @@ def tile_list_msg_relu_noneP_kernel(
             deal(ws_sc[a][:], ws_sc_raw[:, a, :])
         ws = []
 
-        def load_and_deal_ws(a):
+        def load_and_deal_ws(a, how):
             raw = sb([P, 2 * R], U8, f"ws_raw{a}")
             nc.sync.dma_start(raw[:].bitcast(I32), ws_words[a].bitcast(I32))
             ws.append(sb([P, 2 * R], U8, f"ws{a}"))
-            deal_words(ws[a][:], raw[:])
+            how(ws[a][:].bitcast(U16), raw[:].bitcast(U16))
 
-        load_and_deal_ws(0)
+        load_and_deal_ws(0, deal)
         load_and_round_wt(1, 0, PACK, placed([P, PACK, R], F32, "wt1", 60 * KB))
 
         g_sc = sb([P, 2 * J], U8, "g_sc")
@@ -133,7 +130,7 @@ def tile_list_msg_relu_noneP_kernel(
 
         move_rows(0)
         load_tab(sb([P, T], I32, "tab1"))
-        load_and_deal_ws(1)
+        load_and_deal_ws(1, deal_words)
         move_rows(1)
 
         g_words = {}
@@ -158,14 +155,14 @@ def tile_list_msg_relu_noneP_kernel(
             cols = slice(a * R, (a + 1) * R)
             nc.vector.quantize_mx(wt_q[:, cols].bitcast(FP8X4), wt_sc[:, cols], wt_bf[a][:])
 
-        gather_run(sb([P, J], I32, "g_first"), [(SRC, 0, 0, HALF), (DST, 0, 0, HALF)])
+        gather_run(sb([P, HALF + J], I32, "g_first"), [(SRC, 0, 0, J), (DST, 0, 0, HALF)])
         quantize_wt(0)
-        g_pass0 = placed([P, J], I32, "g_pass0", 16 * KB + 64)
+        g_pass0 = placed([P, HALF], I32, "g_pass0", 18 * KB + 64)
         wd_raw = placed([P, 2 * N], U8, "wd_raw", 21 * KB)
         nc.sync.dma_start(wd_raw[:].bitcast(I32), wd_words[0].bitcast(I32))
         wd = sb([P, 2 * N], U8, "wd")
-        deal_words(wd[:], wd_raw[:])
-        gather_run(g_pass0[:], [(SRC, 0, HALF, J), (DST, 0, HALF, J)])
+        deal_words(wd[:].bitcast(U16), wd_raw[:].bitcast(U16))
+        gather_run(g_pass0[:], [(DST, 0, HALF, J)])
         quantize_wt(1)
         pages.append(placed([P, T], F32, "page1", 41 * KB))
         nc.gpsimd.memset(pages[1][:], 0.0)
@@ -206,7 +203,7 @@ def tile_list_msg_relu_noneP_kernel(
 
         h_q = sb([P, J], I32, "h_q")
         h_sc = sb([P, J], U8, "h_sc")
-        y = [sb([P, 2, J], F32, "y01"), placed([P, 2, J], F32, "y23", 10 * KB)]
+        y = [sb([P, 2, J], F32, "y01"), placed([P, 2, J], F32, "y23", 11 * KB)]
 
         def relu(b, h_bf, j0):
             nc.scalar.activation(

@@ -58,11 +58,11 @@ def tile_list_msg_relu_noneP_kernel(
         lists = (src_list, dst_list)
 
         tab_sc = sb([P, T], U8, "tab_sc")
+        nc.gpsimd.memset(tab_sc[0:STAGED, :].bitcast(I32), 0)
         wd_sc_raw = sb([P, N], U8, "wd_sc_raw")
         nc.gpsimd.memset(wd_sc_raw[:].bitcast(I32), 0)
         ws_sc_raw = placed([P, PASSES, R], U8, "ws_sc_raw", 47 * KB)
         nc.gpsimd.memset(ws_sc_raw[:].bitcast(I32), 0)
-        nc.gpsimd.memset(tab_sc[0:STAGED, :].bitcast(I32), 0)
         planes = [sb([P, 2 * J], U8, f"planes{a}") for a in range(PASSES)]
         for plane in planes:
             nc.gpsimd.memset(plane[:].bitcast(I32), 0)
@@ -92,7 +92,7 @@ def tile_list_msg_relu_noneP_kernel(
             nc.gpsimd.tensor_copy(dst.rearrange("p (t m) -> p t m", t=PACK), src.rearrange("p (m t) -> p t m", t=PACK))
 
         nc.sync.dma_start(src_list[:], offs)
-        nc.sync.dma_start(tab_sc[STAGED:P, :].bitcast(I32), tab_scales.rearrange("a q t -> (a q) t").bitcast(I32))
+        nc.scalar.dma_start(tab_sc[STAGED:P, :].bitcast(I32), tab_scales.rearrange("a q t -> (a q) t").bitcast(I32))
         nc.sync.dma_start(dst_list[:], offs2)
         load_tab(sb([P, T], I32, "tab0"))
         for q in range(QUADS):
@@ -269,8 +269,7 @@ def tile_list_msg_relu_noneP_kernel(
         for t in (2, 3):
             pages.append(placed([P, T], F32, f"page{t}", (80 + 9 * (t - 2)) * KB))
             nc.gpsimd.memset(pages[t][:], 0.0)
-        for t in range(2):
-            scatter(t, HALF, HALF + CHUNK_J)
+        scatter(0, HALF, HALF + CHUNK_J)
         for c in (2, 3):
             slices(c, 2, 4, 2 * c - 4)
         for c in (0, 1):
@@ -292,7 +291,7 @@ def tile_list_msg_relu_noneP_kernel(
         def as_words(tile):
             return tile.rearrange("p c i -> p (c i)").bitcast(F32).rearrange("p (c u) -> p c u", u=2)
 
-        for t, j0 in ((0, J - CHUNK_J), (1, J - CHUNK_J), (2, 0), (last, 0)):
+        for t, j0 in ((1, HALF), (0, J - CHUNK_J), (2, 0), (last, 0)):
             scatter(t, j0, J)
             page = pages[t]
             nc.sync.dma_start(out_rows[:, t, :], page[:])
@@ -302,7 +301,7 @@ def tile_list_msg_relu_noneP_kernel(
                 nc.scalar.activation(woven[:, :, 2:4], page[:, 0:V_COLS].unsqueeze(2).to_broadcast([P, V_COLS, 2]), ACT.Copy)
             if t < last:
                 nc.scalar.activation(pairs_s[:, t // 2, :, t % 2], page[:, V_COLS:T], ACT.Copy)
-            if t == 1:
+            if t == 0:
                 words01 = pairs01[:].rearrange("p c e -> p (c e)").bitcast(F32)
                 nc.scalar.copy(as_words(woven[:]), words01.unsqueeze(2).to_broadcast([P, V_COLS, 2]))
 

@@ -21,21 +21,22 @@ PACK = 4
 K_PASS = P * PACK
 PASSES = K // K_PASS
 QUADS = 4
+QUAD_P = P // QUADS
+QUAD_ROWS = 4
+PASS_ROWS = QUADS * QUAD_ROWS
 LIST_ROWS = 16
 SRC, DST = 0, 1
 BANK_J = 128
 BANKS = J // BANK_J
 CHUNK_J = 256
-CHUNKS = J // CHUNK_J
 HALF = J // 2
 KB = 1024
-STAGED = 96
-EARLY_BANKS = 0
-OUT_CUTS = ((0, 512), (512, 1024), (1024, 1536), (1536, 1792), (1792, 2048))
+STAGED = P - PASSES * PASS_ROWS
 V_COLS = 1024
+OUT_CUTS = ((0, 512), (512, 1024), (1024, 1536), (1536, 1792), (1792, 2048))
 ROUND_C = 512
-PLANE_C = 512
-CALL_C = 256
+PLANE_C = T // QUADS
+CALL_C = PLANE_C // 2
 
 
 def tile_list_msg_relu_noneP_kernel(
@@ -53,71 +54,85 @@ def tile_list_msg_relu_noneP_kernel(
         def placed(shape, dtype, name, offset):
             return shared.tile(shape, dtype, name=name, tag=name, align_bytes=64, offset=offset)
 
+        def plane_rows(q):
+            return slice(QUAD_P * q, QUAD_P * q + QUAD_ROWS)
+
+        def scale_rows(q):
+            return slice(QUAD_ROWS * q, QUAD_ROWS * (q + 1))
+
+        at_wt_bf = (4 * KB, 48 * KB)
+        at_wt_raw = (20 * KB, 60 * KB)
+        at_ws_sc_raw = 47 * KB
+        at_g_pass0 = at_wt_raw[0] - 2 * KB + 64
+        at_wd_raw = at_wt_raw[0] + KB
+        at_y23 = at_g_pass0 - 7 * KB - 64
+        at_page1 = at_wt_bf[1] - 7 * KB
+        at_edge_w = at_wt_bf[1] + 3 * KB
+        at_g_pass1 = at_wt_raw[1] + 7 * KB
+        at_page2, at_page3 = 80 * KB, 89 * KB
+        at_h_last = at_page2 + 7 * KB + 512
+
         src_list = keep.tile([P, J // LIST_ROWS], U16, name="src_list")
         dst_list = keep.tile([P, J // LIST_ROWS], U16, name="dst_list")
         lists = (src_list, dst_list)
 
         tab_sc = sb([P, T], U8, "tab_sc")
-        nc.gpsimd.memset(tab_sc[0:STAGED, :].bitcast(I32), 0)
         wd_sc_raw = sb([P, N], U8, "wd_sc_raw")
         nc.gpsimd.memset(wd_sc_raw[:].bitcast(I32), 0)
-        ws_sc_raw = placed([P, PASSES, R], U8, "ws_sc_raw", 47 * KB)
+        ws_sc_raw = placed([P, PASSES, R], U8, "ws_sc_raw", at_ws_sc_raw)
         nc.gpsimd.memset(ws_sc_raw[:].bitcast(I32), 0)
+        nc.gpsimd.memset(tab_sc[0:STAGED, :].bitcast(I32), 0)
         planes = [sb([P, 2 * J], U8, f"planes{a}") for a in range(PASSES)]
         for plane in planes:
             nc.gpsimd.memset(plane[:].bitcast(I32), 0)
         pages = [sb([P, T], F32, "page0")]
         nc.gpsimd.memset(pages[0][:], 0.0)
 
-        wt_bf = [placed([P, R * PACK], BF16, "wt_bf0", 4 * KB), placed([P, R * PACK], BF16, "wt_bf1", 48 * KB)]
+        wt_bf = [placed([P, R * PACK], BF16, f"wt_bf{a}", at_wt_bf[a]) for a in range(PASSES)]
         tab = []
+        ws = []
 
-        def load_tab(tile):
-            nc.sync.dma_start(tile[:], tab_words[len(tab)].rearrange("p t i -> p (t i)").bitcast(I32))
-            tab.append(tile)
+        def load_tab(a):
+            tab.append(sb([P, T], I32, f"tab{a}"))
+            nc.sync.dma_start(tab[a][:], tab_words[a].rearrange("p t i -> p (t i)").bitcast(I32))
 
-        def load_and_round_wt(a, i0, i1, part):
-            rows = wt[a * K_PASS : (a + 1) * K_PASS, :].rearrange("(p i) c -> p i c", i=PACK)
-            nc.sync.dma_start(part[:], rows[:, i0:i1, :])
+        def load_and_round_wt(a):
+            raw = placed([P, PACK, R], F32, f"wt{a}", at_wt_raw[a])
+            nc.sync.dma_start(raw[:], wt[a * K_PASS : (a + 1) * K_PASS, :].rearrange("(p i) c -> p i c", i=PACK))
             nc.scalar.activation(
-                wt_bf[a][:].rearrange("p (t m i) -> p m i t", t=PACK, i=PACK)[:, :, i0:i1, :],
-                part[:].rearrange("p i (m t) -> p m i t", t=PACK),
+                wt_bf[a][:].rearrange("p (t m i) -> p m i t", t=PACK, i=PACK),
+                raw[:].rearrange("p i (m t) -> p m i t", t=PACK),
                 ACT.Copy,
             )
 
-        def deal_words(dst, src):
-            nc.scalar.copy(dst.rearrange("p (t m) -> p t m", t=PACK), src.rearrange("p (m t) -> p t m", t=PACK))
+        def deal(copy, dst, src):
+            copy(dst.rearrange("p (t m) -> p t m", t=PACK), src.rearrange("p (m t) -> p t m", t=PACK))
 
-        def deal(dst, src):
-            nc.gpsimd.tensor_copy(dst.rearrange("p (t m) -> p t m", t=PACK), src.rearrange("p (m t) -> p t m", t=PACK))
-
-        nc.sync.dma_start(src_list[:], offs)
-        nc.scalar.dma_start(tab_sc[STAGED:P, :].bitcast(I32), tab_scales.rearrange("a q t -> (a q) t").bitcast(I32))
-        nc.sync.dma_start(dst_list[:], offs2)
-        load_tab(sb([P, T], I32, "tab0"))
-        for q in range(QUADS):
-            nc.sync.dma_start(wd_sc_raw[32 * q : 32 * q + 4, :].bitcast(I32), wd_scales[0, 4 * q : 4 * q + 4, :].bitcast(I32))
-        load_and_round_wt(0, 0, PACK, placed([P, PACK, R], F32, "wt0", 20 * KB))
-        for q in range(QUADS):
-            nc.sync.dma_start(
-                ws_sc_raw[32 * q : 32 * q + 4, :, :].bitcast(I32),
-                ws_scales[:, 4 * q : 4 * q + 4, :].rearrange("a r c -> r a c").bitcast(I32),
-            )
-        wd_sc = sb([P, N], U8, "wd_sc")
-        deal(wd_sc[:], wd_sc_raw[:])
-        ws_sc = [sb([P, R], U8, f"ws_sc{a}") for a in range(PASSES)]
-        for a in range(PASSES):
-            deal(ws_sc[a][:], ws_sc_raw[:, a, :])
-        ws = []
-
-        def load_and_deal_ws(a, how):
+        def load_and_deal_ws(a, copy):
             raw = sb([P, 2 * R], U8, f"ws_raw{a}")
             nc.sync.dma_start(raw[:].bitcast(I32), ws_words[a].bitcast(I32))
             ws.append(sb([P, 2 * R], U8, f"ws{a}"))
-            how(ws[a][:].bitcast(U16), raw[:].bitcast(U16))
+            deal(copy, ws[a][:].bitcast(U16), raw[:].bitcast(U16))
 
-        load_and_deal_ws(0, deal)
-        load_and_round_wt(1, 0, PACK, placed([P, PACK, R], F32, "wt1", 60 * KB))
+        nc.sync.dma_start(src_list[:], offs)
+        nc.sync.dma_start(tab_sc[STAGED:P, :].bitcast(I32), tab_scales.rearrange("a q t -> (a q) t").bitcast(I32))
+        nc.sync.dma_start(dst_list[:], offs2)
+        load_tab(0)
+        for q in range(QUADS):
+            nc.sync.dma_start(wd_sc_raw[plane_rows(q), :].bitcast(I32), wd_scales[0, scale_rows(q), :].bitcast(I32))
+        load_and_round_wt(0)
+        for q in range(QUADS):
+            nc.sync.dma_start(
+                ws_sc_raw[plane_rows(q), :, :].bitcast(I32),
+                ws_scales[:, scale_rows(q), :].rearrange("a r c -> r a c").bitcast(I32),
+            )
+        wd_sc = sb([P, N], U8, "wd_sc")
+        deal(nc.gpsimd.tensor_copy, wd_sc[:], wd_sc_raw[:])
+        ws_sc = [sb([P, R], U8, f"ws_sc{a}") for a in range(PASSES)]
+        for a in range(PASSES):
+            deal(nc.gpsimd.tensor_copy, ws_sc[a][:], ws_sc_raw[:, a, :])
+        load_and_deal_ws(0, nc.gpsimd.tensor_copy)
+        load_and_round_wt(1)
 
         g_sc = sb([P, 2 * J], U8, "g_sc")
         for side in (SRC, DST):
@@ -125,27 +140,25 @@ def tile_list_msg_relu_noneP_kernel(
 
         def move_rows(a):
             for q in range(QUADS):
-                row = STAGED + 16 * a + 4 * q
-                nc.sync.dma_start(planes[a][32 * q : 32 * q + 4, :].bitcast(I32), g_sc[row : row + 4, :].bitcast(I32))
+                row = STAGED + PASS_ROWS * a + QUAD_ROWS * q
+                nc.sync.dma_start(planes[a][plane_rows(q), :].bitcast(I32), g_sc[row : row + QUAD_ROWS, :].bitcast(I32))
 
         move_rows(0)
-        load_tab(sb([P, T], I32, "tab1"))
-        load_and_deal_ws(1, deal_words)
+        load_tab(1)
+        load_and_deal_ws(1, nc.scalar.copy)
         move_rows(1)
 
         g_words = {}
 
-        def gather_words(side, a, j0, j1, dst):
-            for j in range(j0, j1, BANK_J):
-                g_words[(side, a, j // BANK_J)] = dst[:, j - j0 : j - j0 + BANK_J]
-            nc.vector.tensor_copy(
-                dst.bitcast(U32), tab[a][:].bitcast(U32).indirect(lists[side][:, j0 // LIST_ROWS : j1 // LIST_ROWS])
-            )
-
-        def gather_run(tile, pieces):
+        def gather_words(tile, pieces):
             at = 0
             for side, a, j0, j1 in pieces:
-                gather_words(side, a, j0, j1, tile[:, at : at + j1 - j0])
+                dst = tile[:, at : at + j1 - j0]
+                for j in range(j0, j1, BANK_J):
+                    g_words[(side, a, j // BANK_J)] = dst[:, j - j0 : j - j0 + BANK_J]
+                nc.vector.tensor_copy(
+                    dst.bitcast(U32), tab[a][:].bitcast(U32).indirect(lists[side][:, j0 // LIST_ROWS : j1 // LIST_ROWS])
+                )
                 at = at + j1 - j0
 
         wt_q = sb([P, PASSES * R], I32, "wt_q")
@@ -155,31 +168,30 @@ def tile_list_msg_relu_noneP_kernel(
             cols = slice(a * R, (a + 1) * R)
             nc.vector.quantize_mx(wt_q[:, cols].bitcast(FP8X4), wt_sc[:, cols], wt_bf[a][:])
 
-        gather_run(sb([P, HALF + J], I32, "g_first"), [(SRC, 0, 0, J), (DST, 0, 0, HALF)])
+        gather_words(sb([P, HALF + J], I32, "g_first"), [(SRC, 0, 0, J), (DST, 0, 0, HALF)])
         quantize_wt(0)
-        g_pass0 = placed([P, HALF], I32, "g_pass0", 18 * KB + 64)
-        wd_raw = placed([P, 2 * N], U8, "wd_raw", 21 * KB)
+        g_pass0 = placed([P, HALF], I32, "g_pass0", at_g_pass0)
+        wd_raw = placed([P, 2 * N], U8, "wd_raw", at_wd_raw)
         nc.sync.dma_start(wd_raw[:].bitcast(I32), wd_words[0].bitcast(I32))
         wd = sb([P, 2 * N], U8, "wd")
-        deal_words(wd[:].bitcast(U16), wd_raw[:].bitcast(U16))
-        gather_run(g_pass0[:], [(DST, 0, HALF, J)])
+        deal(nc.scalar.copy, wd[:].bitcast(U16), wd_raw[:].bitcast(U16))
+        gather_words(g_pass0[:], [(DST, 0, HALF, J)])
         quantize_wt(1)
-        pages.append(placed([P, T], F32, "page1", 41 * KB))
+        pages.append(placed([P, T], F32, "page1", at_page1))
         nc.gpsimd.memset(pages[1][:], 0.0)
-        edge_w = placed([P, J], F32, "edge_w", 51 * KB)
+        edge_w = placed([P, J], F32, "edge_w", at_edge_w)
         nc.sync.dma_start(edge_w[:], wgo)
-        gather_run(
-            placed([P, 3 * HALF], I32, "g_second", 67 * KB),
-            [(SRC, 1, 0, CHUNK_J), (DST, 1, 0, CHUNK_J), (SRC, 1, CHUNK_J, HALF), (DST, 1, CHUNK_J, HALF), (SRC, 1, HALF, J)],
+        gather_words(
+            placed([P, 3 * HALF], I32, "g_pass1", at_g_pass1),
+            [(side, 1, j, j + CHUNK_J) for j in (0, CHUNK_J) for side in (DST, SRC)] + [(SRC, 1, HALF, J)],
         )
 
         acc = [psum.tile([P, PACK, BANK_J], F32, name=f"acc{b}", tag=f"bank{b}") for b in range(BANKS)]
+        half_banks = BANKS // 2
 
         def bank_order(b):
-            if b < BANKS // 2:
-                return ((SRC, 0), (DST, 0), (SRC, 1), (DST, 1))
-            if b < BANKS // 2 + EARLY_BANKS:
-                return ((SRC, 0), (DST, 1), (SRC, 1), (DST, 0))
+            if b < half_banks:
+                return ((SRC, 0), (DST, 0), (DST, 1), (SRC, 1))
             return ((DST, 1), (SRC, 0), (SRC, 1), (DST, 0))
 
         def first_product(side, a, b):
@@ -203,22 +215,21 @@ def tile_list_msg_relu_noneP_kernel(
 
         h_q = sb([P, J], I32, "h_q")
         h_sc = sb([P, J], U8, "h_sc")
-        y = [sb([P, 2, J], F32, "y01"), placed([P, 2, J], F32, "y23", 11 * KB)]
+        y = [sb([P, 2, J], F32, "y01"), placed([P, 2, J], F32, "y23", at_y23)]
 
-        def relu(b, h_bf, j0):
+        def relu(b, h_bf):
+            j0 = b % 2 * BANK_J
             nc.scalar.activation(
-                h_bf[:, (b * BANK_J - j0) * PACK : ((b + 1) * BANK_J - j0) * PACK].rearrange("p (j t) -> p j t", t=PACK),
+                h_bf[:, j0 * PACK : (j0 + BANK_J) * PACK].rearrange("p (j t) -> p j t", t=PACK),
                 acc[b][:].rearrange("p t j -> p j t"),
                 ACT.Relu,
             )
 
-        def second_product(c, h_bf, groups):
+        def quantize_h(c, h_bf):
             cols = slice(c * CHUNK_J, (c + 1) * CHUNK_J)
             nc.vector.quantize_mx(h_q[:, cols].bitcast(FP8X4), h_sc[:, cols], h_bf[:])
-            for t0, t1, bank in groups:
-                slices(c, t0, t1, bank)
 
-        def slices(c, t0, t1, bank):
+        def second_product(c, t0, t1, bank):
             cols = slice(c * CHUNK_J, (c + 1) * CHUNK_J)
             res = psum.tile([P, t1 - t0, CHUNK_J], F32, name=f"res{c}_{t0}", tag=f"bank{bank}")
             for t in range(t0, t1):
@@ -241,45 +252,49 @@ def tile_list_msg_relu_noneP_kernel(
                 MULT,
             )
 
-        half_banks = BANKS // 2
         for side in (SRC, DST):
             for b in range(half_banks):
                 first_product(side, 0, b)
-        h_first = [sb([P, CHUNK_J * PACK], BF16, "h_first0"), sb([P, CHUNK_J * PACK], BF16, "h_first1")]
+        h_bf = [sb([P, CHUNK_J * PACK], BF16, f"h_bf{c}") for c in range(2)]
         for b in range(half_banks):
-            first_product(SRC, 1, b)
-            first_product(DST, 1, b)
-            relu(b, h_first[b // 2], b // 2 * CHUNK_J)
+            for side in (DST, SRC):
+                first_product(side, 1, b)
+            relu(b, h_bf[b // 2])
 
-        second_product(0, h_first[0], ((0, 2, 0),))
-        gather_run(sb([P, HALF], I32, "g_last", tag="h_first0"), [(DST, 1, HALF, J)])
-        second_product(1, h_first[1], ((0, 1, 2),))
-        for t, c in ((0, 0), (1, 0), (0, 1)):
-            scatter(t, c * CHUNK_J, (c + 1) * CHUNK_J)
-        h_second = [sb([P, CHUNK_J * PACK], BF16, "h_second2"), placed([P, CHUNK_J * PACK], BF16, "h_second3", 87 * KB + 512)]
+        quantize_h(0, h_bf[0])
+        second_product(0, 0, 2, 0)
+        gather_words(sb([P, HALF], I32, "g_last", tag="h_bf0"), [(DST, 1, HALF, J)])
+        quantize_h(1, h_bf[1])
+        second_product(1, 1, 2, 2)
+        scatter(0, 0, CHUNK_J)
+        scatter(1, 0, HALF)
+
+        h_bf.append(sb([P, CHUNK_J * PACK], BF16, "h_bf2"))
+        h_bf.append(placed([P, CHUNK_J * PACK], BF16, "h_bf3", at_h_last))
+        chunk2_last_bank = half_banks + 1
         for b in range(half_banks, BANKS):
             for side, a in bank_order(b):
                 first_product(side, a, b)
-            relu(b, h_second[b // 2 - 2], b // 2 * CHUNK_J)
-            if b == 5:
-                slices(1, 1, 2, b)
-        second_product(2, h_second[0], ((0, 2, 4),))
-        scatter(1, CHUNK_J, HALF)
-        second_product(3, h_second[1], ((0, 2, 6),))
-        for t in (2, 3):
-            pages.append(placed([P, T], F32, f"page{t}", (80 + 9 * (t - 2)) * KB))
+            relu(b, h_bf[b // 2])
+            if b == chunk2_last_bank:
+                second_product(1, 0, 1, b)
+        quantize_h(2, h_bf[2])
+        second_product(2, 0, 2, 4)
+        scatter(0, CHUNK_J, HALF)
+        quantize_h(3, h_bf[3])
+        second_product(3, 0, 2, 6)
+        for t, at in ((2, at_page2), (3, at_page3)):
+            pages.append(placed([P, T], F32, f"page{t}", at))
             nc.gpsimd.memset(pages[t][:], 0.0)
-        scatter(0, HALF, HALF + CHUNK_J)
-        for c in (2, 3):
-            slices(c, 2, 4, 2 * c - 4)
-        for c in (0, 1):
-            slices(c, 2, 4, 2 * c + 1)
+        scatter(1, HALF, HALF + CHUNK_J)
+        for c, bank in ((2, 0), (3, 2), (0, 1), (1, 3)):
+            second_product(c, 2, 4, bank)
 
-        S_COLS = T - V_COLS
-        pairs01 = sb([P, V_COLS, 2], BF16, "pairs01")
-        pairs_s = sb([P, 2, S_COLS, 2], BF16, "pairs_s")
-        woven = sb([P, V_COLS, PACK], BF16, "woven")
-        o_bf = [woven[:, c0:c1, :] if c0 < V_COLS else sb([P, c1 - c0, PACK], BF16, f"o_bf{c0}")[:] for c0, c1 in OUT_CUTS]
+        s_cols = T - V_COLS
+        pairs_v = sb([P, V_COLS, 2], BF16, "pairs_v")
+        pairs_s = sb([P, 2, s_cols, 2], BF16, "pairs_s")
+        woven_v = sb([P, V_COLS, PACK], BF16, "woven_v")
+        woven = [woven_v[:, c0:c1, :] if c0 < V_COLS else sb([P, c1 - c0, PACK], BF16, f"woven{c0}")[:] for c0, c1 in OUT_CUTS]
         v_cuts = [(k, c0, c1) for k, (c0, c1) in enumerate(OUT_CUTS) if c0 < V_COLS]
         s_cuts = [(k, c0, c1) for k, (c0, c1) in enumerate(OUT_CUTS) if c0 >= V_COLS]
         o_q = sb([P, T], I32, "o_q")
@@ -291,39 +306,39 @@ def tile_list_msg_relu_noneP_kernel(
         def as_words(tile):
             return tile.rearrange("p c i -> p (c i)").bitcast(F32).rearrange("p (c u) -> p c u", u=2)
 
-        for t, j0 in ((1, HALF), (0, J - CHUNK_J), (2, 0), (last, 0)):
+        for t, j0 in ((0, HALF), (1, J - CHUNK_J), (2, 0), (last, 0)):
             scatter(t, j0, J)
             page = pages[t]
             nc.sync.dma_start(out_rows[:, t, :], page[:])
             if t < 2:
-                nc.scalar.activation(pairs01[:, :, t], page[:, 0:V_COLS], ACT.Copy)
+                nc.scalar.activation(pairs_v[:, :, t], page[:, 0:V_COLS], ACT.Copy)
             if t == 2:
-                nc.scalar.activation(woven[:, :, 2:4], page[:, 0:V_COLS].unsqueeze(2).to_broadcast([P, V_COLS, 2]), ACT.Copy)
+                nc.scalar.activation(woven_v[:, :, 2:4], page[:, 0:V_COLS].unsqueeze(2).to_broadcast([P, V_COLS, 2]), ACT.Copy)
             if t < last:
                 nc.scalar.activation(pairs_s[:, t // 2, :, t % 2], page[:, V_COLS:T], ACT.Copy)
-            if t == 0:
-                words01 = pairs01[:].rearrange("p c e -> p (c e)").bitcast(F32)
-                nc.scalar.copy(as_words(woven[:]), words01.unsqueeze(2).to_broadcast([P, V_COLS, 2]))
+            if t == 1:
+                words = pairs_v[:].rearrange("p c e -> p (c e)").bitcast(F32)
+                nc.scalar.copy(as_words(woven_v[:]), words.unsqueeze(2).to_broadcast([P, V_COLS, 2]))
 
         for k, c0, c1 in v_cuts:
-            nc.vector.tensor_copy(o_bf[k][:, :, last], pages[last][:, c0:c1])
+            nc.vector.tensor_copy(woven[k][:, :, last], pages[last][:, c0:c1])
         for c0 in range(V_COLS, T, ROUND_C):
             nc.scalar.activation(pairs_s[:, 1, c0 - V_COLS : c0 - V_COLS + ROUND_C, 1], pages[last][:, c0 : c0 + ROUND_C], ACT.Copy)
         for k, c0, c1 in s_cuts:
             words = pairs_s[:].rearrange("p u c e -> p u (c e)").bitcast(F32)[:, :, c0 - V_COLS : c1 - V_COLS]
-            nc.scalar.copy(as_words(o_bf[k]), words.rearrange("p u c -> p c u"))
+            nc.scalar.copy(as_words(woven[k]), words.rearrange("p u c -> p c u"))
         for k, (c0, c1) in enumerate(OUT_CUTS):
             for c in range(c0, c1, CALL_C):
-                row, at = QUADS * (c // PLANE_C), c % PLANE_C
+                row, at = QUAD_ROWS * (c // PLANE_C), c % PLANE_C
                 nc.vector.quantize_mx(
                     o_q[:, c : c + CALL_C].bitcast(FP8X4),
                     o_sc[row:P, at : at + CALL_C],
-                    o_bf[k][:, c - c0 : c - c0 + CALL_C, :].rearrange("p c i -> p (c i)"),
+                    woven[k][:, c - c0 : c - c0 + CALL_C, :].rearrange("p c i -> p (c i)"),
                 )
             nc.sync.dma_start(out_words[:, c0:c1], o_q[:, c0:c1])
         for q in range(QUADS):
             queue = nc.scalar if q % 2 == 0 else nc.sync
             queue.dma_start(
-                out_2[0, 4 * q : 4 * q + 4, :].rearrange("r (k c) -> k r c", c=PLANE_C).bitcast(I32),
-                o_sc[32 * q : 32 * q + 16, :].bitcast(I32),
+                out_2[0, scale_rows(q), :].rearrange("r (k c) -> k r c", c=PLANE_C).bitcast(I32),
+                o_sc[QUAD_P * q : QUAD_P * q + PASS_ROWS, :].bitcast(I32),
             )

@@ -262,12 +262,13 @@ def tile_list_msg_relu_noneP_kernel(
             relu(b, h_bf[b // 2])
 
         quantize_h(0, h_bf[0])
-        second_product(0, 0, 2, 0)
+        for t in range(2):
+            second_product(0, t, t + 1, t)
         gather_words(sb([P, HALF], I32, "g_last", tag="h_bf0"), [(DST, 1, HALF, J)])
         quantize_h(1, h_bf[1])
-        second_product(1, 1, 2, 2)
-        scatter(0, 0, CHUNK_J)
-        scatter(1, 0, HALF)
+        second_product(1, 0, 1, 2)
+        for t, c in ((0, 0), (1, 0), (0, 1)):
+            scatter(t, c * CHUNK_J, (c + 1) * CHUNK_J)
 
         h_bf.append(sb([P, CHUNK_J * PACK], BF16, "h_bf2"))
         h_bf.append(placed([P, CHUNK_J * PACK], BF16, "h_bf3", at_h_last))
@@ -277,16 +278,17 @@ def tile_list_msg_relu_noneP_kernel(
                 first_product(side, a, b)
             relu(b, h_bf[b // 2])
             if b == chunk2_last_bank:
-                second_product(1, 0, 1, b)
+                second_product(1, 1, 2, b)
         quantize_h(2, h_bf[2])
         second_product(2, 0, 2, 4)
-        scatter(0, CHUNK_J, HALF)
+        scatter(1, CHUNK_J, HALF)
         quantize_h(3, h_bf[3])
         second_product(3, 0, 2, 6)
         for t, at in ((2, at_page2), (3, at_page3)):
             pages.append(placed([P, T], F32, f"page{t}", at))
             nc.gpsimd.memset(pages[t][:], 0.0)
-        scatter(1, HALF, HALF + CHUNK_J)
+        for t in range(2):
+            scatter(t, HALF, HALF + CHUNK_J)
         for c, bank in ((2, 0), (3, 2), (0, 1), (1, 3)):
             second_product(c, 2, 4, bank)
 
@@ -306,7 +308,7 @@ def tile_list_msg_relu_noneP_kernel(
         def as_words(tile):
             return tile.rearrange("p c i -> p (c i)").bitcast(F32).rearrange("p (c u) -> p c u", u=2)
 
-        for t, j0 in ((0, HALF), (1, J - CHUNK_J), (2, 0), (last, 0)):
+        for t, j0 in ((0, J - CHUNK_J), (1, J - CHUNK_J), (2, 0), (last, 0)):
             scatter(t, j0, J)
             page = pages[t]
             nc.sync.dma_start(out_rows[:, t, :], page[:])

@@ -33,7 +33,8 @@ HALF = J // 2
 KB = 1024
 STAGED = P - PASSES * PASS_ROWS
 V_COLS = 1024
-OUT_CUTS = ((0, 512), (512, 1024), (1024, 1536), (1536, 1792), (1792, 2048))
+OUT_CUTS = ((0, 512), (512, 768), (768, 1024), (1024, 1536), (1536, 1792), (1792, 1920), (1920, 2048))
+STORE_CUTS = ((0, 512), (512, 1024), (1024, 1536), (1536, 1792), (1792, 2048))
 ROUND_C = 512
 PLANE_C = T // QUADS
 CALL_C = PLANE_C // 2
@@ -186,11 +187,11 @@ def tile_list_msg_relu_noneP_kernel(
             [(side, 1, j, j + CHUNK_J) for j in (0, CHUNK_J) for side in (DST, SRC)] + [(SRC, 1, HALF, J)],
         )
 
-        acc = [psum.tile([P, PACK, BANK_J], F32, name=f"acc{b}", tag=f"bank{b}") for b in range(BANKS)]
         half_banks = BANKS // 2
+        acc = [psum.tile([P, PACK, BANK_J], F32, name=f"acc{b}", tag=f"bank{b}") for b in range(half_banks)]
 
         def bank_order(b):
-            if b < half_banks:
+            if b <= half_banks:
                 return ((SRC, 0), (DST, 0), (DST, 1), (SRC, 1))
             return ((DST, 1), (SRC, 0), (SRC, 1), (DST, 0))
 
@@ -261,9 +262,12 @@ def tile_list_msg_relu_noneP_kernel(
                 first_product(side, 1, b)
             relu(b, h_bf[b // 2])
 
+        acc.append(psum.tile([P, PACK, BANK_J], F32, name="acc4", tag="bank0"))
+        for side in (SRC, DST):
+            first_product(side, 0, half_banks)
         quantize_h(0, h_bf[0])
-        for t in range(2):
-            second_product(0, t, t + 1, t)
+        for t, bank in ((0, 4), (1, 1)):
+            second_product(0, t, t + 1, bank)
         gather_words(sb([P, HALF], I32, "g_last", tag="h_bf0"), [(DST, 1, HALF, J)])
         quantize_h(1, h_bf[1])
         second_product(1, 0, 1, 2)
@@ -273,8 +277,11 @@ def tile_list_msg_relu_noneP_kernel(
         h_bf.append(sb([P, CHUNK_J * PACK], BF16, "h_bf2"))
         h_bf.append(placed([P, CHUNK_J * PACK], BF16, "h_bf3", at_h_last))
         chunk2_last_bank = half_banks + 1
+        for b in range(chunk2_last_bank, BANKS):
+            acc.append(psum.tile([P, PACK, BANK_J], F32, name=f"acc{b}", tag=f"bank{b}"))
         for b in range(half_banks, BANKS):
-            for side, a in bank_order(b):
+            done = 2 if b == half_banks else 0
+            for side, a in bank_order(b)[done:]:
                 first_product(side, a, b)
             relu(b, h_bf[b // 2])
             if b == chunk2_last_bank:
@@ -322,22 +329,33 @@ def tile_list_msg_relu_noneP_kernel(
                 words = pairs_v[:].rearrange("p c e -> p (c e)").bitcast(F32)
                 nc.scalar.copy(as_words(woven_v[:]), words.unsqueeze(2).to_broadcast([P, V_COLS, 2]))
 
-        for k, c0, c1 in v_cuts:
+        def round_last_page(k):
+            c0, c1 = OUT_CUTS[k]
             nc.vector.tensor_copy(woven[k][:, :, last], pages[last][:, c0:c1])
+
+        def quantize_and_store(k):
+            c0, c1 = OUT_CUTS[k]
+            for c in range(c0, c1, CALL_C):
+                row, at, width = QUAD_ROWS * (c // PLANE_C), c % PLANE_C, min(CALL_C, c1 - c)
+                nc.vector.quantize_mx(
+                    o_q[:, c : c + width].bitcast(FP8X4),
+                    o_sc[row:P, at : at + width],
+                    woven[k][:, c - c0 : c - c0 + width, :].rearrange("p c i -> p (c i)"),
+                )
+            for s0, s1 in STORE_CUTS:
+                if s1 == c1:
+                    nc.sync.dma_start(out_words[:, s0:s1], o_q[:, s0:s1])
+
         for c0 in range(V_COLS, T, ROUND_C):
             nc.scalar.activation(pairs_s[:, 1, c0 - V_COLS : c0 - V_COLS + ROUND_C, 1], pages[last][:, c0 : c0 + ROUND_C], ACT.Copy)
         for k, c0, c1 in s_cuts:
             words = pairs_s[:].rearrange("p u c e -> p u (c e)").bitcast(F32)[:, :, c0 - V_COLS : c1 - V_COLS]
             nc.scalar.copy(as_words(woven[k]), words.rearrange("p u c -> p c u"))
-        for k, (c0, c1) in enumerate(OUT_CUTS):
-            for c in range(c0, c1, CALL_C):
-                row, at = QUAD_ROWS * (c // PLANE_C), c % PLANE_C
-                nc.vector.quantize_mx(
-                    o_q[:, c : c + CALL_C].bitcast(FP8X4),
-                    o_sc[row:P, at : at + CALL_C],
-                    woven[k][:, c - c0 : c - c0 + CALL_C, :].rearrange("p c i -> p (c i)"),
-                )
-            nc.sync.dma_start(out_words[:, c0:c1], o_q[:, c0:c1])
+        round_last_page(0)
+        for k in range(len(OUT_CUTS)):
+            if k + 1 < len(v_cuts):
+                round_last_page(k + 1)
+            quantize_and_store(k)
         for q in range(QUADS):
             queue = nc.scalar if q % 2 == 0 else nc.sync
             queue.dma_start(

@@ -61,16 +61,13 @@ def tile_list_msg_relu_noneP_kernel(
         def scale_rows(q):
             return slice(QUAD_ROWS * q, QUAD_ROWS * (q + 1))
 
-        at_wt_bf = (4 * KB, 48 * KB)
-        at_wt_raw = (20 * KB, 60 * KB)
-        at_ws_sc_raw = 47 * KB
-        at_g_pass0 = at_wt_raw[0] - 2 * KB + 64
-        at_wd_raw = at_wt_raw[0] + KB
-        at_y23 = at_g_pass0 - 7 * KB - 64
-        at_page1 = at_wt_bf[1] - 7 * KB
+        at_wt_raw = (0, 8 * KB)
+        at_ws_raw1 = 16 * KB
+        at_y23 = at_ws_raw1 + 512
+        at_page1 = 26 * KB
+        at_wt_bf = (40 * KB, at_page1 + 7 * KB)
         at_edge_w = at_wt_bf[1] + 3 * KB
-        at_g_pass1 = at_wt_raw[1] + 7 * KB
-        at_page2, at_page3 = 80 * KB, 89 * KB
+        at_page2, at_page3 = 44 * KB, 53 * KB
         at_h_last = at_page2 + 7 * KB + 512
 
         src_list = keep.tile([P, J // LIST_ROWS], U16, name="src_list")
@@ -78,14 +75,14 @@ def tile_list_msg_relu_noneP_kernel(
         lists = (src_list, dst_list)
 
         tab_sc = sb([P, T], U8, "tab_sc")
-        wd_sc_raw = sb([P, N], U8, "wd_sc_raw")
-        nc.gpsimd.memset(wd_sc_raw[:].bitcast(I32), 0)
-        ws_sc_raw = placed([P, PASSES, R], U8, "ws_sc_raw", at_ws_sc_raw)
-        nc.gpsimd.memset(ws_sc_raw[:].bitcast(I32), 0)
         nc.gpsimd.memset(tab_sc[0:STAGED, :].bitcast(I32), 0)
+        ws_sc_raw = sb([P, PASSES, R], U8, "ws_sc_raw")
+        nc.gpsimd.memset(ws_sc_raw[:].bitcast(I32), 0)
         planes = [sb([P, 2 * J], U8, f"planes{a}") for a in range(PASSES)]
         for plane in planes:
             nc.gpsimd.memset(plane[:].bitcast(I32), 0)
+        wd_sc_raw = sb([P, N], U8, "wd_sc_raw")
+        nc.gpsimd.memset(wd_sc_raw[:].bitcast(I32), 0)
         pages = [sb([P, T], F32, "page0")]
         nc.gpsimd.memset(pages[0][:], 0.0)
 
@@ -109,31 +106,24 @@ def tile_list_msg_relu_noneP_kernel(
         def deal(copy, dst, src):
             copy(dst.rearrange("p (t m) -> p t m", t=PACK), src.rearrange("p (m t) -> p t m", t=PACK))
 
-        def load_and_deal_ws(a, copy):
-            raw = sb([P, 2 * R], U8, f"ws_raw{a}")
-            nc.sync.dma_start(raw[:].bitcast(I32), ws_words[a].bitcast(I32))
-            ws.append(sb([P, 2 * R], U8, f"ws{a}"))
-            deal(copy, ws[a][:].bitcast(U16), raw[:].bitcast(U16))
+        def load_and_deal_words(raw, words, name, copy):
+            nc.sync.dma_start(raw[:].bitcast(I32), words.bitcast(I32))
+            dealt = sb([P, 2 * R], U8, name)
+            deal(copy, dealt[:].bitcast(U16), raw[:].bitcast(U16))
+            return dealt
 
         nc.sync.dma_start(src_list[:], offs)
         nc.sync.dma_start(tab_sc[STAGED:P, :].bitcast(I32), tab_scales.rearrange("a q t -> (a q) t").bitcast(I32))
         nc.sync.dma_start(dst_list[:], offs2)
-        load_tab(0)
-        for q in range(QUADS):
-            nc.sync.dma_start(wd_sc_raw[plane_rows(q), :].bitcast(I32), wd_scales[0, scale_rows(q), :].bitcast(I32))
         load_and_round_wt(0)
+        load_tab(0)
         for q in range(QUADS):
             nc.sync.dma_start(
                 ws_sc_raw[plane_rows(q), :, :].bitcast(I32),
                 ws_scales[:, scale_rows(q), :].rearrange("a r c -> r a c").bitcast(I32),
             )
-        wd_sc = sb([P, N], U8, "wd_sc")
-        deal(nc.gpsimd.tensor_copy, wd_sc[:], wd_sc_raw[:])
-        ws_sc = [sb([P, R], U8, f"ws_sc{a}") for a in range(PASSES)]
-        for a in range(PASSES):
-            deal(nc.gpsimd.tensor_copy, ws_sc[a][:], ws_sc_raw[:, a, :])
-        load_and_deal_ws(0, nc.gpsimd.tensor_copy)
         load_and_round_wt(1)
+        ws.append(load_and_deal_words(sb([P, 2 * R], U8, "ws_raw0"), ws_words[0], "ws0", nc.gpsimd.tensor_copy))
 
         g_sc = sb([P, 2 * J], U8, "g_sc")
         for side in (SRC, DST):
@@ -146,8 +136,11 @@ def tile_list_msg_relu_noneP_kernel(
 
         move_rows(0)
         load_tab(1)
-        load_and_deal_ws(1, nc.scalar.copy)
+        ws.append(load_and_deal_words(placed([P, 2 * R], U8, "ws_raw1", at_ws_raw1), ws_words[1], "ws1", nc.scalar.copy))
         move_rows(1)
+        for q in range(QUADS):
+            nc.sync.dma_start(wd_sc_raw[plane_rows(q), :].bitcast(I32), wd_scales[0, scale_rows(q), :].bitcast(I32))
+        wd = load_and_deal_words(sb([P, 2 * N], U8, "wd_raw"), wd_words[0], "wd", nc.scalar.copy)
 
         g_words = {}
 
@@ -169,31 +162,34 @@ def tile_list_msg_relu_noneP_kernel(
             cols = slice(a * R, (a + 1) * R)
             nc.vector.quantize_mx(wt_q[:, cols].bitcast(FP8X4), wt_sc[:, cols], wt_bf[a][:])
 
-        gather_words(sb([P, HALF + J], I32, "g_first"), [(SRC, 0, 0, J), (DST, 0, 0, HALF)])
+        gather_words(sb([P, J - CHUNK_J], I32, "g_first"), [(DST, 0, 0, J - CHUNK_J)])
         quantize_wt(0)
-        g_pass0 = placed([P, HALF], I32, "g_pass0", at_g_pass0)
-        wd_raw = placed([P, 2 * N], U8, "wd_raw", at_wd_raw)
-        nc.sync.dma_start(wd_raw[:].bitcast(I32), wd_words[0].bitcast(I32))
-        wd = sb([P, 2 * N], U8, "wd")
-        deal(nc.scalar.copy, wd[:].bitcast(U16), wd_raw[:].bitcast(U16))
-        gather_words(g_pass0[:], [(DST, 0, HALF, J)])
+        gather_words(placed([P, J], I32, "g_pass0", at_wt_raw[0]), [(SRC, 0, 0, J)])
+        ws_sc = [sb([P, R], U8, "ws_sc0"), placed([P, R], U8, "ws_sc1", at_wt_bf[0])]
+        for a in range(PASSES):
+            deal(nc.gpsimd.tensor_copy, ws_sc[a][:], ws_sc_raw[:, a, :])
         quantize_wt(1)
         pages.append(placed([P, T], F32, "page1", at_page1))
         nc.gpsimd.memset(pages[1][:], 0.0)
+        wd_sc = sb([P, N], U8, "wd_sc")
+        deal(nc.gpsimd.tensor_copy, wd_sc[:], wd_sc_raw[:])
         edge_w = placed([P, J], F32, "edge_w", at_edge_w)
         nc.sync.dma_start(edge_w[:], wgo)
         gather_words(
-            placed([P, 3 * HALF], I32, "g_pass1", at_g_pass1),
-            [(side, 1, j, j + CHUNK_J) for j in (0, CHUNK_J) for side in (DST, SRC)] + [(SRC, 1, HALF, J)],
+            placed([P, 5 * CHUNK_J], I32, "g_pass1", at_wt_raw[1]),
+            [(DST, 1, 0, CHUNK_J), (SRC, 1, 0, CHUNK_J), (DST, 1, CHUNK_J, HALF), (SRC, 1, CHUNK_J, J - CHUNK_J)],
         )
+        gather_words(placed([P, CHUNK_J], I32, "g_late", at_ws_raw1), [(DST, 0, J - CHUNK_J, J)])
 
         half_banks = BANKS // 2
         acc = [psum.tile([P, PACK, BANK_J], F32, name=f"acc{b}", tag=f"bank{b}") for b in range(half_banks)]
 
         def bank_order(b):
-            if b <= half_banks:
-                return ((SRC, 0), (DST, 0), (DST, 1), (SRC, 1))
-            return ((DST, 1), (SRC, 0), (SRC, 1), (DST, 0))
+            if b < 2:
+                return ((DST, 0), (SRC, 0), (DST, 1), (SRC, 1))
+            if b < half_banks:
+                return ((DST, 0), (DST, 1), (SRC, 0), (SRC, 1))
+            return ((SRC, 0), (SRC, 1), (DST, 1), (DST, 0))
 
         def first_product(side, a, b):
             cols = slice(side * J + b * BANK_J, side * J + (b + 1) * BANK_J)
@@ -253,41 +249,38 @@ def tile_list_msg_relu_noneP_kernel(
                 MULT,
             )
 
-        for side in (SRC, DST):
-            for b in range(half_banks):
-                first_product(side, 0, b)
         h_bf = [sb([P, CHUNK_J * PACK], BF16, f"h_bf{c}") for c in range(2)]
         for b in range(half_banks):
-            for side in (DST, SRC):
-                first_product(side, 1, b)
-            relu(b, h_bf[b // 2])
+            first_product(DST, 0, b)
+        for c in range(2):
+            for side, a in bank_order(2 * c)[1:-1]:
+                for b in (2 * c, 2 * c + 1):
+                    first_product(side, a, b)
+            for b in (2 * c, 2 * c + 1):
+                first_product(SRC, 1, b)
+                relu(b, h_bf[c])
 
-        acc.append(psum.tile([P, PACK, BANK_J], F32, name="acc4", tag="bank0"))
-        for side in (SRC, DST):
-            first_product(side, 0, half_banks)
         quantize_h(0, h_bf[0])
-        for t, bank in ((0, 4), (1, 1)):
+        for t, bank in ((0, 4), (1, 5)):
             second_product(0, t, t + 1, bank)
-        gather_words(sb([P, HALF], I32, "g_last", tag="h_bf0"), [(DST, 1, HALF, J)])
+        gather_words(sb([P, HALF + CHUNK_J], I32, "g_last", tag="h_bf0"), [(DST, 1, HALF, J), (SRC, 1, J - CHUNK_J, J)])
         quantize_h(1, h_bf[1])
-        second_product(1, 0, 1, 2)
+        second_product(1, 0, 1, 6)
         for t, c in ((0, 0), (1, 0), (0, 1)):
             scatter(t, c * CHUNK_J, (c + 1) * CHUNK_J)
 
         h_bf.append(sb([P, CHUNK_J * PACK], BF16, "h_bf2"))
         h_bf.append(placed([P, CHUNK_J * PACK], BF16, "h_bf3", at_h_last))
         chunk2_last_bank = half_banks + 1
-        for b in range(chunk2_last_bank, BANKS):
-            acc.append(psum.tile([P, PACK, BANK_J], F32, name=f"acc{b}", tag=f"bank{b}"))
-        for b in range(half_banks, BANKS):
-            done = 2 if b == half_banks else 0
-            for side, a in bank_order(b)[done:]:
+        for b, bank in zip(range(half_banks, BANKS), (4, 5, 6, 4)):
+            acc.append(psum.tile([P, PACK, BANK_J], F32, name=f"acc{b}", tag=f"bank{bank}"))
+            for side, a in bank_order(b):
                 first_product(side, a, b)
             relu(b, h_bf[b // 2])
             if b == chunk2_last_bank:
-                second_product(1, 1, 2, b)
+                second_product(1, 1, 2, bank)
         quantize_h(2, h_bf[2])
-        second_product(2, 0, 2, 4)
+        second_product(2, 0, 2, 7)
         scatter(1, CHUNK_J, HALF)
         quantize_h(3, h_bf[3])
         second_product(3, 0, 2, 6)

@@ -61,12 +61,12 @@ def tile_list_msg_relu_noneP_kernel(
         def scale_rows(q):
             return slice(QUAD_ROWS * q, QUAD_ROWS * (q + 1))
 
-        at_wt_raw = (0, 8 * KB)
-        at_ws_raw1 = 16 * KB
-        at_y23 = at_ws_raw1 + 512
-        at_page1 = 26 * KB
-        at_wt_bf = (40 * KB, at_page1 + 7 * KB)
-        at_edge_w = at_wt_bf[1] + 3 * KB
+        at_wt_raw = (8 * KB, 16 * KB)
+        at_g_late = at_wt_raw[0] - KB
+        at_y23 = at_g_late - 7 * KB
+        at_wt_bf = (24 * KB, 32 * KB)
+        at_edge_w = at_wt_bf[1] - 3 * KB
+        at_page1 = at_wt_bf[1] + 3 * KB
         at_page2, at_page3 = 44 * KB, 53 * KB
         at_h_last = at_page2 + 7 * KB + 512
 
@@ -76,13 +76,13 @@ def tile_list_msg_relu_noneP_kernel(
 
         tab_sc = sb([P, T], U8, "tab_sc")
         nc.gpsimd.memset(tab_sc[0:STAGED, :].bitcast(I32), 0)
+        wd_sc_raw = sb([P, N], U8, "wd_sc_raw")
+        nc.gpsimd.memset(wd_sc_raw[:].bitcast(I32), 0)
         ws_sc_raw = sb([P, PASSES, R], U8, "ws_sc_raw")
         nc.gpsimd.memset(ws_sc_raw[:].bitcast(I32), 0)
         planes = [sb([P, 2 * J], U8, f"planes{a}") for a in range(PASSES)]
         for plane in planes:
             nc.gpsimd.memset(plane[:].bitcast(I32), 0)
-        wd_sc_raw = sb([P, N], U8, "wd_sc_raw")
-        nc.gpsimd.memset(wd_sc_raw[:].bitcast(I32), 0)
         pages = [sb([P, T], F32, "page0")]
         nc.gpsimd.memset(pages[0][:], 0.0)
 
@@ -115,15 +115,22 @@ def tile_list_msg_relu_noneP_kernel(
         nc.sync.dma_start(src_list[:], offs)
         nc.sync.dma_start(tab_sc[STAGED:P, :].bitcast(I32), tab_scales.rearrange("a q t -> (a q) t").bitcast(I32))
         nc.sync.dma_start(dst_list[:], offs2)
-        load_and_round_wt(0)
         load_tab(0)
+        for q in range(QUADS):
+            nc.sync.dma_start(wd_sc_raw[plane_rows(q), :].bitcast(I32), wd_scales[0, scale_rows(q), :].bitcast(I32))
+        wd_sc = sb([P, N], U8, "wd_sc")
+        deal(nc.gpsimd.tensor_copy, wd_sc[:], wd_sc_raw[:])
+        load_and_round_wt(0)
         for q in range(QUADS):
             nc.sync.dma_start(
                 ws_sc_raw[plane_rows(q), :, :].bitcast(I32),
                 ws_scales[:, scale_rows(q), :].rearrange("a r c -> r a c").bitcast(I32),
             )
-        load_and_round_wt(1)
+        ws_sc = [sb([P, R], U8, f"ws_sc{a}") for a in range(PASSES)]
+        for a in range(PASSES):
+            deal(nc.gpsimd.tensor_copy, ws_sc[a][:], ws_sc_raw[:, a, :])
         ws.append(load_and_deal_words(sb([P, 2 * R], U8, "ws_raw0"), ws_words[0], "ws0", nc.gpsimd.tensor_copy))
+        load_and_round_wt(1)
 
         g_sc = sb([P, 2 * J], U8, "g_sc")
         for side in (SRC, DST):
@@ -136,10 +143,8 @@ def tile_list_msg_relu_noneP_kernel(
 
         move_rows(0)
         load_tab(1)
-        ws.append(load_and_deal_words(placed([P, 2 * R], U8, "ws_raw1", at_ws_raw1), ws_words[1], "ws1", nc.scalar.copy))
+        ws.append(load_and_deal_words(sb([P, 2 * R], U8, "ws_raw1"), ws_words[1], "ws1", nc.scalar.copy))
         move_rows(1)
-        for q in range(QUADS):
-            nc.sync.dma_start(wd_sc_raw[plane_rows(q), :].bitcast(I32), wd_scales[0, scale_rows(q), :].bitcast(I32))
         wd = load_and_deal_words(sb([P, 2 * N], U8, "wd_raw"), wd_words[0], "wd", nc.scalar.copy)
 
         g_words = {}
@@ -162,33 +167,25 @@ def tile_list_msg_relu_noneP_kernel(
             cols = slice(a * R, (a + 1) * R)
             nc.vector.quantize_mx(wt_q[:, cols].bitcast(FP8X4), wt_sc[:, cols], wt_bf[a][:])
 
-        gather_words(sb([P, J - CHUNK_J], I32, "g_first"), [(DST, 0, 0, J - CHUNK_J)])
+        gather_words(sb([P, HALF + J], I32, "g_first"), [(SRC, 0, 0, J), (DST, 0, 0, HALF)])
         quantize_wt(0)
-        gather_words(placed([P, J], I32, "g_pass0", at_wt_raw[0]), [(SRC, 0, 0, J)])
-        ws_sc = [sb([P, R], U8, "ws_sc0"), placed([P, R], U8, "ws_sc1", at_wt_bf[0])]
-        for a in range(PASSES):
-            deal(nc.gpsimd.tensor_copy, ws_sc[a][:], ws_sc_raw[:, a, :])
+        gather_words(placed([P, HALF], I32, "g_late", at_g_late), [(DST, 0, HALF, J)])
         quantize_wt(1)
         pages.append(placed([P, T], F32, "page1", at_page1))
         nc.gpsimd.memset(pages[1][:], 0.0)
-        wd_sc = sb([P, N], U8, "wd_sc")
-        deal(nc.gpsimd.tensor_copy, wd_sc[:], wd_sc_raw[:])
         edge_w = placed([P, J], F32, "edge_w", at_edge_w)
         nc.sync.dma_start(edge_w[:], wgo)
         gather_words(
-            placed([P, 5 * CHUNK_J], I32, "g_pass1", at_wt_raw[1]),
-            [(DST, 1, 0, CHUNK_J), (SRC, 1, 0, CHUNK_J), (DST, 1, CHUNK_J, HALF), (SRC, 1, CHUNK_J, J - CHUNK_J)],
+            placed([P, 3 * HALF], I32, "g_pass1", at_wt_raw[1]),
+            [(side, 1, j, j + CHUNK_J) for j in (0, CHUNK_J) for side in (DST, SRC)] + [(SRC, 1, HALF, J)],
         )
-        gather_words(placed([P, CHUNK_J], I32, "g_late", at_ws_raw1), [(DST, 0, J - CHUNK_J, J)])
 
         half_banks = BANKS // 2
         acc = [psum.tile([P, PACK, BANK_J], F32, name=f"acc{b}", tag=f"bank{b}") for b in range(half_banks)]
 
         def bank_order(b):
-            if b < 2:
-                return ((DST, 0), (SRC, 0), (DST, 1), (SRC, 1))
-            if b < half_banks:
-                return ((DST, 0), (DST, 1), (SRC, 0), (SRC, 1))
+            if b <= half_banks:
+                return ((SRC, 0), (DST, 0), (DST, 1), (SRC, 1))
             return ((SRC, 0), (SRC, 1), (DST, 1), (DST, 0))
 
         def first_product(side, a, b):
@@ -250,20 +247,21 @@ def tile_list_msg_relu_noneP_kernel(
             )
 
         h_bf = [sb([P, CHUNK_J * PACK], BF16, f"h_bf{c}") for c in range(2)]
+        for side in (SRC, DST):
+            for b in range(half_banks):
+                first_product(side, 0, b)
         for b in range(half_banks):
-            first_product(DST, 0, b)
-        for c in range(2):
-            for side, a in bank_order(2 * c)[1:-1]:
-                for b in (2 * c, 2 * c + 1):
-                    first_product(side, a, b)
-            for b in (2 * c, 2 * c + 1):
-                first_product(SRC, 1, b)
-                relu(b, h_bf[c])
+            for side in (DST, SRC):
+                first_product(side, 1, b)
+            relu(b, h_bf[b // 2])
 
+        acc.append(psum.tile([P, PACK, BANK_J], F32, name="acc4", tag="bank0"))
+        for side in (SRC, DST):
+            first_product(side, 0, half_banks)
         quantize_h(0, h_bf[0])
         for t, bank in ((0, 4), (1, 5)):
             second_product(0, t, t + 1, bank)
-        gather_words(sb([P, HALF + CHUNK_J], I32, "g_last", tag="h_bf0"), [(DST, 1, HALF, J), (SRC, 1, J - CHUNK_J, J)])
+        gather_words(sb([P, HALF], I32, "g_last", tag="h_bf0"), [(DST, 1, HALF, J)])
         quantize_h(1, h_bf[1])
         second_product(1, 0, 1, 6)
         for t, c in ((0, 0), (1, 0), (0, 1)):
@@ -272,9 +270,11 @@ def tile_list_msg_relu_noneP_kernel(
         h_bf.append(sb([P, CHUNK_J * PACK], BF16, "h_bf2"))
         h_bf.append(placed([P, CHUNK_J * PACK], BF16, "h_bf3", at_h_last))
         chunk2_last_bank = half_banks + 1
-        for b, bank in zip(range(half_banks, BANKS), (4, 5, 6, 4)):
-            acc.append(psum.tile([P, PACK, BANK_J], F32, name=f"acc{b}", tag=f"bank{bank}"))
-            for side, a in bank_order(b):
+        for b, bank in zip(range(half_banks, BANKS), (0, 4, 5, 6)):
+            done = 2 if b == half_banks else 0
+            if not done:
+                acc.append(psum.tile([P, PACK, BANK_J], F32, name=f"acc{b}", tag=f"bank{bank}"))
+            for side, a in bank_order(b)[done:]:
                 first_product(side, a, b)
             relu(b, h_bf[b // 2])
             if b == chunk2_last_bank:
@@ -283,7 +283,7 @@ def tile_list_msg_relu_noneP_kernel(
         second_product(2, 0, 2, 7)
         scatter(1, CHUNK_J, HALF)
         quantize_h(3, h_bf[3])
-        second_product(3, 0, 2, 6)
+        second_product(3, 0, 2, 5)
         for t, at in ((2, at_page2), (3, at_page3)):
             pages.append(placed([P, T], F32, f"page{t}", at))
             nc.gpsimd.memset(pages[t][:], 0.0)

@@ -61,13 +61,16 @@ def tile_list_msg_relu_noneP_kernel(
         def scale_rows(q):
             return slice(QUAD_ROWS * q, QUAD_ROWS * (q + 1))
 
-        at_wt_raw = (8 * KB, 16 * KB)
-        at_g_late = at_wt_raw[0] - KB
-        at_y23 = at_g_late - 7 * KB
-        at_wt_bf = (24 * KB, 32 * KB)
-        at_edge_w = at_wt_bf[1] - 3 * KB
-        at_page1 = at_wt_bf[1] + 3 * KB
-        at_page2, at_page3 = 44 * KB, 53 * KB
+        at_wt_bf = (4 * KB, 48 * KB)
+        at_wt_raw = (20 * KB, 60 * KB)
+        at_ws_sc_raw = 47 * KB
+        at_g_pass0 = at_wt_raw[0] - 2 * KB + 64
+        at_wd_raw = at_wt_raw[0] + KB
+        at_y23 = at_g_pass0 - 7 * KB - 64
+        at_page1 = at_wt_bf[1] - 7 * KB
+        at_edge_w = at_wt_bf[1] + 3 * KB
+        at_g_pass1 = at_wt_raw[1] + 7 * KB
+        at_page2, at_page3 = 80 * KB, 89 * KB
         at_h_last = at_page2 + 7 * KB + 512
 
         src_list = keep.tile([P, J // LIST_ROWS], U16, name="src_list")
@@ -75,11 +78,11 @@ def tile_list_msg_relu_noneP_kernel(
         lists = (src_list, dst_list)
 
         tab_sc = sb([P, T], U8, "tab_sc")
-        nc.gpsimd.memset(tab_sc[0:STAGED, :].bitcast(I32), 0)
         wd_sc_raw = sb([P, N], U8, "wd_sc_raw")
         nc.gpsimd.memset(wd_sc_raw[:].bitcast(I32), 0)
-        ws_sc_raw = sb([P, PASSES, R], U8, "ws_sc_raw")
+        ws_sc_raw = placed([P, PASSES, R], U8, "ws_sc_raw", at_ws_sc_raw)
         nc.gpsimd.memset(ws_sc_raw[:].bitcast(I32), 0)
+        nc.gpsimd.memset(tab_sc[0:STAGED, :].bitcast(I32), 0)
         planes = [sb([P, 2 * J], U8, f"planes{a}") for a in range(PASSES)]
         for plane in planes:
             nc.gpsimd.memset(plane[:].bitcast(I32), 0)
@@ -106,11 +109,11 @@ def tile_list_msg_relu_noneP_kernel(
         def deal(copy, dst, src):
             copy(dst.rearrange("p (t m) -> p t m", t=PACK), src.rearrange("p (m t) -> p t m", t=PACK))
 
-        def load_and_deal_words(raw, words, name, copy):
-            nc.sync.dma_start(raw[:].bitcast(I32), words.bitcast(I32))
-            dealt = sb([P, 2 * R], U8, name)
-            deal(copy, dealt[:].bitcast(U16), raw[:].bitcast(U16))
-            return dealt
+        def load_and_deal_ws(a, copy):
+            raw = sb([P, 2 * R], U8, f"ws_raw{a}")
+            nc.sync.dma_start(raw[:].bitcast(I32), ws_words[a].bitcast(I32))
+            ws.append(sb([P, 2 * R], U8, f"ws{a}"))
+            deal(copy, ws[a][:].bitcast(U16), raw[:].bitcast(U16))
 
         nc.sync.dma_start(src_list[:], offs)
         nc.sync.dma_start(tab_sc[STAGED:P, :].bitcast(I32), tab_scales.rearrange("a q t -> (a q) t").bitcast(I32))
@@ -118,18 +121,18 @@ def tile_list_msg_relu_noneP_kernel(
         load_tab(0)
         for q in range(QUADS):
             nc.sync.dma_start(wd_sc_raw[plane_rows(q), :].bitcast(I32), wd_scales[0, scale_rows(q), :].bitcast(I32))
-        wd_sc = sb([P, N], U8, "wd_sc")
-        deal(nc.gpsimd.tensor_copy, wd_sc[:], wd_sc_raw[:])
         load_and_round_wt(0)
         for q in range(QUADS):
             nc.sync.dma_start(
                 ws_sc_raw[plane_rows(q), :, :].bitcast(I32),
                 ws_scales[:, scale_rows(q), :].rearrange("a r c -> r a c").bitcast(I32),
             )
+        wd_sc = sb([P, N], U8, "wd_sc")
+        deal(nc.gpsimd.tensor_copy, wd_sc[:], wd_sc_raw[:])
         ws_sc = [sb([P, R], U8, f"ws_sc{a}") for a in range(PASSES)]
         for a in range(PASSES):
             deal(nc.gpsimd.tensor_copy, ws_sc[a][:], ws_sc_raw[:, a, :])
-        ws.append(load_and_deal_words(sb([P, 2 * R], U8, "ws_raw0"), ws_words[0], "ws0", nc.gpsimd.tensor_copy))
+        load_and_deal_ws(0, nc.gpsimd.tensor_copy)
         load_and_round_wt(1)
 
         g_sc = sb([P, 2 * J], U8, "g_sc")
@@ -143,9 +146,8 @@ def tile_list_msg_relu_noneP_kernel(
 
         move_rows(0)
         load_tab(1)
-        ws.append(load_and_deal_words(sb([P, 2 * R], U8, "ws_raw1"), ws_words[1], "ws1", nc.scalar.copy))
+        load_and_deal_ws(1, nc.scalar.copy)
         move_rows(1)
-        wd = load_and_deal_words(sb([P, 2 * N], U8, "wd_raw"), wd_words[0], "wd", nc.scalar.copy)
 
         g_words = {}
 
@@ -169,24 +171,27 @@ def tile_list_msg_relu_noneP_kernel(
 
         gather_words(sb([P, HALF + J], I32, "g_first"), [(SRC, 0, 0, J), (DST, 0, 0, HALF)])
         quantize_wt(0)
-        gather_words(placed([P, HALF], I32, "g_late", at_g_late), [(DST, 0, HALF, J)])
+        g_pass0 = placed([P, HALF], I32, "g_pass0", at_g_pass0)
+        wd_raw = placed([P, 2 * N], U8, "wd_raw", at_wd_raw)
+        nc.sync.dma_start(wd_raw[:].bitcast(I32), wd_words[0].bitcast(I32))
+        wd = sb([P, 2 * N], U8, "wd")
+        deal(nc.scalar.copy, wd[:].bitcast(U16), wd_raw[:].bitcast(U16))
+        gather_words(g_pass0[:], [(DST, 0, HALF, J)])
         quantize_wt(1)
         pages.append(placed([P, T], F32, "page1", at_page1))
         nc.gpsimd.memset(pages[1][:], 0.0)
         edge_w = placed([P, J], F32, "edge_w", at_edge_w)
         nc.sync.dma_start(edge_w[:], wgo)
-        gather_words(
-            placed([P, 3 * HALF], I32, "g_pass1", at_wt_raw[1]),
-            [(side, 1, j, j + CHUNK_J) for j in (0, CHUNK_J) for side in (DST, SRC)] + [(SRC, 1, HALF, J)],
-        )
+        turns = [(DST if b % 2 == 0 else SRC, 1, max(b - 1, 0) * BANK_J, min(b + 1, BANKS // 2) * BANK_J) for b in range(BANKS // 2 + 1)]
+        gather_words(placed([P, 3 * HALF], I32, "g_pass1", at_g_pass1), turns + [(SRC, 1, HALF, J)])
 
         half_banks = BANKS // 2
         acc = [psum.tile([P, PACK, BANK_J], F32, name=f"acc{b}", tag=f"bank{b}") for b in range(half_banks)]
 
         def bank_order(b):
             if b <= half_banks:
-                return ((SRC, 0), (DST, 0), (DST, 1), (SRC, 1))
-            return ((SRC, 0), (SRC, 1), (DST, 1), (DST, 0))
+                return ((SRC, 0), (DST, 0)) + (((DST, 1), (SRC, 1)) if b % 2 == 0 else ((SRC, 1), (DST, 1)))
+            return ((DST, 1), (SRC, 0), (SRC, 1), (DST, 0))
 
         def first_product(side, a, b):
             cols = slice(side * J + b * BANK_J, side * J + (b + 1) * BANK_J)
@@ -246,44 +251,44 @@ def tile_list_msg_relu_noneP_kernel(
                 MULT,
             )
 
-        h_bf = [sb([P, CHUNK_J * PACK], BF16, f"h_bf{c}") for c in range(2)]
         for side in (SRC, DST):
             for b in range(half_banks):
                 first_product(side, 0, b)
+        h_bf = [sb([P, CHUNK_J * PACK], BF16, f"h_bf{c}") for c in range(2)]
         for b in range(half_banks):
-            for side in (DST, SRC):
-                first_product(side, 1, b)
+            for side, a in bank_order(b)[2:]:
+                first_product(side, a, b)
             relu(b, h_bf[b // 2])
 
         acc.append(psum.tile([P, PACK, BANK_J], F32, name="acc4", tag="bank0"))
         for side in (SRC, DST):
             first_product(side, 0, half_banks)
         quantize_h(0, h_bf[0])
-        for t, bank in ((0, 4), (1, 5)):
+        for t, bank in ((0, 4), (1, 1)):
             second_product(0, t, t + 1, bank)
         gather_words(sb([P, HALF], I32, "g_last", tag="h_bf0"), [(DST, 1, HALF, J)])
         quantize_h(1, h_bf[1])
-        second_product(1, 0, 1, 6)
+        second_product(1, 0, 1, 2)
         for t, c in ((0, 0), (1, 0), (0, 1)):
             scatter(t, c * CHUNK_J, (c + 1) * CHUNK_J)
 
         h_bf.append(sb([P, CHUNK_J * PACK], BF16, "h_bf2"))
         h_bf.append(placed([P, CHUNK_J * PACK], BF16, "h_bf3", at_h_last))
         chunk2_last_bank = half_banks + 1
-        for b, bank in zip(range(half_banks, BANKS), (0, 4, 5, 6)):
+        for b in range(chunk2_last_bank, BANKS):
+            acc.append(psum.tile([P, PACK, BANK_J], F32, name=f"acc{b}", tag=f"bank{b}"))
+        for b in range(half_banks, BANKS):
             done = 2 if b == half_banks else 0
-            if not done:
-                acc.append(psum.tile([P, PACK, BANK_J], F32, name=f"acc{b}", tag=f"bank{bank}"))
             for side, a in bank_order(b)[done:]:
                 first_product(side, a, b)
             relu(b, h_bf[b // 2])
             if b == chunk2_last_bank:
-                second_product(1, 1, 2, bank)
+                second_product(1, 1, 2, b)
         quantize_h(2, h_bf[2])
-        second_product(2, 0, 2, 7)
+        second_product(2, 0, 2, 4)
         scatter(1, CHUNK_J, HALF)
         quantize_h(3, h_bf[3])
-        second_product(3, 0, 2, 5)
+        second_product(3, 0, 2, 6)
         for t, at in ((2, at_page2), (3, at_page3)):
             pages.append(placed([P, T], F32, f"page{t}", at))
             nc.gpsimd.memset(pages[t][:], 0.0)

@@ -71,7 +71,7 @@ def tile_list_msg_relu_noneP_kernel(
         at_edge_w = at_wt_bf[1] + 3 * KB
         at_g_pass1 = at_wt_raw[1] + 7 * KB
         at_page2, at_page3 = 80 * KB, 89 * KB
-        at_h_last = at_page2 + 7 * KB + 512
+        at_h1, at_h3 = at_page2, at_page3
 
         src_list = keep.tile([P, J // LIST_ROWS], U16, name="src_list")
         dst_list = keep.tile([P, J // LIST_ROWS], U16, name="dst_list")
@@ -88,6 +88,8 @@ def tile_list_msg_relu_noneP_kernel(
             nc.gpsimd.memset(plane[:].bitcast(I32), 0)
         pages = [sb([P, T], F32, "page0")]
         nc.gpsimd.memset(pages[0][:], 0.0)
+        pairs = sb([P, 2, T, 2], BF16, "pairs")
+        nc.gpsimd.memset(pairs[:, 1, 0:V_COLS, :].rearrange("p c e -> p (c e)").bitcast(I32), 0)
 
         wt_bf = [placed([P, R * PACK], BF16, f"wt_bf{a}", at_wt_bf[a]) for a in range(PASSES)]
         tab = []
@@ -182,15 +184,17 @@ def tile_list_msg_relu_noneP_kernel(
         nc.gpsimd.memset(pages[1][:], 0.0)
         edge_w = placed([P, J], F32, "edge_w", at_edge_w)
         nc.sync.dma_start(edge_w[:], wgo)
-        turns = [(DST if b % 2 == 0 else SRC, 1, max(b - 1, 0) * BANK_J, min(b + 1, BANKS // 2) * BANK_J) for b in range(BANKS // 2 + 1)]
-        gather_words(placed([P, 3 * HALF], I32, "g_pass1", at_g_pass1), turns + [(SRC, 1, HALF, J)])
+        gather_words(
+            placed([P, 3 * HALF], I32, "g_pass1", at_g_pass1),
+            [(side, 1, j, j + CHUNK_J) for j in (0, CHUNK_J) for side in (DST, SRC)] + [(SRC, 1, HALF, J)],
+        )
 
         half_banks = BANKS // 2
         acc = [psum.tile([P, PACK, BANK_J], F32, name=f"acc{b}", tag=f"bank{b}") for b in range(half_banks)]
 
         def bank_order(b):
             if b <= half_banks:
-                return ((SRC, 0), (DST, 0)) + (((DST, 1), (SRC, 1)) if b % 2 == 0 else ((SRC, 1), (DST, 1)))
+                return ((SRC, 0), (DST, 0), (DST, 1), (SRC, 1))
             return ((DST, 1), (SRC, 0), (SRC, 1), (DST, 0))
 
         def first_product(side, a, b):
@@ -228,20 +232,18 @@ def tile_list_msg_relu_noneP_kernel(
             cols = slice(c * CHUNK_J, (c + 1) * CHUNK_J)
             nc.vector.quantize_mx(h_q[:, cols].bitcast(FP8X4), h_sc[:, cols], h_bf[:])
 
-        def second_product(c, t0, t1, bank):
-            cols = slice(c * CHUNK_J, (c + 1) * CHUNK_J)
-            res = psum.tile([P, t1 - t0, CHUNK_J], F32, name=f"res{c}_{t0}", tag=f"bank{bank}")
-            for t in range(t0, t1):
-                nc.tensor.matmul_mx(
-                    res[:, t - t0, :],
-                    lhsT=wd[:, 2 * P * t : 2 * P * (t + 1)].bitcast(FP4X4),
-                    lhsT_scale=wd_sc[:, P * t : P * (t + 1)],
-                    rhs=h_q[:, cols].bitcast(FP8X4),
-                    rhs_scale=h_sc[:, cols],
-                    start=True,
-                    stop=True,
-                )
-            nc.scalar.activation(y[t0 // 2][:, t0 % 2 : t0 % 2 + t1 - t0, cols], res[:], ACT.Copy)
+        def second_product(t, j0, j1, bank):
+            res = psum.tile([P, j1 - j0], F32, name=f"res{t}_{j0}", tag=f"bank{bank}")
+            nc.tensor.matmul_mx(
+                res[:],
+                lhsT=wd[:, 2 * P * t : 2 * P * (t + 1)].bitcast(FP4X4),
+                lhsT_scale=wd_sc[:, P * t : P * (t + 1)],
+                rhs=h_q[:, j0:j1].bitcast(FP8X4),
+                rhs_scale=h_sc[:, j0:j1],
+                start=True,
+                stop=True,
+            )
+            nc.scalar.activation(y[t // 2][:, t % 2, j0:j1], res[:], ACT.Copy)
 
         def scatter(t, j0, j1):
             nc.vector.tensor_tensor(
@@ -254,10 +256,10 @@ def tile_list_msg_relu_noneP_kernel(
         for side in (SRC, DST):
             for b in range(half_banks):
                 first_product(side, 0, b)
-        h_bf = [sb([P, CHUNK_J * PACK], BF16, f"h_bf{c}") for c in range(2)]
+        h_bf = [sb([P, CHUNK_J * PACK], BF16, "h_bf0"), placed([P, CHUNK_J * PACK], BF16, "h_bf1", at_h1)]
         for b in range(half_banks):
-            for side, a in bank_order(b)[2:]:
-                first_product(side, a, b)
+            for side in (DST, SRC):
+                first_product(side, 1, b)
             relu(b, h_bf[b // 2])
 
         acc.append(psum.tile([P, PACK, BANK_J], F32, name="acc4", tag="bank0"))
@@ -265,15 +267,17 @@ def tile_list_msg_relu_noneP_kernel(
             first_product(side, 0, half_banks)
         quantize_h(0, h_bf[0])
         for t, bank in ((0, 4), (1, 1)):
-            second_product(0, t, t + 1, bank)
+            second_product(t, 0, CHUNK_J, bank)
         gather_words(sb([P, HALF], I32, "g_last", tag="h_bf0"), [(DST, 1, HALF, J)])
         quantize_h(1, h_bf[1])
-        second_product(1, 0, 1, 2)
-        for t, c in ((0, 0), (1, 0), (0, 1)):
-            scatter(t, c * CHUNK_J, (c + 1) * CHUNK_J)
+        second_product(1, CHUNK_J, HALF, 2)
+        pages.append(placed([P, T], F32, "page2", at_page2))
+        nc.gpsimd.memset(pages[2][:], 0.0)
+        scatter(0, 0, CHUNK_J)
+        scatter(1, 0, HALF)
 
         h_bf.append(sb([P, CHUNK_J * PACK], BF16, "h_bf2"))
-        h_bf.append(placed([P, CHUNK_J * PACK], BF16, "h_bf3", at_h_last))
+        h_bf.append(placed([P, CHUNK_J * PACK], BF16, "h_bf3", at_h3))
         chunk2_last_bank = half_banks + 1
         for b in range(chunk2_last_bank, BANKS):
             acc.append(psum.tile([P, PACK, BANK_J], F32, name=f"acc{b}", tag=f"bank{b}"))
@@ -283,23 +287,18 @@ def tile_list_msg_relu_noneP_kernel(
                 first_product(side, a, b)
             relu(b, h_bf[b // 2])
             if b == chunk2_last_bank:
-                second_product(1, 1, 2, b)
+                second_product(0, CHUNK_J, HALF, b)
         quantize_h(2, h_bf[2])
-        second_product(2, 0, 2, 4)
-        scatter(1, CHUNK_J, HALF)
+        scatter(0, CHUNK_J, HALF)
         quantize_h(3, h_bf[3])
-        second_product(3, 0, 2, 6)
-        for t, at in ((2, at_page2), (3, at_page3)):
-            pages.append(placed([P, T], F32, f"page{t}", at))
-            nc.gpsimd.memset(pages[t][:], 0.0)
-        for t in range(2):
-            scatter(t, HALF, HALF + CHUNK_J)
-        for c, bank in ((2, 0), (3, 2), (0, 1), (1, 3)):
-            second_product(c, 2, 4, bank)
+        pages.append(placed([P, T], F32, "page3", at_page3))
+        nc.gpsimd.memset(pages[3][:], 0.0)
+        for t in (2, 3):
+            second_product(t, 0, HALF, t)
+        scatter(2, 0, HALF)
+        for t, bank in enumerate((4, 1, 0, 6)):
+            second_product(t, HALF, J, bank)
 
-        s_cols = T - V_COLS
-        pairs_v = sb([P, V_COLS, 2], BF16, "pairs_v")
-        pairs_s = sb([P, 2, s_cols, 2], BF16, "pairs_s")
         woven_v = sb([P, V_COLS, PACK], BF16, "woven_v")
         woven = [woven_v[:, c0:c1, :] if c0 < V_COLS else sb([P, c1 - c0, PACK], BF16, f"woven{c0}")[:] for c0, c1 in OUT_CUTS]
         v_cuts = [(k, c0, c1) for k, (c0, c1) in enumerate(OUT_CUTS) if c0 < V_COLS]
@@ -310,22 +309,23 @@ def tile_list_msg_relu_noneP_kernel(
         out_words = out_1[0].rearrange("p c i -> p (c i)").bitcast(I32)
         last = PACK - 1
 
-        def as_words(tile):
-            return tile.rearrange("p c i -> p (c i)").bitcast(F32).rearrange("p (c u) -> p c u", u=2)
+        def weave(tile, c0, c1):
+            words = pairs[:].rearrange("p u c e -> p u (c e)").bitcast(F32)[:, :, c0:c1]
+            nc.scalar.copy(
+                tile.rearrange("p c i -> p (c i)").bitcast(F32).rearrange("p (c u) -> p c u", u=2),
+                words.rearrange("p u c -> p c u"),
+            )
 
-        for t, j0 in ((0, J - CHUNK_J), (1, J - CHUNK_J), (2, 0), (last, 0)):
+        for t, j0 in ((0, HALF), (1, HALF), (2, HALF), (last, 0)):
             scatter(t, j0, J)
             page = pages[t]
             nc.sync.dma_start(out_rows[:, t, :], page[:])
             if t < 2:
-                nc.scalar.activation(pairs_v[:, :, t], page[:, 0:V_COLS], ACT.Copy)
+                nc.scalar.activation(pairs[:, 0, :, t], page[:], ACT.Copy)
             if t == 2:
-                nc.scalar.activation(woven_v[:, :, 2:4], page[:, 0:V_COLS].unsqueeze(2).to_broadcast([P, V_COLS, 2]), ACT.Copy)
-            if t < last:
-                nc.scalar.activation(pairs_s[:, t // 2, :, t % 2], page[:, V_COLS:T], ACT.Copy)
-            if t == 1:
-                words = pairs_v[:].rearrange("p c e -> p (c e)").bitcast(F32)
-                nc.scalar.copy(as_words(woven_v[:]), words.unsqueeze(2).to_broadcast([P, V_COLS, 2]))
+                nc.scalar.activation(pairs[:, 1, 0:V_COLS, 0], page[:, 0:V_COLS], ACT.Copy)
+                nc.scalar.activation(pairs[:, 1, V_COLS:T, 0], page[:, V_COLS:T], ACT.Copy)
+                weave(woven_v[:], 0, V_COLS)
 
         def round_last_page(k):
             c0, c1 = OUT_CUTS[k]
@@ -345,10 +345,9 @@ def tile_list_msg_relu_noneP_kernel(
                     nc.sync.dma_start(out_words[:, s0:s1], o_q[:, s0:s1])
 
         for c0 in range(V_COLS, T, ROUND_C):
-            nc.scalar.activation(pairs_s[:, 1, c0 - V_COLS : c0 - V_COLS + ROUND_C, 1], pages[last][:, c0 : c0 + ROUND_C], ACT.Copy)
+            nc.scalar.activation(pairs[:, 1, c0 : c0 + ROUND_C, 1], pages[last][:, c0 : c0 + ROUND_C], ACT.Copy)
         for k, c0, c1 in s_cuts:
-            words = pairs_s[:].rearrange("p u c e -> p u (c e)").bitcast(F32)[:, :, c0 - V_COLS : c1 - V_COLS]
-            nc.scalar.copy(as_words(woven[k]), words.rearrange("p u c -> p c u"))
+            weave(woven[k], c0, c1)
         round_last_page(0)
         for k in range(len(OUT_CUTS)):
             if k + 1 < len(v_cuts):

from contextlib import ExitStack

import concourse.mybir as mybir

K, R, N, T, J = 1024, 512, 512, 2048, 1024
FLOPS = 2 * (2 * K * R * J + R * N * J)

F32 = mybir.dt.float32
BF16 = mybir.dt.bfloat16
I32 = mybir.dt.int32
U32 = mybir.dt.uint32
U16 = mybir.dt.uint16
U8 = mybir.dt.uint8
FP8X4 = mybir.dt.float8_e4m3fn_x4
FP4X4 = mybir.dt.float4_e2m1fn_x4
ACT = mybir.ActivationFunctionType
MULT = mybir.AluOpType.mult

P = 128
PACK = 4
K_PASS = P * PACK
PASSES = K // K_PASS
QUADS = 4
QUAD_P = P // QUADS
QUAD_ROWS = 4
PASS_ROWS = QUADS * QUAD_ROWS
LIST_ROWS = 16
SRC, DST = 0, 1
BANK_J = 128
BANKS = J // BANK_J
CHUNK_J = 256
HALF = J // 2
KB = 1024
STAGED = P - PASSES * PASS_ROWS
V_COLS = 1024
OUT_CUTS = ((0, 512), (512, 768), (768, 1024), (1024, 1536), (1536, 1792), (1792, 1920), (1920, 2048))
STORE_CUTS = ((0, 512), (512, 1024), (1024, 1536), (1536, 1792), (1792, 2048))
ROUND_C = 512
PLANE_C = T // QUADS
CALL_C = PLANE_C // 2


def tile_list_msg_relu_noneP_kernel(
    tc, tab_words, tab_scales, ws_words, ws_scales, wt, wd_words, wd_scales, wgo, offs, offs2, out_0, out_1, out_2
):
    nc = tc.nc
    with ExitStack() as ctx:
        keep = ctx.enter_context(tc.tile_pool(name="keep", bufs=1))
        shared = ctx.enter_context(tc.tile_pool(name="shared", bufs=1))
        psum = ctx.enter_context(tc.psum_pool(name="psum", bufs=1))

        def sb(shape, dtype, name, tag=None):
            return keep.tile(shape, dtype, name=name, tag=tag or name, align_bytes=64)

        def placed(shape, dtype, name, offset):
            return shared.tile(shape, dtype, name=name, tag=name, align_bytes=64, offset=offset)

        def plane_rows(q):
            return slice(QUAD_P * q, QUAD_P * q + QUAD_ROWS)

        def scale_rows(q):
            return slice(QUAD_ROWS * q, QUAD_ROWS * (q + 1))

        at_wt_bf = (4 * KB, 48 * KB)
        at_wt_raw = (20 * KB, 60 * KB)
        at_ws_sc_raw = 47 * KB
        at_g_pass0 = at_wt_raw[0] - 2 * KB + 64
        at_wd_raw = at_wt_raw[0] + KB
        at_y23 = at_g_pass0 - 7 * KB - 64
        at_page1 = at_wt_bf[1] - 7 * KB
        at_edge_w = at_wt_bf[1] + 3 * KB
        at_g_pass1 = at_wt_raw[1] + 7 * KB
        at_page2, at_page3 = 80 * KB, 89 * KB
        at_h1, at_h3 = at_page2, at_page3

        src_list = keep.tile([P, J // LIST_ROWS], U16, name="src_list")
        dst_list = keep.tile([P, J // LIST_ROWS], U16, name="dst_list")
        lists = (src_list, dst_list)

        tab_sc = sb([P, T], U8, "tab_sc")
        wd_sc_raw = sb([P, N], U8, "wd_sc_raw")
        nc.gpsimd.memset(wd_sc_raw[:].bitcast(I32), 0)
        ws_sc_raw = placed([P, PASSES, R], U8, "ws_sc_raw", at_ws_sc_raw)
        nc.gpsimd.memset(ws_sc_raw[:].bitcast(I32), 0)
        nc.gpsimd.memset(tab_sc[0:STAGED, :].bitcast(I32), 0)
        planes = [sb([P, 2 * J], U8, f"planes{a}") for a in range(PASSES)]
        for plane in planes:
            nc.gpsimd.memset(plane[:].bitcast(I32), 0)
        pages = [sb([P, T], F32, "page0")]
        nc.gpsimd.memset(pages[0][:], 0.0)
        pairs = sb([P, 2, T, 2], BF16, "pairs")
        nc.gpsimd.memset(pairs[:, 1, 0:V_COLS, :].rearrange("p c e -> p (c e)").bitcast(I32), 0)

        wt_bf = [placed([P, R * PACK], BF16, f"wt_bf{a}", at_wt_bf[a]) for a in range(PASSES)]
        tab = []
        ws = []

        def load_tab(a):
            tab.append(sb([P, T], I32, f"tab{a}"))
            nc.sync.dma_start(tab[a][:], tab_words[a].rearrange("p t i -> p (t i)").bitcast(I32))

        def load_and_round_wt(a):
            raw = placed([P, PACK, R], F32, f"wt{a}", at_wt_raw[a])
            nc.sync.dma_start(raw[:], wt[a * K_PASS : (a + 1) * K_PASS, :].rearrange("(p i) c -> p i c", i=PACK))
            nc.scalar.activation(
                wt_bf[a][:].rearrange("p (t m i) -> p m i t", t=PACK, i=PACK),
                raw[:].rearrange("p i (m t) -> p m i t", t=PACK),
                ACT.Copy,
            )

        def deal(copy, dst, src):
            copy(dst.rearrange("p (t m) -> p t m", t=PACK), src.rearrange("p (m t) -> p t m", t=PACK))

        def load_and_deal_ws(a, copy):
            raw = sb([P, 2 * R], U8, f"ws_raw{a}")
            nc.sync.dma_start(raw[:].bitcast(I32), ws_words[a].bitcast(I32))
            ws.append(sb([P, 2 * R], U8, f"ws{a}"))
            deal(copy, ws[a][:].bitcast(U16), raw[:].bitcast(U16))

        nc.sync.dma_start(src_list[:], offs)
        nc.sync.dma_start(tab_sc[STAGED:P, :].bitcast(I32), tab_scales.rearrange("a q t -> (a q) t").bitcast(I32))
        nc.sync.dma_start(dst_list[:], offs2)
        load_tab(0)
        for q in range(QUADS):
            nc.sync.dma_start(wd_sc_raw[plane_rows(q), :].bitcast(I32), wd_scales[0, scale_rows(q), :].bitcast(I32))
        load_and_round_wt(0)
        for q in range(QUADS):
            nc.sync.dma_start(
                ws_sc_raw[plane_rows(q), :, :].bitcast(I32),
                ws_scales[:, scale_rows(q), :].rearrange("a r c -> r a c").bitcast(I32),
            )
        wd_sc = sb([P, N], U8, "wd_sc")
        deal(nc.gpsimd.tensor_copy, wd_sc[:], wd_sc_raw[:])
        ws_sc = [sb([P, R], U8, f"ws_sc{a}") for a in range(PASSES)]
        for a in range(PASSES):
            deal(nc.gpsimd.tensor_copy, ws_sc[a][:], ws_sc_raw[:, a, :])
        load_and_deal_ws(0, nc.gpsimd.tensor_copy)
        load_and_round_wt(1)

        g_sc = sb([P, 2 * J], U8, "g_sc")
        for side in (SRC, DST):
            nc.vector.tensor_copy(g_sc[:, side * J : (side + 1) * J], tab_sc[:].indirect(lists[side][:]))

        def move_rows(a):
            for q in range(QUADS):
                row = STAGED + PASS_ROWS * a + QUAD_ROWS * q
                nc.sync.dma_start(planes[a][plane_rows(q), :].bitcast(I32), g_sc[row : row + QUAD_ROWS, :].bitcast(I32))

        move_rows(0)
        load_tab(1)
        load_and_deal_ws(1, nc.scalar.copy)
        move_rows(1)

        g_words = {}

        def gather_words(tile, pieces):
            at = 0
            for side, a, j0, j1 in pieces:
                dst = tile[:, at : at + j1 - j0]
                for j in range(j0, j1, BANK_J):
                    g_words[(side, a, j // BANK_J)] = dst[:, j - j0 : j - j0 + BANK_J]
                nc.vector.tensor_copy(
                    dst.bitcast(U32), tab[a][:].bitcast(U32).indirect(lists[side][:, j0 // LIST_ROWS : j1 // LIST_ROWS])
                )
                at = at + j1 - j0

        wt_q = sb([P, PASSES * R], I32, "wt_q")
        wt_sc = sb([P, PASSES * R], U8, "wt_sc")

        def quantize_wt(a):
            cols = slice(a * R, (a + 1) * R)
            nc.vector.quantize_mx(wt_q[:, cols].bitcast(FP8X4), wt_sc[:, cols], wt_bf[a][:])

        gather_words(sb([P, HALF + J], I32, "g_first"), [(SRC, 0, 0, J), (DST, 0, 0, HALF)])
        quantize_wt(0)
        g_pass0 = placed([P, HALF], I32, "g_pass0", at_g_pass0)
        wd_raw = placed([P, 2 * N], U8, "wd_raw", at_wd_raw)
        nc.sync.dma_start(wd_raw[:].bitcast(I32), wd_words[0].bitcast(I32))
        wd = sb([P, 2 * N], U8, "wd")
        deal(nc.scalar.copy, wd[:].bitcast(U16), wd_raw[:].bitcast(U16))
        gather_words(g_pass0[:], [(DST, 0, HALF, J)])
        quantize_wt(1)
        pages.append(placed([P, T], F32, "page1", at_page1))
        nc.gpsimd.memset(pages[1][:], 0.0)
        edge_w = placed([P, J], F32, "edge_w", at_edge_w)
        nc.sync.dma_start(edge_w[:], wgo)
        gather_words(
            placed([P, 3 * HALF], I32, "g_pass1", at_g_pass1),
            [(side, 1, j, j + CHUNK_J) for j in (0, CHUNK_J) for side in (DST, SRC)] + [(SRC, 1, HALF, J)],
        )

        half_banks = BANKS // 2
        acc = [psum.tile([P, PACK, BANK_J], F32, name=f"acc{b}", tag=f"bank{b}") for b in range(half_banks)]

        def bank_order(b):
            if b <= half_banks:
                return ((SRC, 0), (DST, 0), (DST, 1), (SRC, 1))
            return ((DST, 1), (SRC, 0), (SRC, 1), (DST, 0))

        def first_product(side, a, b):
            cols = slice(side * J + b * BANK_J, side * J + (b + 1) * BANK_J)
            for t in range(PACK):
                if side == SRC:
                    lhsT = ws[a][:, 2 * P * t : 2 * P * (t + 1)].bitcast(FP4X4)
                    lhsT_scale = ws_sc[a][:, P * t : P * (t + 1)]
                else:
                    lhsT = wt_q[:, a * R + P * t : a * R + P * (t + 1)].bitcast(FP8X4)
                    lhsT_scale = wt_sc[:, a * R + P * t : a * R + P * (t + 1)]
                nc.tensor.matmul_mx(
                    acc[b][:, t, :],
                    lhsT=lhsT,
                    lhsT_scale=lhsT_scale,
                    rhs=g_words[(side, a, b)].bitcast(FP8X4),
                    rhs_scale=planes[a][:, cols],
                    start=((side, a) == bank_order(b)[0] and t == 0),
                    stop=((side, a) == bank_order(b)[-1] and t == PACK - 1),
                )

        h_q = sb([P, J], I32, "h_q")
        h_sc = sb([P, J], U8, "h_sc")
        y = [sb([P, 2, J], F32, "y01"), placed([P, 2, J], F32, "y23", at_y23)]

        def relu(b, h_bf):
            j0 = b % 2 * BANK_J
            nc.scalar.activation(
                h_bf[:, j0 * PACK : (j0 + BANK_J) * PACK].rearrange("p (j t) -> p j t", t=PACK),
                acc[b][:].rearrange("p t j -> p j t"),
                ACT.Relu,
            )

        def quantize_h(c, h_bf):
            cols = slice(c * CHUNK_J, (c + 1) * CHUNK_J)
            nc.vector.quantize_mx(h_q[:, cols].bitcast(FP8X4), h_sc[:, cols], h_bf[:])

        def second_product(t, j0, j1, bank):
            res = psum.tile([P, j1 - j0], F32, name=f"res{t}_{j0}", tag=f"bank{bank}")
            nc.tensor.matmul_mx(
                res[:],
                lhsT=wd[:, 2 * P * t : 2 * P * (t + 1)].bitcast(FP4X4),
                lhsT_scale=wd_sc[:, P * t : P * (t + 1)],
                rhs=h_q[:, j0:j1].bitcast(FP8X4),
                rhs_scale=h_sc[:, j0:j1],
                start=True,
                stop=True,
            )
            nc.scalar.activation(y[t // 2][:, t % 2, j0:j1], res[:], ACT.Copy)

        def scatter(t, j0, j1):
            nc.vector.tensor_tensor(
                pages[t][:].indirect(dst_list[:, j0 // LIST_ROWS : j1 // LIST_ROWS]),
                y[t // 2][:, t % 2, j0:j1],
                edge_w[:, j0:j1],
                MULT,
            )

        for side in (SRC, DST):
            for b in range(half_banks):
                first_product(side, 0, b)
        h_bf = [sb([P, CHUNK_J * PACK], BF16, "h_bf0"), placed([P, CHUNK_J * PACK], BF16, "h_bf1", at_h1)]
        for b in range(half_banks):
            for side in (DST, SRC):
                first_product(side, 1, b)
            relu(b, h_bf[b // 2])

        acc.append(psum.tile([P, PACK, BANK_J], F32, name="acc4", tag="bank0"))
        for side in (SRC, DST):
            first_product(side, 0, half_banks)
        quantize_h(0, h_bf[0])
        for t, bank in ((0, 4), (1, 1)):
            second_product(t, 0, CHUNK_J, bank)
        gather_words(sb([P, HALF], I32, "g_last", tag="h_bf0"), [(DST, 1, HALF, J)])
        quantize_h(1, h_bf[1])
        second_product(1, CHUNK_J, HALF, 2)
        pages.append(placed([P, T], F32, "page2", at_page2))
        nc.gpsimd.memset(pages[2][:], 0.0)
        scatter(0, 0, CHUNK_J)
        scatter(1, 0, HALF)

        h_bf.append(sb([P, CHUNK_J * PACK], BF16, "h_bf2"))
        h_bf.append(placed([P, CHUNK_J * PACK], BF16, "h_bf3", at_h3))
        chunk2_last_bank = half_banks + 1
        for b in range(chunk2_last_bank, BANKS):
            acc.append(psum.tile([P, PACK, BANK_J], F32, name=f"acc{b}", tag=f"bank{b}"))
        for b in range(half_banks, BANKS):
            done = 2 if b == half_banks else 0
            for side, a in bank_order(b)[done:]:
                first_product(side, a, b)
            relu(b, h_bf[b // 2])
            if b == chunk2_last_bank:
                second_product(0, CHUNK_J, HALF, b)
        quantize_h(2, h_bf[2])
        scatter(0, CHUNK_J, HALF)
        quantize_h(3, h_bf[3])
        pages.append(placed([P, T], F32, "page3", at_page3))
        nc.gpsimd.memset(pages[3][:], 0.0)
        for t in (2, 3):
            second_product(t, 0, HALF, t)
        scatter(2, 0, HALF)
        for t, bank in enumerate((4, 1, 0, 6)):
            second_product(t, HALF, J, bank)

        woven_v = sb([P, V_COLS, PACK], BF16, "woven_v")
        woven = [woven_v[:, c0:c1, :] if c0 < V_COLS else sb([P, c1 - c0, PACK], BF16, f"woven{c0}")[:] for c0, c1 in OUT_CUTS]
        v_cuts = [(k, c0, c1) for k, (c0, c1) in enumerate(OUT_CUTS) if c0 < V_COLS]
        s_cuts = [(k, c0, c1) for k, (c0, c1) in enumerate(OUT_CUTS) if c0 >= V_COLS]
        o_q = sb([P, T], I32, "o_q")
        o_sc = sb([P, PLANE_C], U8, "o_sc")
        out_rows = out_0.rearrange("(p t) c -> p t c", t=PACK)
        out_words = out_1[0].rearrange("p c i -> p (c i)").bitcast(I32)
        last = PACK - 1

        def weave(tile, c0, c1):
            words = pairs[:].rearrange("p u c e -> p u (c e)").bitcast(F32)[:, :, c0:c1]
            nc.scalar.copy(
                tile.rearrange("p c i -> p (c i)").bitcast(F32).rearrange("p (c u) -> p c u", u=2),
                words.rearrange("p u c -> p c u"),
            )

        for t, j0 in ((0, HALF), (1, HALF), (2, HALF), (last, 0)):
            scatter(t, j0, J)
            page = pages[t]
            nc.sync.dma_start(out_rows[:, t, :], page[:])
            if t < 2:
                nc.scalar.activation(pairs[:, 0, :, t], page[:], ACT.Copy)
            if t == 2:
                nc.scalar.activation(pairs[:, 1, 0:V_COLS, 0], page[:, 0:V_COLS], ACT.Copy)
                nc.scalar.activation(pairs[:, 1, V_COLS:T, 0], page[:, V_COLS:T], ACT.Copy)
                weave(woven_v[:], 0, V_COLS)

        def round_last_page(k):
            c0, c1 = OUT_CUTS[k]
            nc.vector.tensor_copy(woven[k][:, :, last], pages[last][:, c0:c1])

        def quantize_and_store(k):
            c0, c1 = OUT_CUTS[k]
            for c in range(c0, c1, CALL_C):
                row, at, width = QUAD_ROWS * (c // PLANE_C), c % PLANE_C, min(CALL_C, c1 - c)
                nc.vector.quantize_mx(
                    o_q[:, c : c + width].bitcast(FP8X4),
                    o_sc[row:P, at : at + width],
                    woven[k][:, c - c0 : c - c0 + width, :].rearrange("p c i -> p (c i)"),
                )
            for s0, s1 in STORE_CUTS:
                if s1 == c1:
                    nc.sync.dma_start(out_words[:, s0:s1], o_q[:, s0:s1])

        for c0 in range(V_COLS, T, ROUND_C):
            nc.scalar.activation(pairs[:, 1, c0 : c0 + ROUND_C, 1], pages[last][:, c0 : c0 + ROUND_C], ACT.Copy)
        for k, c0, c1 in s_cuts:
            weave(woven[k], c0, c1)
        round_last_page(0)
        for k in range(len(OUT_CUTS)):
            if k + 1 < len(v_cuts):
                round_last_page(k + 1)
            quantize_and_store(k)
        for q in range(QUADS):
            queue = nc.scalar if q % 2 == 0 else nc.sync
            queue.dma_start(
                out_2[0, scale_rows(q), :].rearrange("r (k c) -> k r c", c=PLANE_C).bitcast(I32),
                o_sc[QUAD_P * q : QUAD_P * q + PASS_ROWS, :].bitcast(I32),
            )
